import numpy as np
import ml_dtypes


def mxq(x, axis, fmt="e4m3"):
    dtype, down = {"e4m3": (ml_dtypes.float8_e4m3fn, 7), "e5m2": (ml_dtypes.float8_e5m2, 14)}[fmt]
    v = np.moveaxis(np.asarray(x, np.float32).astype(ml_dtypes.bfloat16).astype(np.float64), axis, -1)
    blocks = v.reshape(v.shape[:-1] + (-1, 32))
    amax = np.abs(blocks).max(-1, keepdims=True)
    byte = np.maximum(np.where(amax > 0, np.frexp(amax)[1] - 1 + 127, 0) - down, 1)
    scale = np.exp2(byte - 127.0)
    codes = (blocks / scale).astype(np.float32).astype(dtype).astype(np.float64)
    return np.moveaxis((codes * scale).reshape(v.shape), -1, axis)


WIDE = False


def mx_kscale(k):
    if not WIDE:
        return np.ones(k)
    levels = np.array([24, -24, 12, -12, 0])
    if k % 512:
        return np.exp2(np.random.permutation(np.resize(levels, k // 32))).repeat(32)
    a = np.empty((k // 512, 16))
    for p in range(k // 512):
        a[p, :8] = np.random.permutation(np.resize(levels, 8))
        for g in range(8):
            far = levels[np.abs(levels - a[p, g]) >= 10]
            a[p, g + 8] = far[np.random.randint(len(far))]
    return np.exp2(a.ravel()).repeat(32)


def f64(x):
    return np.asarray(x).astype(np.float64)


def striped(idx):
    return np.tile(idx.reshape(-1, 16).T, (8, 1)).astype(np.uint16)


def unstriped(offs):
    return offs[:16].T.reshape(-1).astype(np.int64)


E2M1 = np.array([0.0, 0.5, 1.0, 1.5, 2.0, 3.0, 4.0, 6.0, -0.0, -0.5, -1.0, -1.5, -2.0, -3.0, -4.0, -6.0])


def pack_weight(w, fmt):
    k, n = w.shape
    w = f64(np.asarray(w, np.float32).astype(ml_dtypes.bfloat16)).reshape(k // 32, 32, n)
    amax = np.abs(w).max(1)
    if fmt == "e4m3":
        byte = np.frexp(amax)[1] - 1 + 127 - 7
    else:
        mant, ex = np.frexp(amax / 6.0)
        byte = np.where(mant > 0.5, ex, ex - 1) + 127
    byte = np.clip(np.where(amax > 0, byte, 1), 1, 254)
    scaled = (w * np.exp2(127.0 - byte)[:, None, :]).reshape(k, n).astype(np.float32)
    by_word = np.ascontiguousarray(scaled.reshape(k // 512, 128, 4, n).transpose(0, 1, 3, 2))
    if fmt == "e4m3":
        words = by_word.astype(ml_dtypes.float8_e4m3fn).view(np.uint8)
    else:
        c = by_word.astype(ml_dtypes.float4_e2m1fn).view(np.uint8) & 0xF
        words = (c[..., 0::2] | (c[..., 1::2] << 4)).reshape(k // 512, 128, 2 * n)
    return np.ascontiguousarray(words), np.ascontiguousarray(byte.astype(np.uint8).reshape(k // 512, 16, n))


def unpack_weight(words, scales, fmt):
    g, _, n = scales.shape
    words = np.ascontiguousarray(words).reshape(g, 128, n, -1)
    if fmt == "e4m3":
        vals = words.view(ml_dtypes.float8_e4m3fn).astype(np.float64)
    else:
        nib = np.empty((g, 128, n, 4), np.uint8)
        nib[..., 0::2] = words & 0xF
        nib[..., 1::2] = words >> 4
        vals = E2M1[nib]
    vals = vals * np.repeat(np.exp2(scales.astype(np.float64) - 127.0), 8, axis=1)[..., None]
    return vals.transpose(0, 1, 3, 2).reshape(g * 512, n)


def sigm(f):
    return 1.0 / (1.0 + np.exp(-np.maximum(f, -700.0)))


K, N, T, J = 512, 512, 2048, 1024


def setup_inputs():
    n = np.random.standard_normal
    s = mx_kscale(K)[:, None]
    p_tab = pack_weight(n((K, T)) * s, "e4m3")
    p_wa = pack_weight(n((K, N)) / np.sqrt(2 * K) / s, "e4m3")
    p_wb = pack_weight(n((K, N)) / np.sqrt(2 * K) / s, "e4m3")
    return {
        "tab_words": p_tab[0],
        "tab_scales": p_tab[1],
        "wa_words": p_wa[0],
        "wa_scales": p_wa[1],
        "wb_words": p_wb[0],
        "wb_scales": p_wb[1],
        "wc": (n((K, N)) / np.sqrt(K) / s).astype(np.float32),
        "rT": (n((N, T))).astype(np.float32),
        "wgo": np.tile(np.random.uniform(0.5, 2.0, J), (128, 1)).astype(np.float32),
        "offs": striped(np.random.permutation(T)[:J]),
        "offs2": striped(np.random.permutation(T)[:J]),
    }


def reference(tab_words, tab_scales, wa_words, wa_scales, wb_words, wb_scales, wc, rT, wgo, offs, offs2):
    idx = unstriped(offs)
    idx2 = unstriped(offs2)
    tab_ = unpack_weight(tab_words, tab_scales, "e4m3")[:, idx]
    tabb_ = unpack_weight(tab_words, tab_scales, "e4m3")[:, idx2]
    wa_ = unpack_weight(wa_words, wa_scales, "e4m3")
    wb_ = unpack_weight(wb_words, wb_scales, "e4m3")
    za = wa_.T @ tabb_ + wb_.T @ tab_
    eta = sigm(za)
    wc_ = mxq(f64(wc), 0, "e4m3")
    ms = wc_.T @ tab_
    out = np.zeros((N, T))
    out[:, idx2] = f64(wgo)[0] * (eta * ms + f64(rT)[:, idx2])
    return out

@@ -1,0 +1,179 @@
+from contextlib import ExitStack
+
+import concourse.mybir as mybir
+
+K, N, T, J = 512, 512, 2048, 1024
+FLOPS = 3 * 2 * K * N * J
+
+F32 = mybir.dt.float32
+BF16 = mybir.dt.bfloat16
+I32 = mybir.dt.int32
+U32 = mybir.dt.uint32
+U16 = mybir.dt.uint16
+U8 = mybir.dt.uint8
+FP8X4 = mybir.dt.float8_e4m3fn_x4
+MULT = mybir.AluOpType.mult
+ADD = mybir.AluOpType.add
+SIGMOID = mybir.ActivationFunctionType.Sigmoid
+
+P = 128
+PACK = 4
+BLOCKS = N // P
+HALF = 512
+HALVES = J // HALF
+LANES = 16
+
+
+def tile_list_rgg_L_kernel(
+    tc, tab_words, tab_scales, wa_words, wa_scales, wb_words, wb_scales, wc, rT, wgo, offs, offs2, out
+):
+    nc = tc.nc
+
+    def words_of(packed):
+        return packed[0].rearrange("p n t -> p (n t)").bitcast(I32)
+
+    def load_scales(plane, scales):
+        for r in range(4):
+            nc.sync.dma_start(out=plane[r:P:32, :], in_=scales[0, r:16:4, :].bitcast(I32))
+
+    with ExitStack() as ctx:
+        held = ctx.enter_context(tc.tile_pool(name="held", bufs=1))
+        psum = ctx.enter_context(tc.psum_pool(name="psum", bufs=4))
+
+        src_list = held.tile([P, J // LANES], U16)
+        dst_list = held.tile([P, J // LANES], U16)
+        tab_s = held.tile([P, T // 4], I32, align_bytes=64)
+        tab_w = held.tile([P, T], I32, align_bytes=64)
+        wa_s = held.tile([P, N // 4], I32, align_bytes=64)
+        wb_s = held.tile([P, N // 4], I32, align_bytes=64)
+        wa_w = held.tile([P, N], I32, align_bytes=64)
+        wb_w = held.tile([P, N], I32, align_bytes=64)
+        wc_raw = [held.tile([P, PACK, N // 2], F32, name="wc_raw%d" % i) for i in range(2)]
+        wc_bf = held.tile([P, N, PACK], BF16, align_bytes=64)
+        wc_w = held.tile([P, N], U32, align_bytes=64)
+        wc_s = held.tile([P, N], U8, align_bytes=64)
+        weight = held.tile([P, J], F32)
+        src_s = held.tile([P, J], U8, align_bytes=64)
+        dst_s = held.tile([P, J], U8, align_bytes=64)
+        src_w = [held.tile([P, HALF], U32, align_bytes=64, name="src_w%d" % h) for h in range(HALVES)]
+        dst_w = [held.tile([P, HALF], U32, align_bytes=64, name="dst_w%d" % h) for h in range(HALVES)]
+        state = [held.tile([P, T], F32, name="state%d" % b) for b in range(BLOCKS)]
+        picked = [held.tile([P, J], F32, name="picked%d" % b) for b in range(BLOCKS)]
+        gate = [held.tile([P, J], F32, name="gate%d" % b) for b in range(BLOCKS)]
+        message = [held.tile([P, J], F32, name="message%d" % b) for b in range(BLOCKS)]
+        gated_a = held.tile([P, J], F32)
+        gated_b = held.tile([P, J], F32)
+        gated = [gated_a, gated_b, gated_a, gated_a]
+        summed = held.tile([P, J], F32)
+        weighted = [held.tile([P, J], F32, name="weighted%d" % b) for b in range(BLOCKS - 1)]
+        placed = [held.tile([P, T], F32, name="placed%d" % i) for i in range(2)]
+        warm = held.tile([P, 1], F32)
+        warm_out = held.tile([P, 1], F32)
+
+        nc.gpsimd.memset(tab_s[:], 0)
+        nc.gpsimd.memset(wa_s[:], 0)
+        nc.gpsimd.memset(wb_s[:], 0)
+        nc.gpsimd.memset(warm[:], 0.0)
+        nc.scalar.activation(warm_out[:], warm[:], SIGMOID)
+        for tile in placed:
+            nc.gpsimd.memset(tile[:], 0.0)
+
+        nc.sync.dma_start(src_list[:], offs)
+        nc.sync.dma_start(dst_list[:], offs2)
+        load_scales(tab_s, tab_scales)
+        load_scales(wa_s, wa_scales)
+        load_scales(wb_s, wb_scales)
+        wc_rows = wc.rearrange("(p i) n -> p i n", i=PACK)
+        nc.sync.dma_start(out=wc_raw[0][:], in_=wc_rows[:, :, 0 : N // 2])
+        nc.sync.dma_start(out=tab_w[:], in_=words_of(tab_words))
+        nc.sync.dma_start(out=wa_w[:], in_=words_of(wa_words))
+        nc.sync.dma_start(out=wb_w[:], in_=words_of(wb_words))
+        nc.sync.dma_start(out=wc_raw[1][:], in_=wc_rows[:, :, N // 2 : N])
+        nc.sync.dma_start(out=state[0][:], in_=rT[0:P, :])
+        nc.sync.dma_start(out=weight[:], in_=wgo)
+        for b in range(1, BLOCKS):
+            nc.sync.dma_start(out=state[b][:], in_=rT[b * P : (b + 1) * P, :])
+
+        for i in range(2):
+            nc.scalar.copy(wc_bf[:, i * N // 2 : (i + 1) * N // 2, :], wc_raw[i][:].rearrange("p i n -> p n i"))
+
+        nc.vector.tensor_copy(src_s[:], tab_s[:].bitcast(U8).indirect(src_list[:]))
+        nc.vector.tensor_copy(dst_s[:], tab_s[:].bitcast(U8).indirect(dst_list[:]))
+
+        def gather_words(h):
+            cols = slice(h * HALF // LANES, (h + 1) * HALF // LANES)
+            nc.vector.tensor_copy(dst_w[h][:], tab_w[:].bitcast(U32).indirect(dst_list[:, cols]))
+            nc.vector.tensor_copy(src_w[h][:], tab_w[:].bitcast(U32).indirect(src_list[:, cols]))
+
+        def products(b, h):
+            n = slice(b * P, (b + 1) * P)
+            j = slice(h * HALF, (h + 1) * HALF)
+            za = psum.tile([P, HALF], F32)
+            ms = psum.tile([P, HALF], F32)
+            nc.tensor.matmul_mx(
+                za[:], lhsT=wa_w[:, n].bitcast(FP8X4), lhsT_scale=wa_s[:].bitcast(U8)[:, n],
+                rhs=dst_w[h][:].bitcast(FP8X4), rhs_scale=dst_s[:, j], start=True, stop=False,
+            )
+            nc.tensor.matmul_mx(
+                za[:], lhsT=wb_w[:, n].bitcast(FP8X4), lhsT_scale=wb_s[:].bitcast(U8)[:, n],
+                rhs=src_w[h][:].bitcast(FP8X4), rhs_scale=src_s[:, j], start=False, stop=True,
+            )
+            nc.tensor.matmul_mx(
+                ms[:], lhsT=wc_w[:, n].bitcast(FP8X4), lhsT_scale=wc_s[:, n],
+                rhs=src_w[h][:].bitcast(FP8X4), rhs_scale=src_s[:, j], start=True, stop=True,
+            )
+            nc.scalar.activation(gate[b][:, j], za[:], SIGMOID)
+            nc.scalar.copy(message[b][:, j], ms[:])
+
+        def gate_message(b, j):
+            nc.gpsimd.tensor_tensor(gated[b][:, j], gate[b][:, j], message[b][:, j], MULT)
+
+        def add_state(b, j):
+            nc.gpsimd.tensor_tensor(summed[:, j], gated[b][:, j], picked[b][:, j], ADD)
+            if b < BLOCKS - 1:
+                nc.gpsimd.tensor_tensor(weighted[b][:, j], summed[:, j], weight[:, j], MULT)
+
+        def quantize(i):
+            n = slice(i * N // 2, (i + 1) * N // 2)
+            nc.vector.quantize_mx(
+                out=wc_w[:, n].bitcast(FP8X4), scales=wc_s[:, n], in_=wc_bf[:, n, :].rearrange("p n i -> p (n i)")
+            )
+
+        quantize(0)
+        gather_words(0)
+        gather_words(1)
+        quantize(1)
+        for b in range(BLOCKS):
+            nc.vector.tensor_copy(picked[b][:], state[b][:].indirect(dst_list[:]))
+
+        first, second, both = slice(0, HALF), slice(HALF, J), slice(0, J)
+        products(0, 0)
+        gate_message(0, first)
+        products(1, 0)
+        gate_message(1, first)
+        add_state(0, first)
+        products(0, 1)
+        gate_message(0, second)
+        add_state(0, second)
+        products(1, 1)
+        gate_message(1, second)
+        add_state(1, both)
+        for b in range(2, BLOCKS):
+            products(b, 0)
+            products(b, 1)
+            gate_message(b, both)
+            add_state(b, both)
+
+        for b in range(BLOCKS):
+            window = placed[b % 2]
+            if b == 0:
+                for h in range(HALVES):
+                    cols = slice(h * HALF // LANES, (h + 1) * HALF // LANES)
+                    nc.vector.tensor_copy(
+                        window[:].indirect(dst_list[:, cols]), weighted[b][:, h * HALF : (h + 1) * HALF]
+                    )
+            elif b < BLOCKS - 1:
+                nc.vector.tensor_copy(window[:].indirect(dst_list[:]), weighted[b][:])
+            else:
+                nc.vector.tensor_tensor(window[:].indirect(dst_list[:]), summed[:], weight[:], MULT)
+            nc.sync.dma_start(out=out[b * P : (b + 1) * P, :], in_=window[:])

@@ -1,6 +1,7 @@
 from contextlib import ExitStack
 
 import concourse.mybir as mybir
+from concourse.masks import make_identity
 
 K, N, T, J = 512, 512, 2048, 1024
 FLOPS = 3 * 2 * K * N * J
@@ -13,14 +14,15 @@ U16 = mybir.dt.uint16
 U8 = mybir.dt.uint8
 FP8X4 = mybir.dt.float8_e4m3fn_x4
 MULT = mybir.AluOpType.mult
-ADD = mybir.AluOpType.add
 SIGMOID = mybir.ActivationFunctionType.Sigmoid
+COPY = mybir.ActivationFunctionType.Copy
 
 P = 128
 PACK = 4
 BLOCKS = N // P
 HALF = 512
 HALVES = J // HALF
+SQUARES = HALF // P
 LANES = 16
 
 
@@ -38,142 +40,136 @@ def tile_list_rgg_L_kernel(
 
     with ExitStack() as ctx:
         held = ctx.enter_context(tc.tile_pool(name="held", bufs=1))
-        psum = ctx.enter_context(tc.psum_pool(name="psum", bufs=4))
+        ring = ctx.enter_context(tc.tile_pool(name="ring", bufs=2))
+        psum = ctx.enter_context(tc.psum_pool(name="psum", bufs=1))
 
         src_list = held.tile([P, J // LANES], U16)
         dst_list = held.tile([P, J // LANES], U16)
         tab_s = held.tile([P, T // 4], I32, align_bytes=64)
         tab_w = held.tile([P, T], I32, align_bytes=64)
-        wa_s = held.tile([P, N // 4], I32, align_bytes=64)
-        wb_s = held.tile([P, N // 4], I32, align_bytes=64)
+        w_s = held.tile([P, 2, N // 4], I32, align_bytes=64)
+        wa_s, wb_s = w_s[:, 0, :], w_s[:, 1, :]
         wa_w = held.tile([P, N], I32, align_bytes=64)
         wb_w = held.tile([P, N], I32, align_bytes=64)
-        wc_raw = [held.tile([P, PACK, N // 2], F32, name="wc_raw%d" % i) for i in range(2)]
-        wc_bf = held.tile([P, N, PACK], BF16, align_bytes=64)
+        wc_raw = held.tile([P, PACK, N], F32)
+        wc_bf = held.tile([P, N, PACK], BF16, align_bytes=64, tag="shared")
         wc_w = held.tile([P, N], U32, align_bytes=64)
         wc_s = held.tile([P, N], U8, align_bytes=64)
-        weight = held.tile([P, J], F32)
+        weight_rows = held.tile([P, P], F32)
+        weight_col = held.tile([P, J // P], F32)
+        identity = held.tile([P, P], F32)
         src_s = held.tile([P, J], U8, align_bytes=64)
         dst_s = held.tile([P, J], U8, align_bytes=64)
-        src_w = [held.tile([P, HALF], U32, align_bytes=64, name="src_w%d" % h) for h in range(HALVES)]
-        dst_w = [held.tile([P, HALF], U32, align_bytes=64, name="dst_w%d" % h) for h in range(HALVES)]
         state = [held.tile([P, T], F32, name="state%d" % b) for b in range(BLOCKS)]
-        picked = [held.tile([P, J], F32, name="picked%d" % b) for b in range(BLOCKS)]
-        gate = [held.tile([P, J], F32, name="gate%d" % b) for b in range(BLOCKS)]
-        message = [held.tile([P, J], F32, name="message%d" % b) for b in range(BLOCKS)]
-        gated_a = held.tile([P, J], F32)
-        gated_b = held.tile([P, J], F32)
-        gated = [gated_a, gated_b, gated_a, gated_a]
-        summed = held.tile([P, J], F32)
-        weighted = [held.tile([P, J], F32, name="weighted%d" % b) for b in range(BLOCKS - 1)]
+        gate = held.tile([P, J], F32)
+        message = held.tile([P, J], F32)
+        gated = held.tile([P, J], F32)
+        result = [held.tile([P, J], F32, name="result%d" % b) for b in range(BLOCKS)]
         placed = [held.tile([P, T], F32, name="placed%d" % i) for i in range(2)]
         warm = held.tile([P, 1], F32)
         warm_out = held.tile([P, 1], F32)
 
         nc.gpsimd.memset(tab_s[:], 0)
-        nc.gpsimd.memset(wa_s[:], 0)
-        nc.gpsimd.memset(wb_s[:], 0)
+        nc.gpsimd.memset(w_s[:], 0)
         nc.gpsimd.memset(warm[:], 0.0)
         nc.scalar.activation(warm_out[:], warm[:], SIGMOID)
+        make_identity(nc, identity[:])
         for tile in placed:
             nc.gpsimd.memset(tile[:], 0.0)
 
         nc.sync.dma_start(src_list[:], offs)
         nc.sync.dma_start(dst_list[:], offs2)
         load_scales(tab_s, tab_scales)
+        nc.sync.dma_start(out=tab_w[:], in_=words_of(tab_words))
+        nc.sync.dma_start(out=wc_raw[:], in_=wc.rearrange("(p i) n -> p i n", i=PACK))
         load_scales(wa_s, wa_scales)
         load_scales(wb_s, wb_scales)
-        wc_rows = wc.rearrange("(p i) n -> p i n", i=PACK)
-        nc.sync.dma_start(out=wc_raw[0][:], in_=wc_rows[:, :, 0 : N // 2])
-        nc.sync.dma_start(out=tab_w[:], in_=words_of(tab_words))
         nc.sync.dma_start(out=wa_w[:], in_=words_of(wa_words))
         nc.sync.dma_start(out=wb_w[:], in_=words_of(wb_words))
-        nc.sync.dma_start(out=wc_raw[1][:], in_=wc_rows[:, :, N // 2 : N])
         nc.sync.dma_start(out=state[0][:], in_=rT[0:P, :])
-        nc.sync.dma_start(out=weight[:], in_=wgo)
+        nc.sync.dma_start(out=weight_rows[:], in_=wgo[0 : P * P // J, :].rearrange("r (c j) -> (r c) j", j=P))
         for b in range(1, BLOCKS):
             nc.sync.dma_start(out=state[b][:], in_=rT[b * P : (b + 1) * P, :])
 
-        for i in range(2):
-            nc.scalar.copy(wc_bf[:, i * N // 2 : (i + 1) * N // 2, :], wc_raw[i][:].rearrange("p i n -> p n i"))
+        nc.scalar.copy(
+            wc_bf[:].rearrange("p (c m) i -> p c i m", m=PACK), wc_raw[:].rearrange("p i (c m) -> p c i m", m=PACK)
+        )
 
         nc.vector.tensor_copy(src_s[:], tab_s[:].bitcast(U8).indirect(src_list[:]))
         nc.vector.tensor_copy(dst_s[:], tab_s[:].bitcast(U8).indirect(dst_list[:]))
 
-        def gather_words(h):
+        def gather_words(h, tag):
             cols = slice(h * HALF // LANES, (h + 1) * HALF // LANES)
-            nc.vector.tensor_copy(dst_w[h][:], tab_w[:].bitcast(U32).indirect(dst_list[:, cols]))
-            nc.vector.tensor_copy(src_w[h][:], tab_w[:].bitcast(U32).indirect(src_list[:, cols]))
+            words = held.tile([P, 2, HALF], U32, align_bytes=64, name="words%d" % h, tag=tag)
+            nc.vector.tensor_copy(words[:, 0, :], tab_w[:].bitcast(U32).indirect(dst_list[:, cols]))
+            nc.vector.tensor_copy(words[:, 1, :], tab_w[:].bitcast(U32).indirect(src_list[:, cols]))
+            return words
+
+        edge_w = [gather_words(0, "first")]
+        nc.vector.quantize_mx(
+            out=wc_w[:].bitcast(FP8X4), scales=wc_s[:], in_=wc_bf[:].rearrange("p n i -> p (n i)")
+        )
+        edge_w.append(gather_words(1, "shared"))
+        picked = [held.tile([P, J], F32, name="picked%d" % b) for b in range(BLOCKS)]
+        for b in range(BLOCKS):
+            nc.vector.tensor_copy(picked[b][:], state[b][:].indirect(dst_list[:]))
+
+        def square(h, s):
+            return slice(h * HALF + s * P, h * HALF + (s + 1) * P)
+
+        product_banks = [psum.tile([P, HALF], F32, name="product%d" % i) for i in range(2)]
+        turned_banks = [psum.tile([P, HALF], F32, name="turned%d" % i) for i in range(3)]
+        back_banks = [psum.tile([P, HALF], F32, name="back%d" % i) for i in range(3)]
+        spare = back_banks[0]
+        nc.tensor.transpose(spare[:, 0:P], weight_rows[:], identity[:])
+        nc.scalar.copy(weight_col[:], spare[:, 0 : J // P])
 
         def products(b, h):
             n = slice(b * P, (b + 1) * P)
             j = slice(h * HALF, (h + 1) * HALF)
-            za = psum.tile([P, HALF], F32)
-            ms = psum.tile([P, HALF], F32)
+            za, ms = product_banks[h], product_banks[1 - h]
             nc.tensor.matmul_mx(
-                za[:], lhsT=wa_w[:, n].bitcast(FP8X4), lhsT_scale=wa_s[:].bitcast(U8)[:, n],
-                rhs=dst_w[h][:].bitcast(FP8X4), rhs_scale=dst_s[:, j], start=True, stop=False,
+                za[:], lhsT=wa_w[:, n].bitcast(FP8X4), lhsT_scale=wa_s.bitcast(U8)[:, n],
+                rhs=edge_w[h][:, 0, :].bitcast(FP8X4), rhs_scale=dst_s[:, j], start=True, stop=False,
             )
             nc.tensor.matmul_mx(
-                za[:], lhsT=wb_w[:, n].bitcast(FP8X4), lhsT_scale=wb_s[:].bitcast(U8)[:, n],
-                rhs=src_w[h][:].bitcast(FP8X4), rhs_scale=src_s[:, j], start=False, stop=True,
+                za[:], lhsT=wb_w[:, n].bitcast(FP8X4), lhsT_scale=wb_s.bitcast(U8)[:, n],
+                rhs=edge_w[h][:, 1, :].bitcast(FP8X4), rhs_scale=src_s[:, j], start=False, stop=True,
             )
             nc.tensor.matmul_mx(
                 ms[:], lhsT=wc_w[:, n].bitcast(FP8X4), lhsT_scale=wc_s[:, n],
-                rhs=src_w[h][:].bitcast(FP8X4), rhs_scale=src_s[:, j], start=True, stop=True,
+                rhs=edge_w[h][:, 1, :].bitcast(FP8X4), rhs_scale=src_s[:, j], start=True, stop=True,
             )
-            nc.scalar.activation(gate[b][:, j], za[:], SIGMOID)
-            nc.scalar.copy(message[b][:, j], ms[:])
+            nc.scalar.activation(gate[:, j], za[:], SIGMOID)
+            nc.scalar.copy(message[:, j], ms[:])
 
-        def gate_message(b, j):
-            nc.gpsimd.tensor_tensor(gated[b][:, j], gate[b][:, j], message[b][:, j], MULT)
+        def finish(b, h):
+            j = slice(h * HALF, (h + 1) * HALF)
+            nc.gpsimd.tensor_tensor(gated[:, j], gate[:, j], message[:, j], MULT)
+            turned, back = turned_banks[(2 * b + h) % 3], back_banks[(2 * b + h) % 3]
+            for s in range(SQUARES):
+                nc.tensor.matmul(
+                    turned[:, s * P : (s + 1) * P], gated[:, square(h, s)], identity[:], start=True, stop=False, is_transpose=True
+                )
+                nc.tensor.matmul(
+                    turned[:, s * P : (s + 1) * P], picked[b][:, square(h, s)], identity[:], start=False, stop=True, is_transpose=True
+                )
+            weighted = ring.tile([P, SQUARES, P], F32)
+            for s in range(SQUARES):
+                c = h * SQUARES + s
+                nc.scalar.activation(weighted[:, s, :], turned[:, s * P : (s + 1) * P], COPY, scale=weight_col[:, c : c + 1])
+            for s in range(SQUARES):
+                nc.tensor.transpose(back[:, s * P : (s + 1) * P], weighted[:, s, :], identity[:])
+            nc.scalar.copy(result[b][:, j], back[:])
 
-        def add_state(b, j):
-            nc.gpsimd.tensor_tensor(summed[:, j], gated[b][:, j], picked[b][:, j], ADD)
-            if b < BLOCKS - 1:
-                nc.gpsimd.tensor_tensor(weighted[b][:, j], summed[:, j], weight[:, j], MULT)
-
-        def quantize(i):
-            n = slice(i * N // 2, (i + 1) * N // 2)
-            nc.vector.quantize_mx(
-                out=wc_w[:, n].bitcast(FP8X4), scales=wc_s[:, n], in_=wc_bf[:, n, :].rearrange("p n i -> p (n i)")
-            )
-
-        quantize(0)
-        gather_words(0)
-        gather_words(1)
-        quantize(1)
         for b in range(BLOCKS):
-            nc.vector.tensor_copy(picked[b][:], state[b][:].indirect(dst_list[:]))
-
-        first, second, both = slice(0, HALF), slice(HALF, J), slice(0, J)
-        products(0, 0)
-        gate_message(0, first)
-        products(1, 0)
-        gate_message(1, first)
-        add_state(0, first)
-        products(0, 1)
-        gate_message(0, second)
-        add_state(0, second)
-        products(1, 1)
-        gate_message(1, second)
-        add_state(1, both)
-        for b in range(2, BLOCKS):
-            products(b, 0)
-            products(b, 1)
-            gate_message(b, both)
-            add_state(b, both)
+            for h in range(HALVES):
+                products(b, h)
+                finish(b, h)
 
         for b in range(BLOCKS):
             window = placed[b % 2]
-            if b == 0:
-                for h in range(HALVES):
-                    cols = slice(h * HALF // LANES, (h + 1) * HALF // LANES)
-                    nc.vector.tensor_copy(
-                        window[:].indirect(dst_list[:, cols]), weighted[b][:, h * HALF : (h + 1) * HALF]
-                    )
-            elif b < BLOCKS - 1:
-                nc.vector.tensor_copy(window[:].indirect(dst_list[:]), weighted[b][:])
-            else:
-                nc.vector.tensor_tensor(window[:].indirect(dst_list[:]), summed[:], weight[:], MULT)
+            for h in range(HALVES):
+                cols = slice(h * HALF // LANES, (h + 1) * HALF // LANES)
+                nc.vector.tensor_copy(window[:].indirect(dst_list[:, cols]), result[b][:, h * HALF : (h + 1) * HALF])
             nc.sync.dma_start(out=out[b * P : (b + 1) * P, :], in_=window[:])

@@ -19,11 +19,20 @@ COPY = mybir.ActivationFunctionType.Copy
 
 P = 128
 PACK = 4
-BLOCKS = N // P
+QUADRANT = 32
+SCALE_ROWS = K // 32
+LIST_ROWS = 16
+ROW_BLOCKS = N // P
 HALF = 512
 HALVES = J // HALF
 SQUARES = HALF // P
-LANES = 16
+RING = 2
+TURN_BANKS = 3
+WINDOWS = 3
+
+PIECES = [(pair + i, h) for pair in range(0, ROW_BLOCKS, 2) for h in range(HALVES) for i in range(2)]
+
+GATE, MESSAGE, GATED = range(3)
 
 
 def tile_list_rgg_L_kernel(
@@ -34,25 +43,34 @@ def tile_list_rgg_L_kernel(
     def words_of(packed):
         return packed[0].rearrange("p n t -> p (n t)").bitcast(I32)
 
-    def load_scales(plane, scales):
-        for r in range(4):
-            nc.sync.dma_start(out=plane[r:P:32, :], in_=scales[0, r:16:4, :].bitcast(I32))
+    def load_scales(dest, scales):
+        for r in range(PACK):
+            nc.sync.dma_start(out=dest[r:P:QUADRANT, :], in_=scales[0, r:SCALE_ROWS:PACK, :].bitcast(I32))
+
+    def rows(b):
+        return slice(b * P, (b + 1) * P)
+
+    def edges(h):
+        return slice(h * HALF, (h + 1) * HALF)
+
+    def list_columns(h):
+        return slice(h * HALF // LIST_ROWS, (h + 1) * HALF // LIST_ROWS)
 
     with ExitStack() as ctx:
         held = ctx.enter_context(tc.tile_pool(name="held", bufs=1))
-        ring = ctx.enter_context(tc.tile_pool(name="ring", bufs=2))
+        ring = ctx.enter_context(tc.tile_pool(name="ring", bufs=RING))
         psum = ctx.enter_context(tc.psum_pool(name="psum", bufs=1))
 
-        src_list = held.tile([P, J // LANES], U16)
-        dst_list = held.tile([P, J // LANES], U16)
-        tab_s = held.tile([P, T // 4], I32, align_bytes=64)
+        src_list = held.tile([P, J // LIST_ROWS], U16)
+        dst_list = held.tile([P, J // LIST_ROWS], U16)
+        tab_s = held.tile([P, T // PACK], I32, align_bytes=64)
         tab_w = held.tile([P, T], I32, align_bytes=64)
-        w_s = held.tile([P, 2, N // 4], I32, align_bytes=64)
+        w_s = held.tile([P, 2, N // PACK], I32, align_bytes=64)
         wa_s, wb_s = w_s[:, 0, :], w_s[:, 1, :]
         wa_w = held.tile([P, N], I32, align_bytes=64)
         wb_w = held.tile([P, N], I32, align_bytes=64)
         wc_raw = held.tile([P, PACK, N], F32)
-        wc_bf = held.tile([P, N, PACK], BF16, align_bytes=64, tag="shared")
+        wc_bf = held.tile([P, N, PACK], BF16, align_bytes=64, tag="wc_bf")
         wc_w = held.tile([P, N], U32, align_bytes=64)
         wc_s = held.tile([P, N], U8, align_bytes=64)
         weight_rows = held.tile([P, P], F32)
@@ -60,22 +78,16 @@ def tile_list_rgg_L_kernel(
         identity = held.tile([P, P], F32)
         src_s = held.tile([P, J], U8, align_bytes=64)
         dst_s = held.tile([P, J], U8, align_bytes=64)
-        state = [held.tile([P, T], F32, name="state%d" % b) for b in range(BLOCKS)]
-        gate = held.tile([P, J], F32)
-        message = held.tile([P, J], F32)
-        gated = held.tile([P, J], F32)
-        result = [held.tile([P, J], F32, name="result%d" % b) for b in range(BLOCKS)]
-        placed = [held.tile([P, T], F32, name="placed%d" % i) for i in range(2)]
-        warm = held.tile([P, 1], F32)
-        warm_out = held.tile([P, 1], F32)
+        state = [held.tile([P, T], F32, name="state%d" % b, tag="state%d" % b) for b in range(ROW_BLOCKS)]
+        early = held.tile([P, 3, RING, HALF], F32)
+        later_results = held.tile([P, len(PIECES) - 2, HALF], F32)
+        placed = [held.tile([P, T], F32, name="placed%d" % i) for i in range(WINDOWS)]
 
         nc.gpsimd.memset(tab_s[:], 0)
         nc.gpsimd.memset(w_s[:], 0)
-        nc.gpsimd.memset(warm[:], 0.0)
-        nc.scalar.activation(warm_out[:], warm[:], SIGMOID)
         make_identity(nc, identity[:])
-        for tile in placed:
-            nc.gpsimd.memset(tile[:], 0.0)
+        for window in placed:
+            nc.gpsimd.memset(window[:], 0.0)
 
         nc.sync.dma_start(src_list[:], offs)
         nc.sync.dma_start(dst_list[:], offs2)
@@ -83,13 +95,13 @@ def tile_list_rgg_L_kernel(
         nc.sync.dma_start(out=tab_w[:], in_=words_of(tab_words))
         nc.sync.dma_start(out=wc_raw[:], in_=wc.rearrange("(p i) n -> p i n", i=PACK))
         load_scales(wa_s, wa_scales)
-        load_scales(wb_s, wb_scales)
         nc.sync.dma_start(out=wa_w[:], in_=words_of(wa_words))
         nc.sync.dma_start(out=wb_w[:], in_=words_of(wb_words))
-        nc.sync.dma_start(out=state[0][:], in_=rT[0:P, :])
+        nc.sync.dma_start(out=state[0][:], in_=rT[rows(0), :])
+        load_scales(wb_s, wb_scales)
         nc.sync.dma_start(out=weight_rows[:], in_=wgo[0 : P * P // J, :].rearrange("r (c j) -> (r c) j", j=P))
-        for b in range(1, BLOCKS):
-            nc.sync.dma_start(out=state[b][:], in_=rT[b * P : (b + 1) * P, :])
+        for b in (1, 3, 2):
+            nc.sync.dma_start(out=state[b][:], in_=rT[rows(b), :])
 
         nc.scalar.copy(
             wc_bf[:].rearrange("p (c m) i -> p c i m", m=PACK), wc_raw[:].rearrange("p i (c m) -> p c i m", m=PACK)
@@ -99,77 +111,80 @@ def tile_list_rgg_L_kernel(
         nc.vector.tensor_copy(dst_s[:], tab_s[:].bitcast(U8).indirect(dst_list[:]))
 
         def gather_words(h, tag):
-            cols = slice(h * HALF // LANES, (h + 1) * HALF // LANES)
             words = held.tile([P, 2, HALF], U32, align_bytes=64, name="words%d" % h, tag=tag)
-            nc.vector.tensor_copy(words[:, 0, :], tab_w[:].bitcast(U32).indirect(dst_list[:, cols]))
-            nc.vector.tensor_copy(words[:, 1, :], tab_w[:].bitcast(U32).indirect(src_list[:, cols]))
+            nc.vector.tensor_copy(words[:, 0, :], tab_w[:].bitcast(U32).indirect(dst_list[:, list_columns(h)]))
+            nc.vector.tensor_copy(words[:, 1, :], tab_w[:].bitcast(U32).indirect(src_list[:, list_columns(h)]))
             return words
 
-        edge_w = [gather_words(0, "first")]
-        nc.vector.quantize_mx(
-            out=wc_w[:].bitcast(FP8X4), scales=wc_s[:], in_=wc_bf[:].rearrange("p n i -> p (n i)")
-        )
-        edge_w.append(gather_words(1, "shared"))
-        picked = [held.tile([P, J], F32, name="picked%d" % b) for b in range(BLOCKS)]
-        for b in range(BLOCKS):
-            nc.vector.tensor_copy(picked[b][:], state[b][:].indirect(dst_list[:]))
+        edge_w = [gather_words(0, "words0")]
+        nc.vector.quantize_mx(out=wc_w[:].bitcast(FP8X4), scales=wc_s[:], in_=wc_bf[:].rearrange("p n i -> p (n i)"))
+        edge_w.append(gather_words(1, "wc_bf"))
 
-        def square(h, s):
-            return slice(h * HALF + s * P, h * HALF + (s + 1) * P)
+        picked = []
+        for b in range(ROW_BLOCKS - 1):
+            picked.append(held.tile([P, J], F32, name="picked%d" % b)[:])
+            nc.vector.tensor_copy(picked[b], state[b][:].indirect(dst_list[:]))
+        late = held.tile([P, 5, J], F32, tag="state2")
+        picked.append(late[:, 0, :])
+        nc.vector.tensor_copy(picked[3], state[3][:].indirect(dst_list[:]))
+        result = [late[:, 1, edges(0)], late[:, 1, edges(1)]]
+        result += [later_results[:, u, :] for u in range(len(PIECES) - 2)]
 
-        product_banks = [psum.tile([P, HALF], F32, name="product%d" % i) for i in range(2)]
-        turned_banks = [psum.tile([P, HALF], F32, name="turned%d" % i) for i in range(3)]
-        back_banks = [psum.tile([P, HALF], F32, name="back%d" % i) for i in range(3)]
-        spare = back_banks[0]
-        nc.tensor.transpose(spare[:, 0:P], weight_rows[:], identity[:])
-        nc.scalar.copy(weight_col[:], spare[:, 0 : J // P])
+        first_late = {GATE: 3, MESSAGE: 3, GATED: 2}
 
-        def products(b, h):
-            n = slice(b * P, (b + 1) * P)
-            j = slice(h * HALF, (h + 1) * HALF)
-            za, ms = product_banks[h], product_banks[1 - h]
+        def buffer(kind, u):
+            if u < first_late[kind]:
+                return early[:, kind, u % RING, :]
+            return late[:, 2 + kind, edges(u % RING)]
+
+        za = psum.tile([P, HALF], F32)
+        ms = psum.tile([P, HALF], F32)
+        turned_banks = [psum.tile([P, HALF], F32, name="turned%d" % i) for i in range(TURN_BANKS)]
+        back_banks = [psum.tile([P, HALF], F32, name="back%d" % i) for i in range(TURN_BANKS)]
+
+        nc.tensor.transpose(back_banks[0][:, 0:P], weight_rows[:], identity[:])
+        nc.scalar.copy(weight_col[:], back_banks[0][:, 0 : J // P])
+
+        for u, (b, h) in enumerate(PIECES):
+            n, j = rows(b), edges(h)
+            dst_w, src_w = edge_w[h][:, 0, :].bitcast(FP8X4), edge_w[h][:, 1, :].bitcast(FP8X4)
             nc.tensor.matmul_mx(
                 za[:], lhsT=wa_w[:, n].bitcast(FP8X4), lhsT_scale=wa_s.bitcast(U8)[:, n],
-                rhs=edge_w[h][:, 0, :].bitcast(FP8X4), rhs_scale=dst_s[:, j], start=True, stop=False,
+                rhs=dst_w, rhs_scale=dst_s[:, j], start=True, stop=False,
             )
             nc.tensor.matmul_mx(
                 za[:], lhsT=wb_w[:, n].bitcast(FP8X4), lhsT_scale=wb_s.bitcast(U8)[:, n],
-                rhs=edge_w[h][:, 1, :].bitcast(FP8X4), rhs_scale=src_s[:, j], start=False, stop=True,
+                rhs=src_w, rhs_scale=src_s[:, j], start=False, stop=True,
             )
             nc.tensor.matmul_mx(
                 ms[:], lhsT=wc_w[:, n].bitcast(FP8X4), lhsT_scale=wc_s[:, n],
-                rhs=edge_w[h][:, 1, :].bitcast(FP8X4), rhs_scale=src_s[:, j], start=True, stop=True,
+                rhs=src_w, rhs_scale=src_s[:, j], start=True, stop=True,
             )
-            nc.scalar.activation(gate[:, j], za[:], SIGMOID)
-            nc.scalar.copy(message[:, j], ms[:])
+            gate, message, gated = buffer(GATE, u), buffer(MESSAGE, u), buffer(GATED, u)
+            nc.scalar.activation(gate, za[:], SIGMOID)
+            nc.scalar.copy(message, ms[:])
+            nc.gpsimd.tensor_tensor(gated, gate, message, MULT)
 
-        def finish(b, h):
-            j = slice(h * HALF, (h + 1) * HALF)
-            nc.gpsimd.tensor_tensor(gated[:, j], gate[:, j], message[:, j], MULT)
-            turned, back = turned_banks[(2 * b + h) % 3], back_banks[(2 * b + h) % 3]
+            turned, back = turned_banks[u % TURN_BANKS], back_banks[u % TURN_BANKS]
+            residual = picked[b][:, j]
             for s in range(SQUARES):
+                square = rows(s)
                 nc.tensor.matmul(
-                    turned[:, s * P : (s + 1) * P], gated[:, square(h, s)], identity[:], start=True, stop=False, is_transpose=True
+                    turned[:, square], gated[:, square], identity[:], start=True, stop=False, is_transpose=True
                 )
                 nc.tensor.matmul(
-                    turned[:, s * P : (s + 1) * P], picked[b][:, square(h, s)], identity[:], start=False, stop=True, is_transpose=True
+                    turned[:, square], residual[:, square], identity[:], start=False, stop=True, is_transpose=True
                 )
             weighted = ring.tile([P, SQUARES, P], F32)
             for s in range(SQUARES):
                 c = h * SQUARES + s
-                nc.scalar.activation(weighted[:, s, :], turned[:, s * P : (s + 1) * P], COPY, scale=weight_col[:, c : c + 1])
+                nc.scalar.activation(weighted[:, s, :], turned[:, rows(s)], COPY, scale=weight_col[:, c : c + 1])
             for s in range(SQUARES):
-                nc.tensor.transpose(back[:, s * P : (s + 1) * P], weighted[:, s, :], identity[:])
-            nc.scalar.copy(result[b][:, j], back[:])
+                nc.tensor.transpose(back[:, rows(s)], weighted[:, s, :], identity[:])
+            nc.scalar.copy(result[u], back[:])
 
-        for b in range(BLOCKS):
-            for h in range(HALVES):
-                products(b, h)
-                finish(b, h)
-
-        for b in range(BLOCKS):
-            window = placed[b % 2]
-            for h in range(HALVES):
-                cols = slice(h * HALF // LANES, (h + 1) * HALF // LANES)
-                nc.vector.tensor_copy(window[:].indirect(dst_list[:, cols]), result[b][:, h * HALF : (h + 1) * HALF])
-            nc.sync.dma_start(out=out[b * P : (b + 1) * P, :], in_=window[:])
+        for u, (b, h) in enumerate(PIECES):
+            window = placed[b % WINDOWS]
+            nc.vector.tensor_copy(window[:].indirect(dst_list[:, list_columns(h)]), result[u])
+            if h == HALVES - 1:
+                nc.sync.dma_start(out=out[rows(b), :], in_=window[:])

@@ -19,8 +19,11 @@ COPY = mybir.ActivationFunctionType.Copy
 
 P = 128
 PACK = 4
+MX_BLOCK = 32
+SCALE_ROWS = K // MX_BLOCK
 QUADRANT = 32
-SCALE_ROWS = K // 32
+GROUP_ROWS = QUADRANT * PACK // MX_BLOCK
+COLUMN_RUN = 4
 LIST_ROWS = 16
 ROW_BLOCKS = N // P
 HALF = 512
@@ -29,10 +32,13 @@ SQUARES = HALF // P
 RING = 2
 TURN_BANKS = 3
 WINDOWS = 3
+LAST, NEXT_TO_LAST = ROW_BLOCKS - 1, ROW_BLOCKS - 2
+FIRST_PIECES = 2
 
 PIECES = [(pair + i, h) for pair in range(0, ROW_BLOCKS, 2) for h in range(HALVES) for i in range(2)]
 
-GATE, MESSAGE, GATED = range(3)
+KINDS = 3
+GATE, MESSAGE, GATED = range(KINDS)
 
 
 def tile_list_rgg_L_kernel(
@@ -44,14 +50,14 @@ def tile_list_rgg_L_kernel(
         return packed[0].rearrange("p n t -> p (n t)").bitcast(I32)
 
     def load_scales(dest, scales):
-        for r in range(PACK):
-            nc.sync.dma_start(out=dest[r:P:QUADRANT, :], in_=scales[0, r:SCALE_ROWS:PACK, :].bitcast(I32))
+        for r in range(GROUP_ROWS):
+            nc.sync.dma_start(out=dest[r:P:QUADRANT, :], in_=scales[0, r:SCALE_ROWS:GROUP_ROWS, :].bitcast(I32))
 
-    def rows(b):
-        return slice(b * P, (b + 1) * P)
+    def run_of_128(i):
+        return slice(i * P, (i + 1) * P)
 
-    def edges(h):
-        return slice(h * HALF, (h + 1) * HALF)
+    def run_of_512(i):
+        return slice(i * HALF, (i + 1) * HALF)
 
     def list_columns(h):
         return slice(h * HALF // LIST_ROWS, (h + 1) * HALF // LIST_ROWS)
@@ -79,8 +85,8 @@ def tile_list_rgg_L_kernel(
         src_s = held.tile([P, J], U8, align_bytes=64)
         dst_s = held.tile([P, J], U8, align_bytes=64)
         state = [held.tile([P, T], F32, name="state%d" % b, tag="state%d" % b) for b in range(ROW_BLOCKS)]
-        early = held.tile([P, 3, RING, HALF], F32)
-        later_results = held.tile([P, len(PIECES) - 2, HALF], F32)
+        early = held.tile([P, KINDS, RING, HALF], F32)
+        later_results = held.tile([P, len(PIECES) - FIRST_PIECES, HALF], F32)
         placed = [held.tile([P, T], F32, name="placed%d" % i) for i in range(WINDOWS)]
 
         nc.gpsimd.memset(tab_s[:], 0)
@@ -97,14 +103,17 @@ def tile_list_rgg_L_kernel(
         load_scales(wa_s, wa_scales)
         nc.sync.dma_start(out=wa_w[:], in_=words_of(wa_words))
         nc.sync.dma_start(out=wb_w[:], in_=words_of(wb_words))
-        nc.sync.dma_start(out=state[0][:], in_=rT[rows(0), :])
+        nc.sync.dma_start(out=state[0][:], in_=rT[run_of_128(0), :])
         load_scales(wb_s, wb_scales)
         nc.sync.dma_start(out=weight_rows[:], in_=wgo[0 : P * P // J, :].rearrange("r (c j) -> (r c) j", j=P))
-        for b in (1, 3, 2):
-            nc.sync.dma_start(out=state[b][:], in_=rT[rows(b), :])
+        nc.sync.dma_start(out=state[1][:], in_=rT[run_of_128(1), :])
+        nc.sync.dma_start(out=state[LAST][:, 0 : T // 2], in_=rT[run_of_128(LAST), 0 : T // 2])
+        nc.sync.dma_start(out=state[NEXT_TO_LAST][:], in_=rT[run_of_128(NEXT_TO_LAST), :])
+        nc.sync.dma_start(out=state[LAST][:, T // 2 : T], in_=rT[run_of_128(LAST), T // 2 : T])
 
         nc.scalar.copy(
-            wc_bf[:].rearrange("p (c m) i -> p c i m", m=PACK), wc_raw[:].rearrange("p i (c m) -> p c i m", m=PACK)
+            wc_bf[:].rearrange("p (c m) i -> p c i m", m=COLUMN_RUN),
+            wc_raw[:].rearrange("p i (c m) -> p c i m", m=COLUMN_RUN),
         )
 
         nc.vector.tensor_copy(src_s[:], tab_s[:].bitcast(U8).indirect(src_list[:]))
@@ -121,21 +130,22 @@ def tile_list_rgg_L_kernel(
         edge_w.append(gather_words(1, "wc_bf"))
 
         picked = []
-        for b in range(ROW_BLOCKS - 1):
+        for b in range(LAST):
             picked.append(held.tile([P, J], F32, name="picked%d" % b)[:])
             nc.vector.tensor_copy(picked[b], state[b][:].indirect(dst_list[:]))
-        late = held.tile([P, 5, J], F32, tag="state2")
-        picked.append(late[:, 0, :])
-        nc.vector.tensor_copy(picked[3], state[3][:].indirect(dst_list[:]))
-        result = [late[:, 1, edges(0)], late[:, 1, edges(1)]]
-        result += [later_results[:, u, :] for u in range(len(PIECES) - 2)]
+        late = held.tile([P, 2 + KINDS, J], F32, tag="state%d" % NEXT_TO_LAST)
+        late_picked, late_results, late_buffers = late[:, 0, :], late[:, 1, :], late[:, 2:, :]
+        picked.append(late_picked)
+        nc.vector.tensor_copy(picked[LAST], state[LAST][:].indirect(dst_list[:]))
+        result = [late_results[:, run_of_512(u)] for u in range(FIRST_PIECES)]
+        result += [later_results[:, u, :] for u in range(len(PIECES) - FIRST_PIECES)]
 
-        first_late = {GATE: 3, MESSAGE: 3, GATED: 2}
+        first_late = {GATE: FIRST_PIECES + 1, MESSAGE: FIRST_PIECES + 1, GATED: FIRST_PIECES}
 
         def buffer(kind, u):
             if u < first_late[kind]:
                 return early[:, kind, u % RING, :]
-            return late[:, 2 + kind, edges(u % RING)]
+            return late_buffers[:, kind, run_of_512(u % RING)]
 
         za = psum.tile([P, HALF], F32)
         ms = psum.tile([P, HALF], F32)
@@ -146,7 +156,7 @@ def tile_list_rgg_L_kernel(
         nc.scalar.copy(weight_col[:], back_banks[0][:, 0 : J // P])
 
         for u, (b, h) in enumerate(PIECES):
-            n, j = rows(b), edges(h)
+            n, j = run_of_128(b), run_of_512(h)
             dst_w, src_w = edge_w[h][:, 0, :].bitcast(FP8X4), edge_w[h][:, 1, :].bitcast(FP8X4)
             nc.tensor.matmul_mx(
                 za[:], lhsT=wa_w[:, n].bitcast(FP8X4), lhsT_scale=wa_s.bitcast(U8)[:, n],
@@ -168,7 +178,7 @@ def tile_list_rgg_L_kernel(
             turned, back = turned_banks[u % TURN_BANKS], back_banks[u % TURN_BANKS]
             residual = picked[b][:, j]
             for s in range(SQUARES):
-                square = rows(s)
+                square = run_of_128(s)
                 nc.tensor.matmul(
                     turned[:, square], gated[:, square], identity[:], start=True, stop=False, is_transpose=True
                 )
@@ -178,13 +188,13 @@ def tile_list_rgg_L_kernel(
             weighted = ring.tile([P, SQUARES, P], F32)
             for s in range(SQUARES):
                 c = h * SQUARES + s
-                nc.scalar.activation(weighted[:, s, :], turned[:, rows(s)], COPY, scale=weight_col[:, c : c + 1])
+                nc.scalar.activation(weighted[:, s, :], turned[:, run_of_128(s)], COPY, scale=weight_col[:, c : c + 1])
             for s in range(SQUARES):
-                nc.tensor.transpose(back[:, rows(s)], weighted[:, s, :], identity[:])
+                nc.tensor.transpose(back[:, run_of_128(s)], weighted[:, s, :], identity[:])
             nc.scalar.copy(result[u], back[:])
 
         for u, (b, h) in enumerate(PIECES):
             window = placed[b % WINDOWS]
             nc.vector.tensor_copy(window[:].indirect(dst_list[:, list_columns(h)]), result[u])
             if h == HALVES - 1:
-                nc.sync.dma_start(out=out[rows(b), :], in_=window[:])
+                nc.sync.dma_start(out=out[run_of_128(b), :], in_=window[:])

@@ -14,6 +14,7 @@ U16 = mybir.dt.uint16
 U8 = mybir.dt.uint8
 FP8X4 = mybir.dt.float8_e4m3fn_x4
 MULT = mybir.AluOpType.mult
+ADD = mybir.AluOpType.add
 SIGMOID = mybir.ActivationFunctionType.Sigmoid
 COPY = mybir.ActivationFunctionType.Copy
 
@@ -35,7 +36,11 @@ WINDOWS = 3
 LAST, NEXT_TO_LAST = ROW_BLOCKS - 1, ROW_BLOCKS - 2
 FIRST_PIECES = 2
 
-PIECES = [(pair + i, h) for pair in range(0, ROW_BLOCKS, 2) for h in range(HALVES) for i in range(2)]
+PIECES = [(b, h) for h in range(HALVES) for b in range(2)]
+PIECES = PIECES + [(b, h) for b in range(2, ROW_BLOCKS) for h in range(HALVES)]
+TURNED = [u for u in range(FIRST_PIECES, len(PIECES)) if PIECES[u][0] != NEXT_TO_LAST]
+FIRST_LATE = 3
+CAST_SPLIT = 320
 
 KINDS = 3
 GATE, MESSAGE, GATED = range(KINDS)
@@ -75,18 +80,19 @@ def tile_list_rgg_L_kernel(
         wa_s, wb_s = w_s[:, 0, :], w_s[:, 1, :]
         wa_w = held.tile([P, N], I32, align_bytes=64)
         wb_w = held.tile([P, N], I32, align_bytes=64)
-        wc_raw = held.tile([P, PACK, N], F32)
+        wc_raw = held.tile([P, PACK, N], F32, tag="wc_raw", align_bytes=64)
         wc_bf = held.tile([P, N, PACK], BF16, align_bytes=64, tag="wc_bf")
         wc_w = held.tile([P, N], U32, align_bytes=64)
         wc_s = held.tile([P, N], U8, align_bytes=64)
         weight_rows = held.tile([P, P], F32)
         weight_col = held.tile([P, J // P], F32)
         identity = held.tile([P, P], F32)
+        weight_all = held.tile([P, J], F32)
         src_s = held.tile([P, J], U8, align_bytes=64)
         dst_s = held.tile([P, J], U8, align_bytes=64)
         state = [held.tile([P, T], F32, name="state%d" % b, tag="state%d" % b) for b in range(ROW_BLOCKS)]
-        early = held.tile([P, KINDS, RING, HALF], F32)
-        later_results = held.tile([P, len(PIECES) - FIRST_PIECES, HALF], F32)
+        early = held.tile([P, KINDS, len(PIECES), HALF], F32)
+        results = held.tile([P, len(PIECES), HALF], F32)
         placed = [held.tile([P, T], F32, name="placed%d" % i) for i in range(WINDOWS)]
 
         nc.gpsimd.memset(tab_s[:], 0)
@@ -94,58 +100,62 @@ def tile_list_rgg_L_kernel(
         make_identity(nc, identity[:])
         for window in placed:
             nc.gpsimd.memset(window[:], 0.0)
+        warm = held.tile([P, 1], F32)
+        nc.scalar.activation(warm[:], placed[0][:, 0:1], SIGMOID)
 
         nc.sync.dma_start(src_list[:], offs)
         nc.sync.dma_start(dst_list[:], offs2)
         load_scales(tab_s, tab_scales)
         nc.sync.dma_start(out=tab_w[:], in_=words_of(tab_words))
-        nc.sync.dma_start(out=wc_raw[:], in_=wc.rearrange("(p i) n -> p i n", i=PACK))
-        load_scales(wa_s, wa_scales)
         nc.sync.dma_start(out=wa_w[:], in_=words_of(wa_words))
         nc.sync.dma_start(out=wb_w[:], in_=words_of(wb_words))
-        nc.sync.dma_start(out=state[0][:], in_=rT[run_of_128(0), :])
+        load_scales(wa_s, wa_scales)
+        nc.sync.dma_start(out=wc_raw[:], in_=wc.rearrange("(p i) n -> p i n", i=PACK))
         load_scales(wb_s, wb_scales)
+        nc.sync.dma_start(out=state[0][:], in_=rT[run_of_128(0), :])
         nc.sync.dma_start(out=weight_rows[:], in_=wgo[0 : P * P // J, :].rearrange("r (c j) -> (r c) j", j=P))
         nc.sync.dma_start(out=state[1][:], in_=rT[run_of_128(1), :])
-        nc.sync.dma_start(out=state[LAST][:, 0 : T // 2], in_=rT[run_of_128(LAST), 0 : T // 2])
+        nc.sync.dma_start(out=state[LAST][:, 0 : 3 * T // 4], in_=rT[run_of_128(LAST), 0 : 3 * T // 4])
         nc.sync.dma_start(out=state[NEXT_TO_LAST][:], in_=rT[run_of_128(NEXT_TO_LAST), :])
-        nc.sync.dma_start(out=state[LAST][:, T // 2 : T], in_=rT[run_of_128(LAST), T // 2 : T])
+        nc.sync.dma_start(out=weight_all[:, run_of_512(0)], in_=wgo[:, run_of_512(0)])
+        nc.sync.dma_start(out=state[LAST][:, 3 * T // 4 : T], in_=rT[run_of_128(LAST), 3 * T // 4 : T])
+        nc.sync.dma_start(out=weight_all[:, run_of_512(1)], in_=wgo[:, run_of_512(1)])
 
         nc.scalar.copy(
-            wc_bf[:].rearrange("p (c m) i -> p c i m", m=COLUMN_RUN),
-            wc_raw[:].rearrange("p i (c m) -> p c i m", m=COLUMN_RUN),
+            wc_bf[:, 0:CAST_SPLIT, :].rearrange("p (c m) i -> p c i m", m=COLUMN_RUN),
+            wc_raw[:, :, 0:CAST_SPLIT].rearrange("p i (c m) -> p c i m", m=COLUMN_RUN),
+        )
+        nc.gpsimd.tensor_scalar(
+            wc_bf[:, CAST_SPLIT:N, :], wc_raw[:, :, CAST_SPLIT:N].rearrange("p i n -> p n i"), 1.0, 0.0, MULT, ADD
         )
 
         nc.vector.tensor_copy(src_s[:], tab_s[:].bitcast(U8).indirect(src_list[:]))
         nc.vector.tensor_copy(dst_s[:], tab_s[:].bitcast(U8).indirect(dst_list[:]))
 
-        def gather_words(h, tag):
-            words = held.tile([P, 2, HALF], U32, align_bytes=64, name="words%d" % h, tag=tag)
-            nc.vector.tensor_copy(words[:, 0, :], tab_w[:].bitcast(U32).indirect(dst_list[:, list_columns(h)]))
-            nc.vector.tensor_copy(words[:, 1, :], tab_w[:].bitcast(U32).indirect(src_list[:, list_columns(h)]))
-            return words
+        def gather_words(entries, h, tag):
+            words = held.tile([P, HALF], U32, align_bytes=64, name=tag, tag=tag)
+            nc.vector.tensor_copy(words[:], tab_w[:].bitcast(U32).indirect(entries[:, list_columns(h)]))
+            return words[:].bitcast(FP8X4)
 
-        edge_w = [gather_words(0, "words0")]
+        dst_words = [gather_words(dst_list, 0, "dst0")]
+        src_words = [gather_words(src_list, 0, "src0")]
+        dst_words.append(gather_words(dst_list, 1, "dst1"))
         nc.vector.quantize_mx(out=wc_w[:].bitcast(FP8X4), scales=wc_s[:], in_=wc_bf[:].rearrange("p n i -> p (n i)"))
-        edge_w.append(gather_words(1, "wc_bf"))
+        src_words.append(gather_words(src_list, 1, "wc_raw"))
 
         picked = []
-        for b in range(LAST):
+        for b in range(ROW_BLOCKS):
             picked.append(held.tile([P, J], F32, name="picked%d" % b)[:])
             nc.vector.tensor_copy(picked[b], state[b][:].indirect(dst_list[:]))
-        late = held.tile([P, 2 + KINDS, J], F32, tag="state%d" % NEXT_TO_LAST)
-        late_picked, late_results, late_buffers = late[:, 0, :], late[:, 1, :], late[:, 2:, :]
-        picked.append(late_picked)
-        nc.vector.tensor_copy(picked[LAST], state[LAST][:].indirect(dst_list[:]))
-        result = [late_results[:, run_of_512(u)] for u in range(FIRST_PIECES)]
-        result += [later_results[:, u, :] for u in range(len(PIECES) - FIRST_PIECES)]
-
-        first_late = {GATE: FIRST_PIECES + 1, MESSAGE: FIRST_PIECES + 1, GATED: FIRST_PIECES}
+        late = held.tile([P, 3, J], F32, tag="state%d" % LAST)
+        late_gated = late[:].rearrange("p r j -> p (r j)")
+        result = [results[:, u, :] for u in range(len(PIECES))]
+        summed = [result[FIRST_PIECES + 1 - u] for u in range(FIRST_PIECES)]
 
         def buffer(kind, u):
-            if u < first_late[kind]:
-                return early[:, kind, u % RING, :]
-            return late_buffers[:, kind, run_of_512(u % RING)]
+            if u < FIRST_LATE or kind != GATED:
+                return early[:, kind, u, :]
+            return late_gated[:, run_of_512(u - FIRST_LATE)]
 
         za = psum.tile([P, HALF], F32)
         ms = psum.tile([P, HALF], F32)
@@ -155,9 +165,10 @@ def tile_list_rgg_L_kernel(
         nc.tensor.transpose(back_banks[0][:, 0:P], weight_rows[:], identity[:])
         nc.scalar.copy(weight_col[:], back_banks[0][:, 0 : J // P])
 
-        for u, (b, h) in enumerate(PIECES):
+        def products(u):
+            b, h = PIECES[u]
             n, j = run_of_128(b), run_of_512(h)
-            dst_w, src_w = edge_w[h][:, 0, :].bitcast(FP8X4), edge_w[h][:, 1, :].bitcast(FP8X4)
+            dst_w, src_w = dst_words[h], src_words[h]
             nc.tensor.matmul_mx(
                 za[:], lhsT=wa_w[:, n].bitcast(FP8X4), lhsT_scale=wa_s.bitcast(U8)[:, n],
                 rhs=dst_w, rhs_scale=dst_s[:, j], start=True, stop=False,
@@ -174,9 +185,16 @@ def tile_list_rgg_L_kernel(
             nc.scalar.activation(gate, za[:], SIGMOID)
             nc.scalar.copy(message, ms[:])
             nc.gpsimd.tensor_tensor(gated, gate, message, MULT)
+            if u < FIRST_PIECES:
+                nc.gpsimd.tensor_tensor(summed[u], gated, picked[b][:, j], ADD)
+                nc.gpsimd.tensor_tensor(result[u], summed[u], weight_all[:, j], MULT)
+            elif u not in TURNED:
+                nc.gpsimd.tensor_tensor(result[u], gated, picked[b][:, j], ADD)
 
+        def turn(u):
+            b, h = PIECES[u]
+            gated, residual = buffer(GATED, u), picked[b][:, run_of_512(h)]
             turned, back = turned_banks[u % TURN_BANKS], back_banks[u % TURN_BANKS]
-            residual = picked[b][:, j]
             for s in range(SQUARES):
                 square = run_of_128(s)
                 nc.tensor.matmul(
@@ -185,16 +203,30 @@ def tile_list_rgg_L_kernel(
                 nc.tensor.matmul(
                     turned[:, square], residual[:, square], identity[:], start=False, stop=True, is_transpose=True
                 )
-            weighted = ring.tile([P, SQUARES, P], F32)
+            weighted = ring.tile([P, HALF], F32, name="weighted")[:]
             for s in range(SQUARES):
                 c = h * SQUARES + s
-                nc.scalar.activation(weighted[:, s, :], turned[:, run_of_128(s)], COPY, scale=weight_col[:, c : c + 1])
+                nc.scalar.activation(weighted[:, run_of_128(s)], turned[:, run_of_128(s)], COPY, scale=weight_col[:, c : c + 1])
             for s in range(SQUARES):
-                nc.tensor.transpose(back[:, run_of_128(s)], weighted[:, s, :], identity[:])
+                nc.tensor.transpose(back[:, run_of_128(s)], weighted[:, run_of_128(s)], identity[:])
             nc.scalar.copy(result[u], back[:])
 
-        for u, (b, h) in enumerate(PIECES):
+        for u in range(len(PIECES)):
+            products(u)
+            if u in TURNED:
+                turn(u)
+
+        for u, (b, h) in enumerate(PIECES[: 2 * HALVES]):
             window = placed[b % WINDOWS]
             nc.vector.tensor_copy(window[:].indirect(dst_list[:, list_columns(h)]), result[u])
             if h == HALVES - 1:
                 nc.sync.dma_start(out=out[run_of_128(b), :], in_=window[:])
+        for b in range(2, ROW_BLOCKS):
+            window = placed[b % WINDOWS]
+            first = b * HALVES
+            both = results[:, first : first + HALVES, :].rearrange("p h j -> p (h j)")
+            if b == NEXT_TO_LAST:
+                nc.vector.tensor_tensor(window[:].indirect(dst_list[:]), both, weight_all[:], MULT)
+            else:
+                nc.vector.tensor_copy(window[:].indirect(dst_list[:]), both)
+            nc.sync.dma_start(out=out[run_of_128(b), :], in_=window[:])

@@ -115,8 +115,8 @@ def tile_list_rgg_L_kernel(
         nc.sync.dma_start(out=state[0][:], in_=rT[run_of_128(0), :])
         nc.sync.dma_start(out=weight_rows[:], in_=wgo[0 : P * P // J, :].rearrange("r (c j) -> (r c) j", j=P))
         nc.sync.dma_start(out=state[1][:], in_=rT[run_of_128(1), :])
-        nc.sync.dma_start(out=state[LAST][:, 0 : 3 * T // 4], in_=rT[run_of_128(LAST), 0 : 3 * T // 4])
         nc.sync.dma_start(out=state[NEXT_TO_LAST][:], in_=rT[run_of_128(NEXT_TO_LAST), :])
+        nc.sync.dma_start(out=state[LAST][:, 0 : 3 * T // 4], in_=rT[run_of_128(LAST), 0 : 3 * T // 4])
         nc.sync.dma_start(out=weight_all[:, run_of_512(0)], in_=wgo[:, run_of_512(0)])
         nc.sync.dma_start(out=state[LAST][:, 3 * T // 4 : T], in_=rT[run_of_128(LAST), 3 * T // 4 : T])
         nc.sync.dma_start(out=weight_all[:, run_of_512(1)], in_=wgo[:, run_of_512(1)])

@@ -39,6 +39,7 @@ FIRST_PIECES = 2
 PIECES = [(b, h) for h in range(HALVES) for b in range(2)]
 PIECES = PIECES + [(b, h) for b in range(2, ROW_BLOCKS) for h in range(HALVES)]
 TURNED = [u for u in range(FIRST_PIECES, len(PIECES)) if PIECES[u][0] != NEXT_TO_LAST]
+STAGE = P - SCALE_ROWS
 FIRST_LATE = 3
 CAST_SPLIT = 320
 
@@ -53,10 +54,6 @@ def tile_list_rgg_L_kernel(
 
     def words_of(packed):
         return packed[0].rearrange("p n t -> p (n t)").bitcast(I32)
-
-    def load_scales(dest, scales):
-        for r in range(GROUP_ROWS):
-            nc.sync.dma_start(out=dest[r:P:QUADRANT, :], in_=scales[0, r:SCALE_ROWS:GROUP_ROWS, :].bitcast(I32))
 
     def run_of_128(i):
         return slice(i * P, (i + 1) * P)
@@ -76,8 +73,6 @@ def tile_list_rgg_L_kernel(
         dst_list = held.tile([P, J // LIST_ROWS], U16)
         tab_s = held.tile([P, T // PACK], I32, align_bytes=64)
         tab_w = held.tile([P, T], I32, align_bytes=64)
-        w_s = held.tile([P, 2, N // PACK], I32, align_bytes=64)
-        wa_s, wb_s = w_s[:, 0, :], w_s[:, 1, :]
         wa_w = held.tile([P, N], I32, align_bytes=64)
         wb_w = held.tile([P, N], I32, align_bytes=64)
         wc_raw = held.tile([P, PACK, N], F32, tag="wc_raw", align_bytes=64)
@@ -88,15 +83,19 @@ def tile_list_rgg_L_kernel(
         weight_col = held.tile([P, J // P], F32)
         identity = held.tile([P, P], F32)
         weight_all = held.tile([P, J], F32)
-        src_s = held.tile([P, J], U8, align_bytes=64)
-        dst_s = held.tile([P, J], U8, align_bytes=64)
+        picked_s = held.tile([P, 2 * J], U8, align_bytes=64)
+        staged = held.tile([P, 2 * (J + N) // PACK], I32, align_bytes=64)
+        planes = held.tile([P, 2 * (J + N) // PACK], I32, align_bytes=64)
+        src_s, dst_s = planes[:].bitcast(U8)[:, 0:J], planes[:].bitcast(U8)[:, J : 2 * J]
+        wa_at, wb_at = 2 * J // PACK, (2 * J + N) // PACK
+        wa_s, wb_s = planes[:, wa_at:wb_at], planes[:, wb_at : wb_at + N // PACK]
         state = [held.tile([P, T], F32, name="state%d" % b, tag="state%d" % b) for b in range(ROW_BLOCKS)]
         early = held.tile([P, KINDS, len(PIECES), HALF], F32)
         results = held.tile([P, len(PIECES), HALF], F32)
         placed = [held.tile([P, T], F32, name="placed%d" % i) for i in range(WINDOWS)]
 
-        nc.gpsimd.memset(tab_s[:], 0)
-        nc.gpsimd.memset(w_s[:], 0)
+        nc.gpsimd.memset(tab_s[0:STAGE, :], 0)
+        nc.vector.memset(planes[:], 0)
         make_identity(nc, identity[:])
         for window in placed:
             nc.gpsimd.memset(window[:], 0.0)
@@ -104,14 +103,14 @@ def tile_list_rgg_L_kernel(
         nc.scalar.activation(warm[:], placed[0][:, 0:1], SIGMOID)
 
         nc.sync.dma_start(src_list[:], offs)
+        nc.sync.dma_start(out=tab_s[STAGE:P, :], in_=tab_scales[0].bitcast(I32))
         nc.sync.dma_start(dst_list[:], offs2)
-        load_scales(tab_s, tab_scales)
         nc.sync.dma_start(out=tab_w[:], in_=words_of(tab_words))
+        nc.sync.dma_start(out=wc_raw[:], in_=wc.rearrange("(p i) n -> p i n", i=PACK))
+        nc.sync.dma_start(out=staged[STAGE:P, wa_at:wb_at], in_=wa_scales[0].bitcast(I32))
+        nc.sync.dma_start(out=staged[STAGE:P, wb_at : wb_at + N // PACK], in_=wb_scales[0].bitcast(I32))
         nc.sync.dma_start(out=wa_w[:], in_=words_of(wa_words))
         nc.sync.dma_start(out=wb_w[:], in_=words_of(wb_words))
-        load_scales(wa_s, wa_scales)
-        nc.sync.dma_start(out=wc_raw[:], in_=wc.rearrange("(p i) n -> p i n", i=PACK))
-        load_scales(wb_s, wb_scales)
         nc.sync.dma_start(out=state[0][:], in_=rT[run_of_128(0), :])
         nc.sync.dma_start(out=weight_rows[:], in_=wgo[0 : P * P // J, :].rearrange("r (c j) -> (r c) j", j=P))
         nc.sync.dma_start(out=state[1][:], in_=rT[run_of_128(1), :])
@@ -129,8 +128,17 @@ def tile_list_rgg_L_kernel(
             wc_bf[:, CAST_SPLIT:N, :], wc_raw[:, :, CAST_SPLIT:N].rearrange("p i n -> p n i"), 1.0, 0.0, MULT, ADD
         )
 
-        nc.vector.tensor_copy(src_s[:], tab_s[:].bitcast(U8).indirect(src_list[:]))
-        nc.vector.tensor_copy(dst_s[:], tab_s[:].bitcast(U8).indirect(dst_list[:]))
+        nc.vector.tensor_copy(picked_s[:, 0:J], tab_s[:].bitcast(U8).indirect(src_list[:]))
+        nc.vector.tensor_copy(picked_s[:, J : 2 * J], tab_s[:].bitcast(U8).indirect(dst_list[:]))
+        for i in range(2):
+            words = slice(i * J // PACK, (i + 1) * J // PACK)
+            nc.vector.tensor_copy(staged[:, words], picked_s[:].bitcast(I32)[:, words])
+        for q in range(P // QUADRANT):
+            first = STAGE + q * GROUP_ROWS
+            nc.scalar.dma_start(
+                out=planes[q * QUADRANT : q * QUADRANT + GROUP_ROWS, :],
+                in_=staged[first : first + GROUP_ROWS, :],
+            )
 
         def gather_words(entries, h, tag):
             words = held.tile([P, HALF], U32, align_bytes=64, name=tag, tag=tag)

@@ -40,8 +40,16 @@ PIECES = [(b, h) for h in range(HALVES) for b in range(2)]
 PIECES = PIECES + [(b, h) for b in range(2, ROW_BLOCKS) for h in range(HALVES)]
 TURNED = [u for u in range(FIRST_PIECES, len(PIECES)) if PIECES[u][0] != NEXT_TO_LAST]
 STAGE = P - SCALE_ROWS
+PICKED_AT = 8192
+STATE1_AT = 64
+WINDOW_AT = STATE1_AT + 4 * T
+STATE2_AT = WINDOW_AT + 4 * T
+ROWS_AT = STATE2_AT + 4 * T
+STAGED_AT = ROWS_AT - 64
+STATE3_AT = ROWS_AT + 4 * P
+RAW_AT = STATE3_AT + 4 * 3 * J
+WEIGHT_AT = RAW_AT + 4 * J
 FIRST_LATE = 3
-CAST_SPLIT = 320
 
 KINDS = 3
 GATE, MESSAGE, GATED = range(KINDS)
@@ -68,6 +76,7 @@ def tile_list_rgg_L_kernel(
         held = ctx.enter_context(tc.tile_pool(name="held", bufs=1))
         ring = ctx.enter_context(tc.tile_pool(name="ring", bufs=RING))
         psum = ctx.enter_context(tc.psum_pool(name="psum", bufs=1))
+        shared = ctx.enter_context(tc.tile_pool(name="shared", bufs=1))
 
         src_list = held.tile([P, J // LIST_ROWS], U16)
         dst_list = held.tile([P, J // LIST_ROWS], U16)
@@ -75,30 +84,28 @@ def tile_list_rgg_L_kernel(
         tab_w = held.tile([P, T], I32, align_bytes=64)
         wa_w = held.tile([P, N], I32, align_bytes=64)
         wb_w = held.tile([P, N], I32, align_bytes=64)
-        wc_raw = held.tile([P, PACK, N], F32, tag="wc_raw", align_bytes=64)
+        wc_raw = shared.tile([P, PACK, N], F32, offset=RAW_AT, align_bytes=64)
         wc_bf = held.tile([P, N, PACK], BF16, align_bytes=64, tag="wc_bf")
         wc_w = held.tile([P, N], U32, align_bytes=64)
         wc_s = held.tile([P, N], U8, align_bytes=64)
-        weight_rows = held.tile([P, P], F32)
         weight_col = held.tile([P, J // P], F32)
         identity = held.tile([P, P], F32)
-        weight_all = held.tile([P, J], F32)
-        picked_s = held.tile([P, 2 * J], U8, align_bytes=64)
-        staged = held.tile([P, 2 * (J + N) // PACK], I32, align_bytes=64)
+        picked_s = shared.tile([P, 2 * J], U8, offset=PICKED_AT, align_bytes=64)
+        staged = shared.tile([P, 2 * (J + N) // PACK], I32, offset=STAGED_AT, align_bytes=64)
         planes = held.tile([P, 2 * (J + N) // PACK], I32, align_bytes=64)
         src_s, dst_s = planes[:].bitcast(U8)[:, 0:J], planes[:].bitcast(U8)[:, J : 2 * J]
         wa_at, wb_at = 2 * J // PACK, (2 * J + N) // PACK
         wa_s, wb_s = planes[:, wa_at:wb_at], planes[:, wb_at : wb_at + N // PACK]
-        state = [held.tile([P, T], F32, name="state%d" % b, tag="state%d" % b) for b in range(ROW_BLOCKS)]
+        state = [held.tile([P, T], F32, name="state0")]
         early = held.tile([P, KINDS, len(PIECES), HALF], F32)
         results = held.tile([P, len(PIECES), HALF], F32)
-        placed = [held.tile([P, T], F32, name="placed%d" % i) for i in range(WINDOWS)]
+        placed = [held.tile([P, T], F32, name="placed%d" % i) for i in range(WINDOWS - 1)]
 
         nc.gpsimd.memset(tab_s[0:STAGE, :], 0)
-        nc.vector.memset(planes[:], 0)
-        make_identity(nc, identity[:])
+        nc.gpsimd.memset(planes[:], 0)
         for window in placed:
             nc.gpsimd.memset(window[:], 0.0)
+        make_identity(nc, identity[:])
         warm = held.tile([P, 1], F32)
         nc.scalar.activation(warm[:], placed[0][:, 0:1], SIGMOID)
 
@@ -106,56 +113,60 @@ def tile_list_rgg_L_kernel(
         nc.sync.dma_start(out=tab_s[STAGE:P, :], in_=tab_scales[0].bitcast(I32))
         nc.sync.dma_start(dst_list[:], offs2)
         nc.sync.dma_start(out=tab_w[:], in_=words_of(tab_words))
-        nc.sync.dma_start(out=wc_raw[:], in_=wc.rearrange("(p i) n -> p i n", i=PACK))
         nc.sync.dma_start(out=staged[STAGE:P, wa_at:wb_at], in_=wa_scales[0].bitcast(I32))
         nc.sync.dma_start(out=staged[STAGE:P, wb_at : wb_at + N // PACK], in_=wb_scales[0].bitcast(I32))
+        nc.sync.dma_start(out=wc_raw[:], in_=wc.rearrange("(p i) n -> p i n", i=PACK))
         nc.sync.dma_start(out=wa_w[:], in_=words_of(wa_words))
         nc.sync.dma_start(out=wb_w[:], in_=words_of(wb_words))
         nc.sync.dma_start(out=state[0][:], in_=rT[run_of_128(0), :])
-        nc.sync.dma_start(out=weight_rows[:], in_=wgo[0 : P * P // J, :].rearrange("r (c j) -> (r c) j", j=P))
-        nc.sync.dma_start(out=state[1][:], in_=rT[run_of_128(1), :])
-        nc.sync.dma_start(out=state[NEXT_TO_LAST][:], in_=rT[run_of_128(NEXT_TO_LAST), :])
-        nc.sync.dma_start(out=state[LAST][:, 0 : 3 * T // 4], in_=rT[run_of_128(LAST), 0 : 3 * T // 4])
-        nc.sync.dma_start(out=weight_all[:, run_of_512(0)], in_=wgo[:, run_of_512(0)])
-        nc.sync.dma_start(out=state[LAST][:, 3 * T // 4 : T], in_=rT[run_of_128(LAST), 3 * T // 4 : T])
-        nc.sync.dma_start(out=weight_all[:, run_of_512(1)], in_=wgo[:, run_of_512(1)])
 
         nc.scalar.copy(
-            wc_bf[:, 0:CAST_SPLIT, :].rearrange("p (c m) i -> p c i m", m=COLUMN_RUN),
-            wc_raw[:, :, 0:CAST_SPLIT].rearrange("p i (c m) -> p c i m", m=COLUMN_RUN),
-        )
-        nc.gpsimd.tensor_scalar(
-            wc_bf[:, CAST_SPLIT:N, :], wc_raw[:, :, CAST_SPLIT:N].rearrange("p i n -> p n i"), 1.0, 0.0, MULT, ADD
+            wc_bf[:].rearrange("p (c m) i -> p c i m", m=COLUMN_RUN),
+            wc_raw[:].rearrange("p i (c m) -> p c i m", m=COLUMN_RUN),
         )
 
         nc.vector.tensor_copy(picked_s[:, 0:J], tab_s[:].bitcast(U8).indirect(src_list[:]))
         nc.vector.tensor_copy(picked_s[:, J : 2 * J], tab_s[:].bitcast(U8).indirect(dst_list[:]))
-        for i in range(2):
-            words = slice(i * J // PACK, (i + 1) * J // PACK)
-            nc.vector.tensor_copy(staged[:, words], picked_s[:].bitcast(I32)[:, words])
-        for q in range(P // QUADRANT):
-            first = STAGE + q * GROUP_ROWS
-            nc.scalar.dma_start(
-                out=planes[q * QUADRANT : q * QUADRANT + GROUP_ROWS, :],
-                in_=staged[first : first + GROUP_ROWS, :],
-            )
 
         def gather_words(entries, h, tag):
-            words = held.tile([P, HALF], U32, align_bytes=64, name=tag, tag=tag)
+            if tag == "wc_raw":
+                words = shared.tile([P, HALF], U32, align_bytes=64, name="src1", offset=RAW_AT)
+            else:
+                words = held.tile([P, HALF], U32, align_bytes=64, name=tag, tag=tag)
             nc.vector.tensor_copy(words[:], tab_w[:].bitcast(U32).indirect(entries[:, list_columns(h)]))
             return words[:].bitcast(FP8X4)
 
+        nc.vector.tensor_copy(staged[:, 0:wa_at], picked_s[:].bitcast(I32))
+        placed.append(shared.tile([P, T], F32, name="placed2", offset=WINDOW_AT))
+        nc.gpsimd.memset(placed[2][:], 0.0)
+        for q in range(P // QUADRANT):
+            first = STAGE + q * GROUP_ROWS
+            nc.sync.dma_start(
+                out=planes[q * QUADRANT : q * QUADRANT + GROUP_ROWS, :],
+                in_=staged[first : first + GROUP_ROWS, :],
+            )
+        state.append(shared.tile([P, T], F32, name="state1", offset=STATE1_AT))
+        state.append(shared.tile([P, T], F32, name="state2", offset=STATE2_AT))
+        state.append(shared.tile([P, T], F32, name="state3", offset=STATE3_AT))
+        weight_rows = shared.tile([P, P], F32, offset=ROWS_AT)
+        weight_all = shared.tile([P, J], F32, offset=WEIGHT_AT)
+        nc.sync.dma_start(out=state[1][:], in_=rT[run_of_128(1), :])
+        nc.sync.dma_start(out=state[NEXT_TO_LAST][:], in_=rT[run_of_128(NEXT_TO_LAST), :])
+        nc.sync.dma_start(out=weight_rows[:], in_=wgo[0 : P * P // J, :].rearrange("r (c j) -> (r c) j", j=P))
+        nc.sync.dma_start(out=state[LAST][:], in_=rT[run_of_128(LAST), :])
         dst_words = [gather_words(dst_list, 0, "dst0")]
         src_words = [gather_words(src_list, 0, "src0")]
         dst_words.append(gather_words(dst_list, 1, "dst1"))
         nc.vector.quantize_mx(out=wc_w[:].bitcast(FP8X4), scales=wc_s[:], in_=wc_bf[:].rearrange("p n i -> p (n i)"))
         src_words.append(gather_words(src_list, 1, "wc_raw"))
+        nc.sync.dma_start(out=weight_all[:, run_of_512(0)], in_=wgo[:, run_of_512(0)])
+        nc.sync.dma_start(out=weight_all[:, run_of_512(1)], in_=wgo[:, run_of_512(1)])
 
         picked = []
         for b in range(ROW_BLOCKS):
             picked.append(held.tile([P, J], F32, name="picked%d" % b)[:])
             nc.vector.tensor_copy(picked[b], state[b][:].indirect(dst_list[:]))
-        late = held.tile([P, 3, J], F32, tag="state%d" % LAST)
+        late = shared.tile([P, 3, J], F32, offset=STATE3_AT)
         late_gated = late[:].rearrange("p r j -> p (r j)")
         result = [results[:, u, :] for u in range(len(PIECES))]
         summed = [result[FIRST_PIECES + 1 - u] for u in range(FIRST_PIECES)]

@@ -38,18 +38,17 @@ FIRST_PIECES = 2
 
 PIECES = [(b, h) for h in range(HALVES) for b in range(2)]
 PIECES = PIECES + [(b, h) for b in range(2, ROW_BLOCKS) for h in range(HALVES)]
-TURNED = [u for u in range(FIRST_PIECES, len(PIECES)) if PIECES[u][0] != NEXT_TO_LAST]
+TURNED = [u for u in range(FIRST_PIECES, len(PIECES)) if PIECES[u][0] != LAST]
 STAGE = P - SCALE_ROWS
-PICKED_AT = 8192
-STATE1_AT = 64
-WINDOW_AT = STATE1_AT + 4 * T
-STATE2_AT = WINDOW_AT + 4 * T
+STATE1_AT = 0
+STATE2_AT = STATE1_AT + 4 * T
+TABLE_AT = STATE2_AT - T // 2
 ROWS_AT = STATE2_AT + 4 * T
-STAGED_AT = ROWS_AT - 64
+PICKED_AT = ROWS_AT
 STATE3_AT = ROWS_AT + 4 * P
 RAW_AT = STATE3_AT + 4 * 3 * J
 WEIGHT_AT = RAW_AT + 4 * J
-FIRST_LATE = 3
+FIRST_LATE = 2
 
 KINDS = 3
 GATE, MESSAGE, GATED = range(KINDS)
@@ -62,6 +61,13 @@ def tile_list_rgg_L_kernel(
 
     def words_of(packed):
         return packed[0].rearrange("p n t -> p (n t)").bitcast(I32)
+
+    def move_scales(dest, rows):
+        for q in range(P // QUADRANT):
+            first = STAGE + q * GROUP_ROWS
+            nc.sync.dma_start(
+                out=dest[q * QUADRANT : q * QUADRANT + GROUP_ROWS, :], in_=rows[first : first + GROUP_ROWS, :]
+            )
 
     def run_of_128(i):
         return slice(i * P, (i + 1) * P)
@@ -80,7 +86,7 @@ def tile_list_rgg_L_kernel(
 
         src_list = held.tile([P, J // LIST_ROWS], U16)
         dst_list = held.tile([P, J // LIST_ROWS], U16)
-        tab_s = held.tile([P, T // PACK], I32, align_bytes=64)
+        tab_s = shared.tile([P, T // PACK], I32, offset=TABLE_AT, align_bytes=64)
         tab_w = held.tile([P, T], I32, align_bytes=64)
         wa_w = held.tile([P, N], I32, align_bytes=64)
         wb_w = held.tile([P, N], I32, align_bytes=64)
@@ -91,17 +97,19 @@ def tile_list_rgg_L_kernel(
         weight_col = held.tile([P, J // P], F32)
         identity = held.tile([P, P], F32)
         picked_s = shared.tile([P, 2 * J], U8, offset=PICKED_AT, align_bytes=64)
-        staged = shared.tile([P, 2 * (J + N) // PACK], I32, offset=STAGED_AT, align_bytes=64)
-        planes = held.tile([P, 2 * (J + N) // PACK], I32, align_bytes=64)
+        staged = held.tile([P, 2 * N // PACK], I32, align_bytes=64)
+        planes = held.tile([P, 2 * J // PACK], I32, align_bytes=64)
+        w_s = held.tile([P, 2 * N // PACK], I32, align_bytes=64)
         src_s, dst_s = planes[:].bitcast(U8)[:, 0:J], planes[:].bitcast(U8)[:, J : 2 * J]
-        wa_at, wb_at = 2 * J // PACK, (2 * J + N) // PACK
-        wa_s, wb_s = planes[:, wa_at:wb_at], planes[:, wb_at : wb_at + N // PACK]
+        wa_at, wb_at = 0, N // PACK
+        wa_s, wb_s = w_s[:, wa_at:wb_at], w_s[:, wb_at : wb_at + N // PACK]
         state = [held.tile([P, T], F32, name="state0")]
         early = held.tile([P, KINDS, len(PIECES), HALF], F32)
         results = held.tile([P, len(PIECES), HALF], F32)
-        placed = [held.tile([P, T], F32, name="placed%d" % i) for i in range(WINDOWS - 1)]
+        placed = [held.tile([P, T], F32, name="placed%d" % i) for i in range(WINDOWS)]
 
         nc.gpsimd.memset(tab_s[0:STAGE, :], 0)
+        nc.gpsimd.memset(w_s[:], 0)
         nc.gpsimd.memset(planes[:], 0)
         for window in placed:
             nc.gpsimd.memset(window[:], 0.0)
@@ -118,6 +126,7 @@ def tile_list_rgg_L_kernel(
         nc.sync.dma_start(out=wc_raw[:], in_=wc.rearrange("(p i) n -> p i n", i=PACK))
         nc.sync.dma_start(out=wa_w[:], in_=words_of(wa_words))
         nc.sync.dma_start(out=wb_w[:], in_=words_of(wb_words))
+        move_scales(w_s, staged[:])
         nc.sync.dma_start(out=state[0][:], in_=rT[run_of_128(0), :])
 
         nc.scalar.copy(
@@ -136,15 +145,7 @@ def tile_list_rgg_L_kernel(
             nc.vector.tensor_copy(words[:], tab_w[:].bitcast(U32).indirect(entries[:, list_columns(h)]))
             return words[:].bitcast(FP8X4)
 
-        nc.vector.tensor_copy(staged[:, 0:wa_at], picked_s[:].bitcast(I32))
-        placed.append(shared.tile([P, T], F32, name="placed2", offset=WINDOW_AT))
-        nc.gpsimd.memset(placed[2][:], 0.0)
-        for q in range(P // QUADRANT):
-            first = STAGE + q * GROUP_ROWS
-            nc.sync.dma_start(
-                out=planes[q * QUADRANT : q * QUADRANT + GROUP_ROWS, :],
-                in_=staged[first : first + GROUP_ROWS, :],
-            )
+        move_scales(planes, picked_s[:].bitcast(I32))
         state.append(shared.tile([P, T], F32, name="state1", offset=STATE1_AT))
         state.append(shared.tile([P, T], F32, name="state2", offset=STATE2_AT))
         state.append(shared.tile([P, T], F32, name="state3", offset=STATE3_AT))
@@ -241,10 +242,10 @@ def tile_list_rgg_L_kernel(
             if h == HALVES - 1:
                 nc.sync.dma_start(out=out[run_of_128(b), :], in_=window[:])
         for b in range(2, ROW_BLOCKS):
-            window = placed[b % WINDOWS]
+            window = placed[2 if b == NEXT_TO_LAST else 1]
             first = b * HALVES
             both = results[:, first : first + HALVES, :].rearrange("p h j -> p (h j)")
-            if b == NEXT_TO_LAST:
+            if b == LAST:
                 nc.vector.tensor_tensor(window[:].indirect(dst_list[:]), both, weight_all[:], MULT)
             else:
                 nc.vector.tensor_copy(window[:].indirect(dst_list[:]), both)

@@ -49,6 +49,7 @@ STATE3_AT = ROWS_AT + 4 * P
 RAW_AT = STATE3_AT + 4 * 3 * J
 WEIGHT_AT = RAW_AT + 4 * J
 FIRST_LATE = 2
+WEIGHT_ROW = P - J // P
 
 KINDS = 3
 GATE, MESSAGE, GATED = range(KINDS)
@@ -63,11 +64,8 @@ def tile_list_rgg_L_kernel(
         return packed[0].rearrange("p n t -> p (n t)").bitcast(I32)
 
     def move_scales(dest, rows):
-        for q in range(P // QUADRANT):
-            first = STAGE + q * GROUP_ROWS
-            nc.sync.dma_start(
-                out=dest[q * QUADRANT : q * QUADRANT + GROUP_ROWS, :], in_=rows[first : first + GROUP_ROWS, :]
-            )
+        for r in range(GROUP_ROWS):
+            nc.sync.dma_start(out=dest[r:P:QUADRANT, :], in_=rows[STAGE + r : P : GROUP_ROWS, :])
 
     def run_of_128(i):
         return slice(i * P, (i + 1) * P)
@@ -95,6 +93,7 @@ def tile_list_rgg_L_kernel(
         wc_w = held.tile([P, N], U32, align_bytes=64)
         wc_s = held.tile([P, N], U8, align_bytes=64)
         weight_col = held.tile([P, J // P], F32)
+        weight_rows = held.tile([P, P], F32)
         identity = held.tile([P, P], F32)
         picked_s = shared.tile([P, 2 * J], U8, offset=PICKED_AT, align_bytes=64)
         staged = held.tile([P, 2 * N // PACK], I32, align_bytes=64)
@@ -113,6 +112,7 @@ def tile_list_rgg_L_kernel(
         nc.gpsimd.memset(planes[:], 0)
         for window in placed:
             nc.gpsimd.memset(window[:], 0.0)
+        nc.gpsimd.memset(weight_rows[0:WEIGHT_ROW, :], 0.0)
         make_identity(nc, identity[:])
         warm = held.tile([P, 1], F32)
         nc.scalar.activation(warm[:], placed[0][:, 0:1], SIGMOID)
@@ -120,14 +120,15 @@ def tile_list_rgg_L_kernel(
         nc.sync.dma_start(src_list[:], offs)
         nc.sync.dma_start(out=tab_s[STAGE:P, :], in_=tab_scales[0].bitcast(I32))
         nc.sync.dma_start(dst_list[:], offs2)
-        nc.sync.dma_start(out=tab_w[:], in_=words_of(tab_words))
         nc.sync.dma_start(out=staged[STAGE:P, wa_at:wb_at], in_=wa_scales[0].bitcast(I32))
         nc.sync.dma_start(out=staged[STAGE:P, wb_at : wb_at + N // PACK], in_=wb_scales[0].bitcast(I32))
+        nc.sync.dma_start(out=tab_w[:], in_=words_of(tab_words))
         nc.sync.dma_start(out=wc_raw[:], in_=wc.rearrange("(p i) n -> p i n", i=PACK))
+        move_scales(w_s, staged[:])
         nc.sync.dma_start(out=wa_w[:], in_=words_of(wa_words))
         nc.sync.dma_start(out=wb_w[:], in_=words_of(wb_words))
-        move_scales(w_s, staged[:])
         nc.sync.dma_start(out=state[0][:], in_=rT[run_of_128(0), :])
+        nc.sync.dma_start(out=weight_rows[WEIGHT_ROW:P, :], in_=wgo[0].rearrange("(c j) -> c j", j=P))
 
         nc.scalar.copy(
             wc_bf[:].rearrange("p (c m) i -> p c i m", m=COLUMN_RUN),
@@ -149,11 +150,9 @@ def tile_list_rgg_L_kernel(
         state.append(shared.tile([P, T], F32, name="state1", offset=STATE1_AT))
         state.append(shared.tile([P, T], F32, name="state2", offset=STATE2_AT))
         state.append(shared.tile([P, T], F32, name="state3", offset=STATE3_AT))
-        weight_rows = shared.tile([P, P], F32, offset=ROWS_AT)
         weight_all = shared.tile([P, J], F32, offset=WEIGHT_AT)
         nc.sync.dma_start(out=state[1][:], in_=rT[run_of_128(1), :])
         nc.sync.dma_start(out=state[NEXT_TO_LAST][:], in_=rT[run_of_128(NEXT_TO_LAST), :])
-        nc.sync.dma_start(out=weight_rows[:], in_=wgo[0 : P * P // J, :].rearrange("r (c j) -> (r c) j", j=P))
         nc.sync.dma_start(out=state[LAST][:], in_=rT[run_of_128(LAST), :])
         dst_words = [gather_words(dst_list, 0, "dst0")]
         src_words = [gather_words(src_list, 0, "src0")]
@@ -183,7 +182,7 @@ def tile_list_rgg_L_kernel(
         back_banks = [psum.tile([P, HALF], F32, name="back%d" % i) for i in range(TURN_BANKS)]
 
         nc.tensor.transpose(back_banks[0][:, 0:P], weight_rows[:], identity[:])
-        nc.scalar.copy(weight_col[:], back_banks[0][:, 0 : J // P])
+        nc.scalar.copy(weight_col[:], back_banks[0][:, WEIGHT_ROW:P])
 
         def products(u):
             b, h = PIECES[u]

@@ -117,8 +117,8 @@ def tile_list_rgg_L_kernel(
         warm = held.tile([P, 1], F32)
         nc.scalar.activation(warm[:], placed[0][:, 0:1], SIGMOID)
 
-        nc.sync.dma_start(src_list[:], offs)
         nc.sync.dma_start(out=tab_s[STAGE:P, :], in_=tab_scales[0].bitcast(I32))
+        nc.sync.dma_start(src_list[:], offs)
         nc.sync.dma_start(dst_list[:], offs2)
         nc.sync.dma_start(out=staged[STAGE:P, wa_at:wb_at], in_=wa_scales[0].bitcast(I32))
         nc.sync.dma_start(out=staged[STAGE:P, wb_at : wb_at + N // PACK], in_=wb_scales[0].bitcast(I32))
@@ -139,10 +139,7 @@ def tile_list_rgg_L_kernel(
         nc.vector.tensor_copy(picked_s[:, J : 2 * J], tab_s[:].bitcast(U8).indirect(dst_list[:]))
 
         def gather_words(entries, h, tag):
-            if tag == "wc_raw":
-                words = shared.tile([P, HALF], U32, align_bytes=64, name="src1", offset=RAW_AT)
-            else:
-                words = held.tile([P, HALF], U32, align_bytes=64, name=tag, tag=tag)
+            words = held.tile([P, HALF], U32, align_bytes=64, name=tag)
             nc.vector.tensor_copy(words[:], tab_w[:].bitcast(U32).indirect(entries[:, list_columns(h)]))
             return words[:].bitcast(FP8X4)
 
@@ -154,11 +151,11 @@ def tile_list_rgg_L_kernel(
         nc.sync.dma_start(out=state[1][:], in_=rT[run_of_128(1), :])
         nc.sync.dma_start(out=state[NEXT_TO_LAST][:], in_=rT[run_of_128(NEXT_TO_LAST), :])
         nc.sync.dma_start(out=state[LAST][:], in_=rT[run_of_128(LAST), :])
-        dst_words = [gather_words(dst_list, 0, "dst0")]
-        src_words = [gather_words(src_list, 0, "src0")]
-        dst_words.append(gather_words(dst_list, 1, "dst1"))
+        src_all = held.tile([P, J], U32, align_bytes=64)
+        nc.vector.tensor_copy(src_all[:], tab_w[:].bitcast(U32).indirect(src_list[:]))
+        src_words = [src_all[:, run_of_512(h)].bitcast(FP8X4) for h in range(HALVES)]
+        dst_words = [gather_words(dst_list, h, "dst%d" % h) for h in range(HALVES)]
         nc.vector.quantize_mx(out=wc_w[:].bitcast(FP8X4), scales=wc_s[:], in_=wc_bf[:].rearrange("p n i -> p (n i)"))
-        src_words.append(gather_words(src_list, 1, "wc_raw"))
         nc.sync.dma_start(out=weight_all[:, run_of_512(0)], in_=wgo[:, run_of_512(0)])
         nc.sync.dma_start(out=weight_all[:, run_of_512(1)], in_=wgo[:, run_of_512(1)])
 

@@ -114,8 +114,6 @@ def tile_list_rgg_L_kernel(
             nc.gpsimd.memset(window[:], 0.0)
         nc.gpsimd.memset(weight_rows[0:WEIGHT_ROW, :], 0.0)
         make_identity(nc, identity[:])
-        warm = held.tile([P, 1], F32)
-        nc.scalar.activation(warm[:], placed[0][:, 0:1], SIGMOID)
 
         nc.sync.dma_start(out=tab_s[STAGE:P, :], in_=tab_scales[0].bitcast(I32))
         nc.sync.dma_start(src_list[:], offs)

@@ -29,30 +29,18 @@ LIST_ROWS = 16
 ROW_BLOCKS = N // P
 HALF = 512
 HALVES = J // HALF
+WINDOWS = 2
+BANKS = 3
 SQUARES = HALF // P
-RING = 2
-TURN_BANKS = 3
-WINDOWS = 3
-LAST, NEXT_TO_LAST = ROW_BLOCKS - 1, ROW_BLOCKS - 2
-FIRST_PIECES = 2
-
-PIECES = [(b, h) for h in range(HALVES) for b in range(2)]
-PIECES = PIECES + [(b, h) for b in range(2, ROW_BLOCKS) for h in range(HALVES)]
-TURNED = [u for u in range(FIRST_PIECES, len(PIECES)) if PIECES[u][0] != LAST]
+WEIGHT_ROW = P - SQUARES
+LAST = ROW_BLOCKS - 1
 STAGE = P - SCALE_ROWS
-STATE1_AT = 0
-STATE2_AT = STATE1_AT + 4 * T
-TABLE_AT = STATE2_AT - T // 2
-ROWS_AT = STATE2_AT + 4 * T
-PICKED_AT = ROWS_AT
-STATE3_AT = ROWS_AT + 4 * P
-RAW_AT = STATE3_AT + 4 * 3 * J
-WEIGHT_AT = RAW_AT + 4 * J
-FIRST_LATE = 2
-WEIGHT_ROW = P - J // P
-
-KINDS = 3
-GATE, MESSAGE, GATED = range(KINDS)
+WC_HALF = N // 2
+STATE_BYTES = 4 * T
+TABLE_AT = STATE_BYTES - T // 2
+PICKED_AT = 3 * STATE_BYTES - J
+RAW_AT = ROW_BLOCKS * STATE_BYTES
+RAW_BYTES = 4 * PACK * WC_HALF
 
 
 def tile_list_rgg_L_kernel(
@@ -78,7 +66,6 @@ def tile_list_rgg_L_kernel(
 
     with ExitStack() as ctx:
         held = ctx.enter_context(tc.tile_pool(name="held", bufs=1))
-        ring = ctx.enter_context(tc.tile_pool(name="ring", bufs=RING))
         psum = ctx.enter_context(tc.psum_pool(name="psum", bufs=1))
         shared = ctx.enter_context(tc.tile_pool(name="shared", bufs=1))
 
@@ -88,13 +75,13 @@ def tile_list_rgg_L_kernel(
         tab_w = held.tile([P, T], I32, align_bytes=64)
         wa_w = held.tile([P, N], I32, align_bytes=64)
         wb_w = held.tile([P, N], I32, align_bytes=64)
-        wc_raw = shared.tile([P, PACK, N], F32, offset=RAW_AT, align_bytes=64)
-        wc_bf = held.tile([P, N, PACK], BF16, align_bytes=64, tag="wc_bf")
+        wc_raw = [
+            shared.tile([P, PACK, WC_HALF], F32, offset=RAW_AT + i * RAW_BYTES, align_bytes=64, name="wc_raw%d" % i)
+            for i in range(2)
+        ]
+        wc_bf = held.tile([P, N, PACK], BF16, align_bytes=64)
         wc_w = held.tile([P, N], U32, align_bytes=64)
         wc_s = held.tile([P, N], U8, align_bytes=64)
-        weight_col = held.tile([P, J // P], F32)
-        weight_rows = held.tile([P, P], F32)
-        identity = held.tile([P, P], F32)
         picked_s = shared.tile([P, 2 * J], U8, offset=PICKED_AT, align_bytes=64)
         staged = held.tile([P, 2 * N // PACK], I32, align_bytes=64)
         planes = held.tile([P, 2 * J // PACK], I32, align_bytes=64)
@@ -102,10 +89,17 @@ def tile_list_rgg_L_kernel(
         src_s, dst_s = planes[:].bitcast(U8)[:, 0:J], planes[:].bitcast(U8)[:, J : 2 * J]
         wa_at, wb_at = 0, N // PACK
         wa_s, wb_s = w_s[:, wa_at:wb_at], w_s[:, wb_at : wb_at + N // PACK]
-        state = [held.tile([P, T], F32, name="state0")]
-        early = held.tile([P, KINDS, len(PIECES), HALF], F32)
-        results = held.tile([P, len(PIECES), HALF], F32)
+        gates = held.tile([P, ROW_BLOCKS, J], F32)
+        messages = held.tile([P, ROW_BLOCKS, J], F32)
+        results = held.tile([P, ROW_BLOCKS, J], F32)
+        work = [held.tile([P, J], F32, name="work%d" % i) for i in range(3)]
         placed = [held.tile([P, T], F32, name="placed%d" % i) for i in range(WINDOWS)]
+
+        weight_col = held.tile([P, SQUARES], F32)
+        weight_rows = held.tile([P, P], F32)
+        identity = held.tile([P, P], F32)
+        weighted = held.tile([P, HALF], F32)
+        weight_all = held.tile([P, J], F32)
 
         nc.gpsimd.memset(tab_s[0:STAGE, :], 0)
         nc.gpsimd.memset(w_s[:], 0)
@@ -121,126 +115,127 @@ def tile_list_rgg_L_kernel(
         nc.sync.dma_start(out=staged[STAGE:P, wa_at:wb_at], in_=wa_scales[0].bitcast(I32))
         nc.sync.dma_start(out=staged[STAGE:P, wb_at : wb_at + N // PACK], in_=wb_scales[0].bitcast(I32))
         nc.sync.dma_start(out=tab_w[:], in_=words_of(tab_words))
-        nc.sync.dma_start(out=wc_raw[:], in_=wc.rearrange("(p i) n -> p i n", i=PACK))
+        wc_rows = wc.rearrange("(p i) n -> p i n", i=PACK)
+        for i in range(2):
+            nc.sync.dma_start(out=wc_raw[i][:], in_=wc_rows[:, :, i * WC_HALF : (i + 1) * WC_HALF])
         move_scales(w_s, staged[:])
         nc.sync.dma_start(out=wa_w[:], in_=words_of(wa_words))
         nc.sync.dma_start(out=wb_w[:], in_=words_of(wb_words))
-        nc.sync.dma_start(out=state[0][:], in_=rT[run_of_128(0), :])
-        nc.sync.dma_start(out=weight_rows[WEIGHT_ROW:P, :], in_=wgo[0].rearrange("(c j) -> c j", j=P))
+        nc.sync.dma_start(out=weight_rows[WEIGHT_ROW:P, :], in_=wgo[0, 0:HALF].rearrange("(c j) -> c j", j=P))
+        nc.sync.dma_start(out=weight_all[:, run_of_512(0)], in_=wgo[:, run_of_512(0)])
 
-        nc.scalar.copy(
-            wc_bf[:].rearrange("p (c m) i -> p c i m", m=COLUMN_RUN),
-            wc_raw[:].rearrange("p i (c m) -> p c i m", m=COLUMN_RUN),
-        )
+        for i in range(2):
+            nc.scalar.copy(
+                wc_bf[:, i * WC_HALF : (i + 1) * WC_HALF, :].rearrange("p (c m) i -> p c i m", m=COLUMN_RUN),
+                wc_raw[i][:].rearrange("p i (c m) -> p c i m", m=COLUMN_RUN),
+            )
 
         nc.vector.tensor_copy(picked_s[:, 0:J], tab_s[:].bitcast(U8).indirect(src_list[:]))
         nc.vector.tensor_copy(picked_s[:, J : 2 * J], tab_s[:].bitcast(U8).indirect(dst_list[:]))
 
-        def gather_words(entries, h, tag):
-            words = held.tile([P, HALF], U32, align_bytes=64, name=tag)
-            nc.vector.tensor_copy(words[:], tab_w[:].bitcast(U32).indirect(entries[:, list_columns(h)]))
-            return words[:].bitcast(FP8X4)
-
         move_scales(planes, picked_s[:].bitcast(I32))
-        state.append(shared.tile([P, T], F32, name="state1", offset=STATE1_AT))
-        state.append(shared.tile([P, T], F32, name="state2", offset=STATE2_AT))
-        state.append(shared.tile([P, T], F32, name="state3", offset=STATE3_AT))
-        weight_all = shared.tile([P, J], F32, offset=WEIGHT_AT)
-        nc.sync.dma_start(out=state[1][:], in_=rT[run_of_128(1), :])
-        nc.sync.dma_start(out=state[NEXT_TO_LAST][:], in_=rT[run_of_128(NEXT_TO_LAST), :])
-        nc.sync.dma_start(out=state[LAST][:], in_=rT[run_of_128(LAST), :])
-        src_all = held.tile([P, J], U32, align_bytes=64)
-        nc.vector.tensor_copy(src_all[:], tab_w[:].bitcast(U32).indirect(src_list[:]))
-        src_words = [src_all[:, run_of_512(h)].bitcast(FP8X4) for h in range(HALVES)]
-        dst_words = [gather_words(dst_list, h, "dst%d" % h) for h in range(HALVES)]
-        nc.vector.quantize_mx(out=wc_w[:].bitcast(FP8X4), scales=wc_s[:], in_=wc_bf[:].rearrange("p n i -> p (n i)"))
-        nc.sync.dma_start(out=weight_all[:, run_of_512(0)], in_=wgo[:, run_of_512(0)])
+        state = [
+            shared.tile([P, T], F32, name="state%d" % b, offset=b * STATE_BYTES) for b in range(ROW_BLOCKS)
+        ]
+        for b in range(ROW_BLOCKS):
+            nc.sync.dma_start(out=state[b][:], in_=rT[run_of_128(b), :])
         nc.sync.dma_start(out=weight_all[:, run_of_512(1)], in_=wgo[:, run_of_512(1)])
+
+        def gather_words(words, entries, h):
+            nc.vector.tensor_copy(words[:], tab_w[:].bitcast(U32).indirect(entries[:, list_columns(h)]))
+
+        src_words = [held.tile([P, HALF], U32, align_bytes=64, name="src0")]
+        dst_words = [held.tile([P, HALF], U32, align_bytes=64, name="dst0")]
+        gather_words(src_words[0], src_list, 0)
+        gather_words(dst_words[0], dst_list, 0)
+        nc.vector.quantize_mx(out=wc_w[:].bitcast(FP8X4), scales=wc_s[:], in_=wc_bf[:].rearrange("p n i -> p (n i)"))
+        second_at = RAW_AT + RAW_BYTES
+        src_words.append(shared.tile([P, HALF], U32, align_bytes=64, name="src1", offset=second_at))
+        dst_words.append(shared.tile([P, HALF], U32, align_bytes=64, name="dst1", offset=second_at + 4 * HALF))
+        gather_words(src_words[1], src_list, 1)
+        gather_words(dst_words[1], dst_list, 1)
 
         picked = []
         for b in range(ROW_BLOCKS):
             picked.append(held.tile([P, J], F32, name="picked%d" % b)[:])
             nc.vector.tensor_copy(picked[b], state[b][:].indirect(dst_list[:]))
-        late = shared.tile([P, 3, J], F32, offset=STATE3_AT)
-        late_gated = late[:].rearrange("p r j -> p (r j)")
-        result = [results[:, u, :] for u in range(len(PIECES))]
-        summed = [result[FIRST_PIECES + 1 - u] for u in range(FIRST_PIECES)]
 
-        def buffer(kind, u):
-            if u < FIRST_LATE or kind != GATED:
-                return early[:, kind, u, :]
-            return late_gated[:, run_of_512(u - FIRST_LATE)]
+        za_banks = [psum.tile([P, HALF], F32, name="za%d" % i) for i in range(BANKS)]
+        ms_banks = [psum.tile([P, HALF], F32, name="ms%d" % i) for i in range(BANKS)]
 
-        za = psum.tile([P, HALF], F32)
-        ms = psum.tile([P, HALF], F32)
-        turned_banks = [psum.tile([P, HALF], F32, name="turned%d" % i) for i in range(TURN_BANKS)]
-        back_banks = [psum.tile([P, HALF], F32, name="back%d" % i) for i in range(TURN_BANKS)]
+        turned = psum.tile([P, HALF], F32)
+        back = psum.tile([P, HALF], F32)
+        nc.tensor.transpose(back[:, 0:P], weight_rows[:], identity[:])
+        nc.scalar.copy(weight_col[:], back[:, WEIGHT_ROW:P])
 
-        nc.tensor.transpose(back_banks[0][:, 0:P], weight_rows[:], identity[:])
-        nc.scalar.copy(weight_col[:], back_banks[0][:, WEIGHT_ROW:P])
-
-        def products(u):
-            b, h = PIECES[u]
+        def products(b, h):
             n, j = run_of_128(b), run_of_512(h)
-            dst_w, src_w = dst_words[h], src_words[h]
-            nc.tensor.matmul_mx(
-                za[:], lhsT=wa_w[:, n].bitcast(FP8X4), lhsT_scale=wa_s.bitcast(U8)[:, n],
-                rhs=dst_w, rhs_scale=dst_s[:, j], start=True, stop=False,
-            )
+            u = h * 2 + b
+            za, ms = (za_banks[u % BANKS], ms_banks[u % BANKS]) if b < 2 else (turned, back)
+            dst_w, src_w = dst_words[h][:].bitcast(FP8X4), src_words[h][:].bitcast(FP8X4)
             nc.tensor.matmul_mx(
                 za[:], lhsT=wb_w[:, n].bitcast(FP8X4), lhsT_scale=wb_s.bitcast(U8)[:, n],
-                rhs=src_w, rhs_scale=src_s[:, j], start=False, stop=True,
+                rhs=src_w, rhs_scale=src_s[:, j], start=True, stop=False,
+            )
+            nc.tensor.matmul_mx(
+                za[:], lhsT=wa_w[:, n].bitcast(FP8X4), lhsT_scale=wa_s.bitcast(U8)[:, n],
+                rhs=dst_w, rhs_scale=dst_s[:, j], start=False, stop=True,
             )
             nc.tensor.matmul_mx(
                 ms[:], lhsT=wc_w[:, n].bitcast(FP8X4), lhsT_scale=wc_s[:, n],
                 rhs=src_w, rhs_scale=src_s[:, j], start=True, stop=True,
             )
-            gate, message, gated = buffer(GATE, u), buffer(MESSAGE, u), buffer(GATED, u)
-            nc.scalar.activation(gate, za[:], SIGMOID)
-            nc.scalar.copy(message, ms[:])
-            nc.gpsimd.tensor_tensor(gated, gate, message, MULT)
-            if u < FIRST_PIECES:
-                nc.gpsimd.tensor_tensor(summed[u], gated, picked[b][:, j], ADD)
-                nc.gpsimd.tensor_tensor(result[u], summed[u], weight_all[:, j], MULT)
-            elif u not in TURNED:
-                nc.gpsimd.tensor_tensor(result[u], gated, picked[b][:, j], ADD)
+            nc.scalar.activation(gates[:, b, j], za[:], SIGMOID)
+            nc.scalar.copy(messages[:, b, j], ms[:])
 
-        def turn(u):
-            b, h = PIECES[u]
-            gated, residual = buffer(GATED, u), picked[b][:, run_of_512(h)]
-            turned, back = turned_banks[u % TURN_BANKS], back_banks[u % TURN_BANKS]
+        gated = [work[0], work[1], work[2], work[0]]
+        summed = [work[2], work[2], work[0]]
+
+        def finish(b):
+            window = placed[b % WINDOWS]
+            if b == LAST:
+                nc.gpsimd.tensor_tensor(results[:, b, :], gated[b][:], picked[b], ADD)
+                nc.vector.tensor_tensor(window[:].indirect(dst_list[:]), results[:, b, :], weight_all[:], MULT)
+            else:
+                nc.gpsimd.tensor_tensor(summed[b][:], gated[b][:], picked[b], ADD)
+                nc.gpsimd.tensor_tensor(results[:, b, :], summed[b][:], weight_all[:], MULT)
+                nc.vector.tensor_copy(window[:].indirect(dst_list[:]), results[:, b, :])
+            nc.sync.dma_start(out=out[run_of_128(b), :], in_=window[:])
+
+        first, second = run_of_512(0), run_of_512(1)
+
+        def turn():
             for s in range(SQUARES):
                 square = run_of_128(s)
                 nc.tensor.matmul(
-                    turned[:, square], gated[:, square], identity[:], start=True, stop=False, is_transpose=True
+                    turned[:, square], picked[0][:, square], identity[:], start=(s == 0), stop=False, is_transpose=True
                 )
-                nc.tensor.matmul(
-                    turned[:, square], residual[:, square], identity[:], start=False, stop=True, is_transpose=True
-                )
-            weighted = ring.tile([P, HALF], F32, name="weighted")[:]
             for s in range(SQUARES):
-                c = h * SQUARES + s
-                nc.scalar.activation(weighted[:, run_of_128(s)], turned[:, run_of_128(s)], COPY, scale=weight_col[:, c : c + 1])
+                square = run_of_128(s)
+                nc.tensor.matmul(
+                    turned[:, square], gated[0][:, square], identity[:],
+                    start=False, stop=(s == SQUARES - 1), is_transpose=True,
+                )
+            for s in range(SQUARES):
+                square = run_of_128(s)
+                nc.scalar.activation(weighted[:, square], turned[:, square], COPY, scale=weight_col[:, s : s + 1])
             for s in range(SQUARES):
                 nc.tensor.transpose(back[:, run_of_128(s)], weighted[:, run_of_128(s)], identity[:])
-            nc.scalar.copy(result[u], back[:])
+            nc.scalar.copy(results[:, 0, first], back[:])
 
-        for u in range(len(PIECES)):
-            products(u)
-            if u in TURNED:
-                turn(u)
-
-        for u, (b, h) in enumerate(PIECES[: 2 * HALVES]):
-            window = placed[b % WINDOWS]
-            nc.vector.tensor_copy(window[:].indirect(dst_list[:, list_columns(h)]), result[u])
-            if h == HALVES - 1:
-                nc.sync.dma_start(out=out[run_of_128(b), :], in_=window[:])
+        for h in range(HALVES):
+            for b in range(2):
+                products(b, h)
+                j = run_of_512(h)
+                nc.gpsimd.tensor_tensor(gated[b][:, j], gates[:, b, j], messages[:, b, j], MULT)
+        turn()
+        nc.gpsimd.tensor_tensor(summed[0][:, second], gated[0][:, second], picked[0][:, second], ADD)
+        nc.gpsimd.tensor_tensor(results[:, 0, second], summed[0][:, second], weight_all[:, second], MULT)
+        nc.vector.tensor_copy(placed[0][:].indirect(dst_list[:]), results[:, 0, :])
+        nc.sync.dma_start(out=out[run_of_128(0), :], in_=placed[0][:])
+        finish(1)
         for b in range(2, ROW_BLOCKS):
-            window = placed[2 if b == NEXT_TO_LAST else 1]
-            first = b * HALVES
-            both = results[:, first : first + HALVES, :].rearrange("p h j -> p (h j)")
-            if b == LAST:
-                nc.vector.tensor_tensor(window[:].indirect(dst_list[:]), both, weight_all[:], MULT)
-            else:
-                nc.vector.tensor_copy(window[:].indirect(dst_list[:]), both)
-            nc.sync.dma_start(out=out[run_of_128(b), :], in_=window[:])
+            for h in range(HALVES):
+                products(b, h)
+            nc.gpsimd.tensor_tensor(gated[b][:], gates[:, b, :], messages[:, b, :], MULT)
+            finish(b)

@@ -30,17 +30,17 @@ ROW_BLOCKS = N // P
 HALF = 512
 HALVES = J // HALF
 WINDOWS = 2
-BANKS = 3
+BANKS = 2
 SQUARES = HALF // P
-WEIGHT_ROW = P - SQUARES
+WEIGHT_ROW = P - J // P
 LAST = ROW_BLOCKS - 1
 STAGE = P - SCALE_ROWS
-WC_HALF = N // 2
-STATE_BYTES = 4 * T
-TABLE_AT = STATE_BYTES - T // 2
-PICKED_AT = 3 * STATE_BYTES - J
-RAW_AT = ROW_BLOCKS * STATE_BYTES
-RAW_BYTES = 4 * PACK * WC_HALF
+STATE1_AT = 0
+STATE2_AT = STATE1_AT + 4 * T
+TABLE_AT = STATE2_AT - T // 2
+PICKED_AT = STATE2_AT + 4 * T
+STATE3_AT = PICKED_AT + 4 * P
+RAW_AT = STATE3_AT + 4 * T
 
 
 def tile_list_rgg_L_kernel(
@@ -61,9 +61,6 @@ def tile_list_rgg_L_kernel(
     def run_of_512(i):
         return slice(i * HALF, (i + 1) * HALF)
 
-    def list_columns(h):
-        return slice(h * HALF // LIST_ROWS, (h + 1) * HALF // LIST_ROWS)
-
     with ExitStack() as ctx:
         held = ctx.enter_context(tc.tile_pool(name="held", bufs=1))
         psum = ctx.enter_context(tc.psum_pool(name="psum", bufs=1))
@@ -75,10 +72,7 @@ def tile_list_rgg_L_kernel(
         tab_w = held.tile([P, T], I32, align_bytes=64)
         wa_w = held.tile([P, N], I32, align_bytes=64)
         wb_w = held.tile([P, N], I32, align_bytes=64)
-        wc_raw = [
-            shared.tile([P, PACK, WC_HALF], F32, offset=RAW_AT + i * RAW_BYTES, align_bytes=64, name="wc_raw%d" % i)
-            for i in range(2)
-        ]
+        wc_raw = shared.tile([P, PACK, N], F32, offset=RAW_AT, align_bytes=64)
         wc_bf = held.tile([P, N, PACK], BF16, align_bytes=64)
         wc_w = held.tile([P, N], U32, align_bytes=64)
         wc_s = held.tile([P, N], U8, align_bytes=64)
@@ -92,14 +86,14 @@ def tile_list_rgg_L_kernel(
         gates = held.tile([P, ROW_BLOCKS, J], F32)
         messages = held.tile([P, ROW_BLOCKS, J], F32)
         results = held.tile([P, ROW_BLOCKS, J], F32)
-        work = [held.tile([P, J], F32, name="work%d" % i) for i in range(3)]
+        work = [held.tile([P, J], F32, name="work%d" % i) for i in range(2)]
         placed = [held.tile([P, T], F32, name="placed%d" % i) for i in range(WINDOWS)]
 
-        weight_col = held.tile([P, SQUARES], F32)
+        weight_col = held.tile([P, J // P], F32)
         weight_rows = held.tile([P, P], F32)
         identity = held.tile([P, P], F32)
-        weighted = held.tile([P, HALF], F32)
-        weight_all = held.tile([P, J], F32)
+        weighted_tiles = [held.tile([P, HALF], F32, name="weighted%d" % i) for i in range(BANKS)]
+        state = [held.tile([P, T], F32, name="state0")]
 
         nc.gpsimd.memset(tab_s[0:STAGE, :], 0)
         nc.gpsimd.memset(w_s[:], 0)
@@ -115,45 +109,36 @@ def tile_list_rgg_L_kernel(
         nc.sync.dma_start(out=staged[STAGE:P, wa_at:wb_at], in_=wa_scales[0].bitcast(I32))
         nc.sync.dma_start(out=staged[STAGE:P, wb_at : wb_at + N // PACK], in_=wb_scales[0].bitcast(I32))
         nc.sync.dma_start(out=tab_w[:], in_=words_of(tab_words))
-        wc_rows = wc.rearrange("(p i) n -> p i n", i=PACK)
-        for i in range(2):
-            nc.sync.dma_start(out=wc_raw[i][:], in_=wc_rows[:, :, i * WC_HALF : (i + 1) * WC_HALF])
+        nc.sync.dma_start(out=wc_raw[:], in_=wc.rearrange("(p i) n -> p i n", i=PACK))
         move_scales(w_s, staged[:])
         nc.sync.dma_start(out=wa_w[:], in_=words_of(wa_words))
         nc.sync.dma_start(out=wb_w[:], in_=words_of(wb_words))
-        nc.sync.dma_start(out=weight_rows[WEIGHT_ROW:P, :], in_=wgo[0, 0:HALF].rearrange("(c j) -> c j", j=P))
-        nc.sync.dma_start(out=weight_all[:, run_of_512(0)], in_=wgo[:, run_of_512(0)])
+        nc.sync.dma_start(out=state[0][:], in_=rT[run_of_128(0), :])
+        nc.sync.dma_start(out=weight_rows[WEIGHT_ROW:P, :], in_=wgo[0].rearrange("(c j) -> c j", j=P))
 
-        for i in range(2):
-            nc.scalar.copy(
-                wc_bf[:, i * WC_HALF : (i + 1) * WC_HALF, :].rearrange("p (c m) i -> p c i m", m=COLUMN_RUN),
-                wc_raw[i][:].rearrange("p i (c m) -> p c i m", m=COLUMN_RUN),
-            )
+        nc.scalar.copy(
+            wc_bf[:].rearrange("p (c m) i -> p c i m", m=COLUMN_RUN),
+            wc_raw[:].rearrange("p i (c m) -> p c i m", m=COLUMN_RUN),
+        )
 
         nc.vector.tensor_copy(picked_s[:, 0:J], tab_s[:].bitcast(U8).indirect(src_list[:]))
         nc.vector.tensor_copy(picked_s[:, J : 2 * J], tab_s[:].bitcast(U8).indirect(dst_list[:]))
 
         move_scales(planes, picked_s[:].bitcast(I32))
-        state = [
-            shared.tile([P, T], F32, name="state%d" % b, offset=b * STATE_BYTES) for b in range(ROW_BLOCKS)
-        ]
-        for b in range(ROW_BLOCKS):
+        state.append(shared.tile([P, T], F32, name="state1", offset=STATE1_AT))
+        state.append(shared.tile([P, T], F32, name="state2", offset=STATE2_AT))
+        state.append(shared.tile([P, T], F32, name="state3", offset=STATE3_AT))
+        weight_all = shared.tile([P, J], F32, offset=RAW_AT)
+        for b in range(1, ROW_BLOCKS):
             nc.sync.dma_start(out=state[b][:], in_=rT[run_of_128(b), :])
-        nc.sync.dma_start(out=weight_all[:, run_of_512(1)], in_=wgo[:, run_of_512(1)])
+        for h in reversed(range(HALVES)):
+            nc.sync.dma_start(out=weight_all[:, run_of_512(h)], in_=wgo[:, run_of_512(h)])
 
-        def gather_words(words, entries, h):
-            nc.vector.tensor_copy(words[:], tab_w[:].bitcast(U32).indirect(entries[:, list_columns(h)]))
-
-        src_words = [held.tile([P, HALF], U32, align_bytes=64, name="src0")]
-        dst_words = [held.tile([P, HALF], U32, align_bytes=64, name="dst0")]
-        gather_words(src_words[0], src_list, 0)
-        gather_words(dst_words[0], dst_list, 0)
+        src_words = held.tile([P, J], U32, align_bytes=64)
+        dst_words = held.tile([P, J], U32, align_bytes=64)
+        nc.vector.tensor_copy(src_words[:], tab_w[:].bitcast(U32).indirect(src_list[:]))
+        nc.vector.tensor_copy(dst_words[:], tab_w[:].bitcast(U32).indirect(dst_list[:]))
         nc.vector.quantize_mx(out=wc_w[:].bitcast(FP8X4), scales=wc_s[:], in_=wc_bf[:].rearrange("p n i -> p (n i)"))
-        second_at = RAW_AT + RAW_BYTES
-        src_words.append(shared.tile([P, HALF], U32, align_bytes=64, name="src1", offset=second_at))
-        dst_words.append(shared.tile([P, HALF], U32, align_bytes=64, name="dst1", offset=second_at + 4 * HALF))
-        gather_words(src_words[1], src_list, 1)
-        gather_words(dst_words[1], dst_list, 1)
 
         picked = []
         for b in range(ROW_BLOCKS):
@@ -163,16 +148,15 @@ def tile_list_rgg_L_kernel(
         za_banks = [psum.tile([P, HALF], F32, name="za%d" % i) for i in range(BANKS)]
         ms_banks = [psum.tile([P, HALF], F32, name="ms%d" % i) for i in range(BANKS)]
 
-        turned = psum.tile([P, HALF], F32)
-        back = psum.tile([P, HALF], F32)
-        nc.tensor.transpose(back[:, 0:P], weight_rows[:], identity[:])
-        nc.scalar.copy(weight_col[:], back[:, WEIGHT_ROW:P])
+        turned_banks = [psum.tile([P, HALF], F32, name="turned%d" % i) for i in range(BANKS)]
+        back_banks = [psum.tile([P, HALF], F32, name="back%d" % i) for i in range(BANKS)]
+        nc.tensor.transpose(back_banks[0][:, 0:P], weight_rows[:], identity[:])
+        nc.scalar.copy(weight_col[:], back_banks[0][:, WEIGHT_ROW:P])
 
         def products(b, h):
             n, j = run_of_128(b), run_of_512(h)
-            u = h * 2 + b
-            za, ms = (za_banks[u % BANKS], ms_banks[u % BANKS]) if b < 2 else (turned, back)
-            dst_w, src_w = dst_words[h][:].bitcast(FP8X4), src_words[h][:].bitcast(FP8X4)
+            za, ms = za_banks[h], ms_banks[h]
+            dst_w, src_w = dst_words[:, j].bitcast(FP8X4), src_words[:, j].bitcast(FP8X4)
             nc.tensor.matmul_mx(
                 za[:], lhsT=wb_w[:, n].bitcast(FP8X4), lhsT_scale=wb_s.bitcast(U8)[:, n],
                 rhs=src_w, rhs_scale=src_s[:, j], start=True, stop=False,
@@ -188,54 +172,47 @@ def tile_list_rgg_L_kernel(
             nc.scalar.activation(gates[:, b, j], za[:], SIGMOID)
             nc.scalar.copy(messages[:, b, j], ms[:])
 
-        gated = [work[0], work[1], work[2], work[0]]
-        summed = [work[2], work[2], work[0]]
-
-        def finish(b):
-            window = placed[b % WINDOWS]
-            if b == LAST:
-                nc.gpsimd.tensor_tensor(results[:, b, :], gated[b][:], picked[b], ADD)
-                nc.vector.tensor_tensor(window[:].indirect(dst_list[:]), results[:, b, :], weight_all[:], MULT)
-            else:
-                nc.gpsimd.tensor_tensor(summed[b][:], gated[b][:], picked[b], ADD)
-                nc.gpsimd.tensor_tensor(results[:, b, :], summed[b][:], weight_all[:], MULT)
-                nc.vector.tensor_copy(window[:].indirect(dst_list[:]), results[:, b, :])
-            nc.sync.dma_start(out=out[run_of_128(b), :], in_=window[:])
-
         first, second = run_of_512(0), run_of_512(1)
+        gated = [work[0][:], work[1][:], None, gates[:, 2, :]]
+        gated_halves = [[work[b][:, first], work[b][:, second]] for b in range(2)]
+        gated_halves.append([gates[:, 1, second], work[0][:, second]])
+        summed = [work[1][:], work[0][:]]
 
-        def turn():
+        def turn(b, h):
+            turned, back, weighted = turned_banks[(b + h) % BANKS], back_banks[(b + h) % BANKS], weighted_tiles[(b + h) % BANKS]
             for s in range(SQUARES):
-                square = run_of_128(s)
+                square, edges = run_of_128(s), run_of_128(h * SQUARES + s)
                 nc.tensor.matmul(
-                    turned[:, square], picked[0][:, square], identity[:], start=(s == 0), stop=False, is_transpose=True
+                    turned[:, square], gated_halves[b][h][:, square], identity[:], start=True, stop=False, is_transpose=True
+                )
+                nc.tensor.matmul(
+                    turned[:, square], picked[b][:, edges], identity[:], start=False, stop=True, is_transpose=True
                 )
             for s in range(SQUARES):
-                square = run_of_128(s)
-                nc.tensor.matmul(
-                    turned[:, square], gated[0][:, square], identity[:],
-                    start=False, stop=(s == SQUARES - 1), is_transpose=True,
-                )
-            for s in range(SQUARES):
-                square = run_of_128(s)
-                nc.scalar.activation(weighted[:, square], turned[:, square], COPY, scale=weight_col[:, s : s + 1])
+                c = h * SQUARES + s
+                nc.scalar.activation(weighted[:, run_of_128(s)], turned[:, run_of_128(s)], COPY, scale=weight_col[:, c : c + 1])
             for s in range(SQUARES):
                 nc.tensor.transpose(back[:, run_of_128(s)], weighted[:, run_of_128(s)], identity[:])
-            nc.scalar.copy(results[:, 0, first], back[:])
+            nc.scalar.copy(results[:, b, run_of_512(h)], back[:])
 
-        for h in range(HALVES):
-            for b in range(2):
-                products(b, h)
-                j = run_of_512(h)
-                nc.gpsimd.tensor_tensor(gated[b][:, j], gates[:, b, j], messages[:, b, j], MULT)
-        turn()
-        nc.gpsimd.tensor_tensor(summed[0][:, second], gated[0][:, second], picked[0][:, second], ADD)
-        nc.gpsimd.tensor_tensor(results[:, 0, second], summed[0][:, second], weight_all[:, second], MULT)
-        nc.vector.tensor_copy(placed[0][:].indirect(dst_list[:]), results[:, 0, :])
-        nc.sync.dma_start(out=out[run_of_128(0), :], in_=placed[0][:])
-        finish(1)
-        for b in range(2, ROW_BLOCKS):
+        for b in range(ROW_BLOCKS):
             for h in range(HALVES):
                 products(b, h)
-            nc.gpsimd.tensor_tensor(gated[b][:], gates[:, b, :], messages[:, b, :], MULT)
-            finish(b)
+                if b < LAST:
+                    j = run_of_512(h)
+                    nc.gpsimd.tensor_tensor(gated_halves[b][h], gates[:, b, j], messages[:, b, j], MULT)
+            if b == LAST:
+                nc.gpsimd.tensor_tensor(gated[b], gates[:, b, :], messages[:, b, :], MULT)
+            window = placed[b % WINDOWS]
+            if b == LAST:
+                nc.gpsimd.tensor_tensor(results[:, b, :], gated[b], picked[b], ADD)
+                nc.vector.tensor_tensor(window[:].indirect(dst_list[:]), results[:, b, :], weight_all[:], MULT)
+            else:
+                turn(b, 0)
+                if b < 2:
+                    nc.gpsimd.tensor_tensor(summed[b][:, second], gated[b][:, second], picked[b][:, second], ADD)
+                    nc.gpsimd.tensor_tensor(results[:, b, second], summed[b][:, second], weight_all[:, second], MULT)
+                else:
+                    turn(b, 1)
+                nc.vector.tensor_copy(window[:].indirect(dst_list[:]), results[:, b, :])
+            nc.sync.dma_start(out=out[run_of_128(b), :], in_=window[:])

@@ -173,10 +173,14 @@ def tile_list_rgg_L_kernel(
             nc.scalar.copy(messages[:, b, j], ms[:])
 
         first, second = run_of_512(0), run_of_512(1)
-        gated = [work[0][:], work[1][:], None, gates[:, 2, :]]
-        gated_halves = [[work[b][:, first], work[b][:, second]] for b in range(2)]
-        gated_halves.append([gates[:, 1, second], work[0][:, second]])
-        summed = [work[1][:], work[0][:]]
+        gated = [None, None, None, gates[:, 2, :]]
+        summed = [work[1][:, first], work[1][:, second]]
+        gated_halves = [
+            [work[0][:, first], work[0][:, second]],
+            [summed[0], gates[:, 1, first]],
+            [summed[1], gates[:, 2, first]],
+        ]
+        gated[LAST] = messages[:, 2, :]
 
         def turn(b, h):
             turned, back, weighted = turned_banks[(b + h) % BANKS], back_banks[(b + h) % BANKS], weighted_tiles[(b + h) % BANKS]
@@ -210,8 +214,8 @@ def tile_list_rgg_L_kernel(
             else:
                 turn(b, 0)
                 if b < 2:
-                    nc.gpsimd.tensor_tensor(summed[b][:, second], gated[b][:, second], picked[b][:, second], ADD)
-                    nc.gpsimd.tensor_tensor(results[:, b, second], summed[b][:, second], weight_all[:, second], MULT)
+                    nc.gpsimd.tensor_tensor(summed[b], gated_halves[b][1], picked[b][:, second], ADD)
+                    nc.gpsimd.tensor_tensor(results[:, b, second], summed[b], weight_all[:, second], MULT)
                 else:
                     turn(b, 1)
                 nc.vector.tensor_copy(window[:].indirect(dst_list[:]), results[:, b, :])

@@ -41,6 +41,10 @@ TABLE_AT = STATE2_AT - T // 2
 PICKED_AT = STATE2_AT + 4 * T
 STATE3_AT = PICKED_AT + 4 * P
 RAW_AT = STATE3_AT + 4 * T
+QUARTER = J // 4
+LATE_WORDS_AT = RAW_AT + 4 * J
+CAST_AT = RAW_AT + 4 * PACK * N
+WEIGHTED_AT = CAST_AT + 4 * J
 
 
 def tile_list_rgg_L_kernel(
@@ -73,7 +77,7 @@ def tile_list_rgg_L_kernel(
         wa_w = held.tile([P, N], I32, align_bytes=64)
         wb_w = held.tile([P, N], I32, align_bytes=64)
         wc_raw = shared.tile([P, PACK, N], F32, offset=RAW_AT, align_bytes=64)
-        wc_bf = held.tile([P, N, PACK], BF16, align_bytes=64)
+        wc_bf = shared.tile([P, N, PACK], BF16, offset=CAST_AT, align_bytes=64)
         wc_w = held.tile([P, N], U32, align_bytes=64)
         wc_s = held.tile([P, N], U8, align_bytes=64)
         picked_s = shared.tile([P, 2 * J], U8, offset=PICKED_AT, align_bytes=64)
@@ -92,7 +96,7 @@ def tile_list_rgg_L_kernel(
         weight_col = held.tile([P, J // P], F32)
         weight_rows = held.tile([P, P], F32)
         identity = held.tile([P, P], F32)
-        weighted_tiles = [held.tile([P, HALF], F32, name="weighted%d" % i) for i in range(BANKS)]
+        weighted_even = held.tile([P, HALF], F32)
         state = [held.tile([P, T], F32, name="state0")]
 
         nc.gpsimd.memset(tab_s[0:STAGE, :], 0)
@@ -113,8 +117,7 @@ def tile_list_rgg_L_kernel(
         move_scales(w_s, staged[:])
         nc.sync.dma_start(out=wa_w[:], in_=words_of(wa_words))
         nc.sync.dma_start(out=wb_w[:], in_=words_of(wb_words))
-        nc.sync.dma_start(out=state[0][:], in_=rT[run_of_128(0), :])
-        nc.sync.dma_start(out=weight_rows[WEIGHT_ROW:P, :], in_=wgo[0].rearrange("(c j) -> c j", j=P))
+        nc.sync.dma_start(out=state[0][:, 0:J], in_=rT[run_of_128(0), 0:J])
 
         nc.scalar.copy(
             wc_bf[:].rearrange("p (c m) i -> p c i m", m=COLUMN_RUN),
@@ -125,6 +128,8 @@ def tile_list_rgg_L_kernel(
         nc.vector.tensor_copy(picked_s[:, J : 2 * J], tab_s[:].bitcast(U8).indirect(dst_list[:]))
 
         move_scales(planes, picked_s[:].bitcast(I32))
+        nc.sync.dma_start(out=state[0][:, J:T], in_=rT[run_of_128(0), J:T])
+        nc.sync.dma_start(out=weight_rows[WEIGHT_ROW:P, :], in_=wgo[0].rearrange("(c j) -> c j", j=P))
         state.append(shared.tile([P, T], F32, name="state1", offset=STATE1_AT))
         state.append(shared.tile([P, T], F32, name="state2", offset=STATE2_AT))
         state.append(shared.tile([P, T], F32, name="state3", offset=STATE3_AT))
@@ -135,28 +140,41 @@ def tile_list_rgg_L_kernel(
             nc.sync.dma_start(out=weight_all[:, run_of_512(h)], in_=wgo[:, run_of_512(h)])
 
         src_words = held.tile([P, J], U32, align_bytes=64)
-        dst_words = held.tile([P, J], U32, align_bytes=64)
+        dst_words = [
+            held.tile([P, HALF], U32, name="dst_words0", align_bytes=64),
+            shared.tile([P, HALF], U32, name="dst_words1", offset=LATE_WORDS_AT, align_bytes=64),
+        ]
         nc.vector.tensor_copy(src_words[:], tab_w[:].bitcast(U32).indirect(src_list[:]))
-        nc.vector.tensor_copy(dst_words[:], tab_w[:].bitcast(U32).indirect(dst_list[:]))
+        nc.vector.tensor_copy(dst_words[0][:], tab_w[:].bitcast(U32).indirect(dst_list[:, 0 : HALF // LIST_ROWS]))
         nc.vector.quantize_mx(out=wc_w[:].bitcast(FP8X4), scales=wc_s[:], in_=wc_bf[:].rearrange("p n i -> p (n i)"))
+        nc.vector.tensor_copy(dst_words[1][:], tab_w[:].bitcast(U32).indirect(dst_list[:, HALF // LIST_ROWS : J // LIST_ROWS]))
 
         picked = []
-        for b in range(ROW_BLOCKS):
-            picked.append(held.tile([P, J], F32, name="picked%d" % b)[:])
+        for b in range(LAST):
+            if b == 0:
+                picked.append(shared.tile([P, J], F32, name="picked0", offset=CAST_AT)[:])
+            else:
+                picked.append(held.tile([P, J], F32, name="picked%d" % b)[:])
             nc.vector.tensor_copy(picked[b], state[b][:].indirect(dst_list[:]))
+        last_picked = [held.tile([P, HALF], F32, name="picked_early")]
+        last_edges = [slice(0, HALF), slice(HALF, HALF + QUARTER), slice(HALF + QUARTER, J)]
+
+        def pick_last(i):
+            columns = slice(last_edges[i].start // LIST_ROWS, last_edges[i].stop // LIST_ROWS)
+            nc.vector.tensor_copy(last_picked[i][:], state[LAST][:].indirect(dst_list[:, columns]))
+
+        pick_last(0)
 
         za_banks = [psum.tile([P, HALF], F32, name="za%d" % i) for i in range(BANKS)]
         ms_banks = [psum.tile([P, HALF], F32, name="ms%d" % i) for i in range(BANKS)]
 
         turned_banks = [psum.tile([P, HALF], F32, name="turned%d" % i) for i in range(BANKS)]
         back_banks = [psum.tile([P, HALF], F32, name="back%d" % i) for i in range(BANKS)]
-        nc.tensor.transpose(back_banks[0][:, 0:P], weight_rows[:], identity[:])
-        nc.scalar.copy(weight_col[:], back_banks[0][:, WEIGHT_ROW:P])
 
         def products(b, h):
             n, j = run_of_128(b), run_of_512(h)
             za, ms = za_banks[h], ms_banks[h]
-            dst_w, src_w = dst_words[:, j].bitcast(FP8X4), src_words[:, j].bitcast(FP8X4)
+            dst_w, src_w = dst_words[h][:].bitcast(FP8X4), src_words[:, j].bitcast(FP8X4)
             nc.tensor.matmul_mx(
                 za[:], lhsT=wb_w[:, n].bitcast(FP8X4), lhsT_scale=wb_s.bitcast(U8)[:, n],
                 rhs=src_w, rhs_scale=src_s[:, j], start=True, stop=False,
@@ -183,7 +201,9 @@ def tile_list_rgg_L_kernel(
         gated[LAST] = messages[:, 2, :]
 
         def turn(b, h):
-            turned, back, weighted = turned_banks[(b + h) % BANKS], back_banks[(b + h) % BANKS], weighted_tiles[(b + h) % BANKS]
+            turned, back, weighted = turned_banks[(b + h) % BANKS], back_banks[(b + h) % BANKS], weighted_even
+            if (b, h) in ((1, 0), (2, 1)):
+                weighted = shared.tile([P, HALF], F32, name="weighted%d%d" % (b, h), offset=WEIGHTED_AT + 4 * HALF * h)
             for s in range(SQUARES):
                 square, edges = run_of_128(s), run_of_128(h * SQUARES + s)
                 nc.tensor.matmul(
@@ -198,6 +218,9 @@ def tile_list_rgg_L_kernel(
             for s in range(SQUARES):
                 nc.tensor.transpose(back[:, run_of_128(s)], weighted[:, run_of_128(s)], identity[:])
             nc.scalar.copy(results[:, b, run_of_512(h)], back[:])
+            if (b, h) in ((1, 0), (2, 1)):
+                last_picked.append(shared.tile([P, QUARTER], F32, name="picked_late%d" % h, offset=WEIGHTED_AT + 4 * HALF * h))
+                pick_last(1 + h)
 
         for b in range(ROW_BLOCKS):
             for h in range(HALVES):
@@ -207,9 +230,13 @@ def tile_list_rgg_L_kernel(
                     nc.gpsimd.tensor_tensor(gated_halves[b][h], gates[:, b, j], messages[:, b, j], MULT)
             if b == LAST:
                 nc.gpsimd.tensor_tensor(gated[b], gates[:, b, :], messages[:, b, :], MULT)
+            if b == 0:
+                nc.tensor.transpose(back_banks[0][:, 0:P], weight_rows[:], identity[:])
+                nc.scalar.copy(weight_col[:], back_banks[0][:, WEIGHT_ROW:P])
             window = placed[b % WINDOWS]
             if b == LAST:
-                nc.gpsimd.tensor_tensor(results[:, b, :], gated[b], picked[b], ADD)
+                for edges, values in zip(last_edges, last_picked):
+                    nc.gpsimd.tensor_tensor(results[:, b, edges], gated[b][:, edges], values[:], ADD)
                 nc.vector.tensor_tensor(window[:].indirect(dst_list[:]), results[:, b, :], weight_all[:], MULT)
             else:
                 turn(b, 0)

@@ -41,10 +41,12 @@ TABLE_AT = STATE2_AT - T // 2
 PICKED_AT = STATE2_AT + 4 * T
 STATE3_AT = PICKED_AT + 4 * P
 RAW_AT = STATE3_AT + 4 * T
-QUARTER = J // 4
+WEIGHTS_AT = RAW_AT
 LATE_WORDS_AT = RAW_AT + 4 * J
 CAST_AT = RAW_AT + 4 * PACK * N
-WEIGHTED_AT = CAST_AT + 4 * J
+QUARTER = J // 4
+PIECES_AT = CAST_AT + 4 * J
+PIECE_BYTES = 4 * HALF
 
 
 def tile_list_rgg_L_kernel(
@@ -64,6 +66,12 @@ def tile_list_rgg_L_kernel(
 
     def run_of_512(i):
         return slice(i * HALF, (i + 1) * HALF)
+
+    def run_of_256(i):
+        return slice(i * QUARTER, (i + 1) * QUARTER)
+
+    def entries(first, last):
+        return slice(first // LIST_ROWS, last // LIST_ROWS)
 
     with ExitStack() as ctx:
         held = ctx.enter_context(tc.tile_pool(name="held", bufs=1))
@@ -87,16 +95,11 @@ def tile_list_rgg_L_kernel(
         src_s, dst_s = planes[:].bitcast(U8)[:, 0:J], planes[:].bitcast(U8)[:, J : 2 * J]
         wa_at, wb_at = 0, N // PACK
         wa_s, wb_s = w_s[:, wa_at:wb_at], w_s[:, wb_at : wb_at + N // PACK]
-        gates = held.tile([P, ROW_BLOCKS, J], F32)
-        messages = held.tile([P, ROW_BLOCKS, J], F32)
-        results = held.tile([P, ROW_BLOCKS, J], F32)
-        work = [held.tile([P, J], F32, name="work%d" % i) for i in range(2)]
         placed = [held.tile([P, T], F32, name="placed%d" % i) for i in range(WINDOWS)]
 
         weight_col = held.tile([P, J // P], F32)
         weight_rows = held.tile([P, P], F32)
         identity = held.tile([P, P], F32)
-        weighted_even = held.tile([P, HALF], F32)
         state = [held.tile([P, T], F32, name="state0")]
 
         nc.gpsimd.memset(tab_s[0:STAGE, :], 0)
@@ -129,13 +132,15 @@ def tile_list_rgg_L_kernel(
 
         move_scales(planes, picked_s[:].bitcast(I32))
         nc.sync.dma_start(out=state[0][:, J:T], in_=rT[run_of_128(0), J:T])
-        nc.sync.dma_start(out=weight_rows[WEIGHT_ROW:P, :], in_=wgo[0].rearrange("(c j) -> c j", j=P))
         state.append(shared.tile([P, T], F32, name="state1", offset=STATE1_AT))
         state.append(shared.tile([P, T], F32, name="state2", offset=STATE2_AT))
         state.append(shared.tile([P, T], F32, name="state3", offset=STATE3_AT))
-        weight_all = shared.tile([P, J], F32, offset=RAW_AT)
-        for b in range(1, ROW_BLOCKS):
-            nc.sync.dma_start(out=state[b][:], in_=rT[run_of_128(b), :])
+        weight_all = shared.tile([P, J], F32, offset=WEIGHTS_AT)
+        nc.sync.dma_start(out=state[1][:], in_=rT[run_of_128(1), :])
+        nc.sync.dma_start(out=state[2][:, 0:J], in_=rT[run_of_128(2), 0:J])
+        nc.sync.dma_start(out=weight_rows[WEIGHT_ROW:P, :], in_=wgo[0].rearrange("(c j) -> c j", j=P))
+        nc.sync.dma_start(out=state[2][:, J:T], in_=rT[run_of_128(2), J:T])
+        nc.sync.dma_start(out=state[LAST][:], in_=rT[run_of_128(LAST), :])
         for h in reversed(range(HALVES)):
             nc.sync.dma_start(out=weight_all[:, run_of_512(h)], in_=wgo[:, run_of_512(h)])
 
@@ -145,25 +150,30 @@ def tile_list_rgg_L_kernel(
             shared.tile([P, HALF], U32, name="dst_words1", offset=LATE_WORDS_AT, align_bytes=64),
         ]
         nc.vector.tensor_copy(src_words[:], tab_w[:].bitcast(U32).indirect(src_list[:]))
-        nc.vector.tensor_copy(dst_words[0][:], tab_w[:].bitcast(U32).indirect(dst_list[:, 0 : HALF // LIST_ROWS]))
+        nc.vector.tensor_copy(dst_words[0][:], tab_w[:].bitcast(U32).indirect(dst_list[:, entries(0, HALF)]))
         nc.vector.quantize_mx(out=wc_w[:].bitcast(FP8X4), scales=wc_s[:], in_=wc_bf[:].rearrange("p n i -> p (n i)"))
-        nc.vector.tensor_copy(dst_words[1][:], tab_w[:].bitcast(U32).indirect(dst_list[:, HALF // LIST_ROWS : J // LIST_ROWS]))
+        nc.vector.tensor_copy(dst_words[1][:], tab_w[:].bitcast(U32).indirect(dst_list[:, entries(HALF, J)]))
 
-        picked = []
-        for b in range(LAST):
-            if b == 0:
-                picked.append(shared.tile([P, J], F32, name="picked0", offset=CAST_AT)[:])
-            else:
-                picked.append(held.tile([P, J], F32, name="picked%d" % b)[:])
-            nc.vector.tensor_copy(picked[b], state[b][:].indirect(dst_list[:]))
-        last_picked = [held.tile([P, HALF], F32, name="picked_early")]
-        last_edges = [slice(0, HALF), slice(HALF, HALF + QUARTER), slice(HALF + QUARTER, J)]
+        def offsets_of(piece):
+            return dst_list[:, entries(piece.start, piece.stop)]
 
-        def pick_last(i):
-            columns = slice(last_edges[i].start // LIST_ROWS, last_edges[i].stop // LIST_ROWS)
-            nc.vector.tensor_copy(last_picked[i][:], state[LAST][:].indirect(dst_list[:, columns]))
+        def placed_at(name, kib, width):
+            return shared.tile([P, width], F32, name=name, offset=PIECES_AT + int(1024 * kib))
 
-        pick_last(0)
+        picked = {}
+
+        def pick(b, edges, tile):
+            nc.vector.tensor_copy(tile, state[b][:].indirect(offsets_of(edges)))
+            for s in range(edges.start // P, edges.stop // P):
+                picked[b, s] = tile[:, s * P - edges.start : (s + 1) * P - edges.start]
+
+        picked0 = shared.tile([P, J], F32, offset=CAST_AT)
+        picked1 = held.tile([P, J], F32)
+        picked2 = held.tile([P, HALF], F32)
+        for h in range(HALVES):
+            pick(0, run_of_512(h), picked0[:, run_of_512(h)])
+        pick(1, slice(0, J), picked1[:])
+        pick(2, run_of_512(0), picked2[:])
 
         za_banks = [psum.tile([P, HALF], F32, name="za%d" % i) for i in range(BANKS)]
         ms_banks = [psum.tile([P, HALF], F32, name="ms%d" % i) for i in range(BANKS)]
@@ -171,9 +181,12 @@ def tile_list_rgg_L_kernel(
         turned_banks = [psum.tile([P, HALF], F32, name="turned%d" % i) for i in range(BANKS)]
         back_banks = [psum.tile([P, HALF], F32, name="back%d" % i) for i in range(BANKS)]
 
-        def products(b, h):
+        gated = {}
+
+        def products(b, h, gates, messages):
             n, j = run_of_128(b), run_of_512(h)
-            za, ms = za_banks[h], ms_banks[h]
+            bank = len(gated) % BANKS
+            za, ms = za_banks[bank], ms_banks[bank]
             dst_w, src_w = dst_words[h][:].bitcast(FP8X4), src_words[:, j].bitcast(FP8X4)
             nc.tensor.matmul_mx(
                 za[:], lhsT=wb_w[:, n].bitcast(FP8X4), lhsT_scale=wb_s.bitcast(U8)[:, n],
@@ -187,63 +200,117 @@ def tile_list_rgg_L_kernel(
                 ms[:], lhsT=wc_w[:, n].bitcast(FP8X4), lhsT_scale=wc_s[:, n],
                 rhs=src_w, rhs_scale=src_s[:, j], start=True, stop=True,
             )
-            nc.scalar.activation(gates[:, b, j], za[:], SIGMOID)
-            nc.scalar.copy(messages[:, b, j], ms[:])
+            nc.scalar.activation(gates, za[:], SIGMOID)
+            nc.scalar.copy(messages, ms[:])
 
-        first, second = run_of_512(0), run_of_512(1)
-        gated = [None, None, None, gates[:, 2, :]]
-        summed = [work[1][:, first], work[1][:, second]]
-        gated_halves = [
-            [work[0][:, first], work[0][:, second]],
-            [summed[0], gates[:, 1, first]],
-            [summed[1], gates[:, 2, first]],
-        ]
-        gated[LAST] = messages[:, 2, :]
+        WEIGHTED_A, SUM2, SUM3, SUM11, SUM21, WEIGHTED20 = 3.5, 9, 13, 20, 27, 31
+        WEIGHTED_B = SUM3 + 0.5
+        factors_at = {(1, 1): WEIGHTED_A - 3.5, (1, 0): WEIGHTED_A + 0.5, (2, 0): WEIGHTED_B + 0.75, (3, 1): WEIGHTED20}
+        gated_at = {
+            (1, 1): SUM2 + 0.5, (1, 0): factors_at[1, 1], (2, 0): SUM2 + 0.5, (2, 1): factors_at[2, 0],
+            (3, 0): SUM21 + 1,
+        }
 
-        def turn(b, h):
-            turned, back, weighted = turned_banks[(b + h) % BANKS], back_banks[(b + h) % BANKS], weighted_even
-            if (b, h) in ((1, 0), (2, 1)):
-                weighted = shared.tile([P, HALF], F32, name="weighted%d%d" % (b, h), offset=WEIGHTED_AT + 4 * HALF * h)
-            for s in range(SQUARES):
-                square, edges = run_of_128(s), run_of_128(h * SQUARES + s)
-                nc.tensor.matmul(
-                    turned[:, square], gated_halves[b][h][:, square], identity[:], start=True, stop=False, is_transpose=True
-                )
-                nc.tensor.matmul(
-                    turned[:, square], picked[b][:, edges], identity[:], start=False, stop=True, is_transpose=True
-                )
-            for s in range(SQUARES):
-                c = h * SQUARES + s
-                nc.scalar.activation(weighted[:, run_of_128(s)], turned[:, run_of_128(s)], COPY, scale=weight_col[:, c : c + 1])
-            for s in range(SQUARES):
-                nc.tensor.transpose(back[:, run_of_128(s)], weighted[:, run_of_128(s)], identity[:])
-            nc.scalar.copy(results[:, b, run_of_512(h)], back[:])
-            if (b, h) in ((1, 0), (2, 1)):
-                last_picked.append(shared.tile([P, QUARTER], F32, name="picked_late%d" % h, offset=WEIGHTED_AT + 4 * HALF * h))
-                pick_last(1 + h)
-
-        for b in range(ROW_BLOCKS):
-            for h in range(HALVES):
-                products(b, h)
-                if b < LAST:
-                    j = run_of_512(h)
-                    nc.gpsimd.tensor_tensor(gated_halves[b][h], gates[:, b, j], messages[:, b, j], MULT)
-            if b == LAST:
-                nc.gpsimd.tensor_tensor(gated[b], gates[:, b, :], messages[:, b, :], MULT)
-            if b == 0:
-                nc.tensor.transpose(back_banks[0][:, 0:P], weight_rows[:], identity[:])
-                nc.scalar.copy(weight_col[:], back_banks[0][:, WEIGHT_ROW:P])
-            window = placed[b % WINDOWS]
-            if b == LAST:
-                for edges, values in zip(last_edges, last_picked):
-                    nc.gpsimd.tensor_tensor(results[:, b, edges], gated[b][:, edges], values[:], ADD)
-                nc.vector.tensor_tensor(window[:].indirect(dst_list[:]), results[:, b, :], weight_all[:], MULT)
+        def gate(b, h):
+            if (b, h) in factors_at:
+                factors = placed_at("factors%d%d" % (b, h), factors_at[b, h], J)
             else:
-                turn(b, 0)
-                if b < 2:
-                    nc.gpsimd.tensor_tensor(summed[b], gated_halves[b][1], picked[b][:, second], ADD)
-                    nc.gpsimd.tensor_tensor(results[:, b, second], summed[b], weight_all[:, second], MULT)
-                else:
-                    turn(b, 1)
-                nc.vector.tensor_copy(window[:].indirect(dst_list[:]), results[:, b, :])
-            nc.sync.dma_start(out=out[run_of_128(b), :], in_=window[:])
+                factors = held.tile([P, J], F32, name="factors%d%d" % (b, h))
+            products(b, h, factors[:, 0:HALF], factors[:, HALF:J])
+            if (b, h) in gated_at:
+                gated[b, h] = placed_at("gated%d%d" % (b, h), gated_at[b, h], HALF)
+            else:
+                gated[b, h] = held.tile([P, HALF], F32, name="gated%d%d" % (b, h))
+            nc.gpsimd.tensor_tensor(gated[b, h][:], factors[:, 0:HALF], factors[:, HALF:J], MULT)
+
+        def turn_and_add(b, squares, turned):
+            for i, s in enumerate(squares):
+                nc.tensor.matmul(turned[:, run_of_128(i)], picked[b, s], identity[:], start=i == 0, stop=False, is_transpose=True)
+            for i, s in enumerate(squares):
+                nc.tensor.matmul(
+                    turned[:, run_of_128(i)], gated[b, s // SQUARES][:, run_of_128(s % SQUARES)], identity[:],
+                    start=False, stop=i == len(squares) - 1, is_transpose=True,
+                )
+
+        def turn_pairs(b, squares, turned):
+            for i, s in enumerate(squares):
+                nc.tensor.matmul(
+                    turned[:, run_of_128(i)], gated[b, s // SQUARES][:, run_of_128(s % SQUARES)], identity[:],
+                    start=True, stop=False, is_transpose=True,
+                )
+                nc.tensor.matmul(turned[:, run_of_128(i)], picked[b, s], identity[:], start=False, stop=True, is_transpose=True)
+
+        def weigh_and_turn_back(squares, turned, back, weighted, result):
+            for i, s in enumerate(squares):
+                nc.scalar.activation(weighted[:, run_of_128(i)], turned[:, run_of_128(i)], COPY, scale=weight_col[:, s : s + 1])
+            for i in range(len(squares)):
+                nc.tensor.transpose(back[:, run_of_128(i)], weighted[:, run_of_128(i)], identity[:])
+            nc.scalar.copy(result, back[:, 0 : len(squares) * P])
+
+        def scatter(window, edges, values):
+            nc.vector.tensor_copy(placed[window][:].indirect(offsets_of(edges)), values)
+
+        late = {}
+
+        def pick_late(b, q, kib):
+            late[b, q] = placed_at("late%d%d" % (b, q), kib, QUARTER)
+            pick(b, run_of_256(q), late[b, q][:])
+
+        pieces = [held.tile([P, QUARTER], F32, name="result0%d" % q) for q in range(4)]
+        results = [None] + [held.tile([P, J], F32, name="results%d" % b) for b in range(1, ROW_BLOCKS)]
+
+        def finish_on_gpsimd(b, residual, kib):
+            summed = placed_at("sum%d1" % b, kib, HALF)
+            for i, values in enumerate(residual):
+                width = HALF // len(residual)
+                part = slice(i * width, (i + 1) * width)
+                nc.gpsimd.tensor_tensor(summed[:, part], gated[b, 1][:, part], values, ADD)
+            nc.gpsimd.tensor_tensor(results[b][:, run_of_512(1)], summed[:], weight_all[:, run_of_512(1)], MULT)
+
+        gate(0, 0)
+        gate(0, 1)
+        nc.tensor.transpose(back_banks[1][:, 0:P], weight_rows[:], identity[:])
+        nc.scalar.copy(weight_col[:], back_banks[1][:, WEIGHT_ROW:P])
+        turn_and_add(0, (0, 1), za_banks[0])
+        weigh_and_turn_back((0, 1), za_banks[0], za_banks[1], placed_at("weighted_a", WEIGHTED_A, QUARTER), pieces[0][:])
+        scatter(0, run_of_256(0), pieces[0][:])
+        turn_and_add(0, (2, 3), turned_banks[1])
+        sums = {2: placed_at("sum2", SUM2, QUARTER), 3: placed_at("sum3", SUM3, QUARTER)}
+        for q in (2, 3):
+            nc.gpsimd.tensor_tensor(sums[q][:], gated[0, 1][:, run_of_256(q - 2)], picked0[:, run_of_256(q)], ADD)
+        for q in (2, 3):
+            nc.gpsimd.tensor_tensor(pieces[q][:], sums[q][:], weight_all[:, run_of_256(q)], MULT)
+        for q, kib in ((2, SUM2 - 0.5), (3, SUM3 - 0.75)):
+            pick_late(2, q, kib)
+            scatter(0, run_of_256(q), pieces[q][:])
+        weigh_and_turn_back((2, 3), turned_banks[1], back_banks[1], placed_at("weighted_b", WEIGHTED_B, QUARTER), pieces[1][:])
+        pick_late(LAST, 0, WEIGHTED_B - 0.25)
+        scatter(0, run_of_256(1), pieces[1][:])
+        nc.sync.dma_start(out=out[run_of_128(0), :], in_=placed[0][:])
+
+        gate(1, 1)
+        gate(1, 0)
+        finish_on_gpsimd(1, [picked1[:, run_of_512(1)]], SUM11)
+        pick_late(LAST, 1, SUM11)
+        scatter(1, run_of_512(1), results[1][:, run_of_512(1)])
+        turn_pairs(1, range(SQUARES), turned_banks[0])
+        weigh_and_turn_back(range(SQUARES), turned_banks[0], back_banks[0], placed_at("weighted10", SUM11 + 1, HALF), results[1][:, run_of_512(0)])
+        pick_late(LAST, 2, SUM11 + 1)
+        scatter(1, run_of_512(0), results[1][:, run_of_512(0)])
+        nc.sync.dma_start(out=out[run_of_128(1), :], in_=placed[1][:])
+
+        gate(2, 0)
+        gate(2, 1)
+        turn_pairs(2, range(SQUARES), turned_banks[1])
+        weigh_and_turn_back(range(SQUARES), turned_banks[1], back_banks[1], placed_at("weighted20", WEIGHTED20, HALF), results[2][:, run_of_512(0)])
+        finish_on_gpsimd(2, [late[2, 2][:], late[2, 3][:]], SUM21)
+        pick_late(LAST, 3, SUM21)
+        scatter(0, slice(0, J), results[2][:])
+        nc.sync.dma_start(out=out[run_of_128(2), :], in_=placed[0][:])
+
+        for h in range(HALVES):
+            gate(LAST, h)
+        for q in range(4):
+            nc.gpsimd.tensor_tensor(results[LAST][:, run_of_256(q)], gated[LAST, q // 2][:, run_of_256(q % 2)], late[LAST, q][:], ADD)
+        nc.vector.tensor_tensor(placed[1][:].indirect(dst_list[:]), results[LAST][:], weight_all[:], MULT)
+        nc.sync.dma_start(out=out[run_of_128(LAST), :], in_=placed[1][:])

@@ -27,14 +27,17 @@ GROUP_ROWS = QUADRANT * PACK // MX_BLOCK
 COLUMN_RUN = 4
 LIST_ROWS = 16
 ROW_BLOCKS = N // P
+LAST = ROW_BLOCKS - 1
 HALF = 512
 HALVES = J // HALF
+QUARTER = J // 4
+SQUARES = HALF // P
 WINDOWS = 2
 BANKS = 2
-SQUARES = HALF // P
-WEIGHT_ROW = P - J // P
-LAST = ROW_BLOCKS - 1
 STAGE = P - SCALE_ROWS
+WEIGHT_ROW = P - SQUARES
+KIB = 1024
+
 STATE1_AT = 0
 STATE2_AT = STATE1_AT + 4 * T
 TABLE_AT = STATE2_AT - T // 2
@@ -44,9 +47,34 @@ RAW_AT = STATE3_AT + 4 * T
 WEIGHTS_AT = RAW_AT
 LATE_WORDS_AT = RAW_AT + 4 * J
 CAST_AT = RAW_AT + 4 * PACK * N
-QUARTER = J // 4
 PIECES_AT = CAST_AT + 4 * J
-PIECE_BYTES = 4 * HALF
+
+WEIGHTED_Q0 = 3.5
+FACTORS_11 = WEIGHTED_Q0 - 3.5
+FACTORS_10 = WEIGHTED_Q0 + 0.5
+SUM_02 = 9
+LATE_22 = SUM_02 - 0.5
+GATED_11 = SUM_02 + 0.5
+SUM_03 = 13
+LATE_23 = SUM_03 - 0.75
+WEIGHTED_Q1 = SUM_03 + 0.5
+LATE_30 = WEIGHTED_Q1 - 0.25
+FACTORS_20 = WEIGHTED_Q1 + 0.75
+SUM_12 = 19
+LATE_31 = SUM_12
+SUM_13 = 20.5
+LATE_32 = SUM_13 - 0.5
+WEIGHTED_10 = SUM_13 + 0.5
+LATE_33 = WEIGHTED_10
+SUM_21 = 27
+GATED_30 = SUM_21 + 1
+GATED_31 = SUM_21 - 1
+WEIGHTED_20 = 31
+FACTORS_31 = WEIGHTED_20
+FACTORS_AT = {(1, 1): FACTORS_11, (1, 0): FACTORS_10, (2, 0): FACTORS_20, (LAST, 1): FACTORS_31}
+GATED_AT = {
+    (1, 1): GATED_11, (1, 0): FACTORS_11, (2, 0): GATED_11, (2, 1): FACTORS_20, (LAST, 0): GATED_30, (LAST, 1): GATED_31,
+}
 
 
 def tile_list_rgg_L_kernel(
@@ -57,21 +85,18 @@ def tile_list_rgg_L_kernel(
     def words_of(packed):
         return packed[0].rearrange("p n t -> p (n t)").bitcast(I32)
 
-    def move_scales(dest, rows):
+    def move_scales(plane, rows):
         for r in range(GROUP_ROWS):
-            nc.sync.dma_start(out=dest[r:P:QUADRANT, :], in_=rows[STAGE + r : P : GROUP_ROWS, :])
+            nc.sync.dma_start(out=plane[r:P:QUADRANT, :], in_=rows[STAGE + r : P : GROUP_ROWS, :])
 
     def run_of_128(i):
         return slice(i * P, (i + 1) * P)
 
-    def run_of_512(i):
-        return slice(i * HALF, (i + 1) * HALF)
-
     def run_of_256(i):
         return slice(i * QUARTER, (i + 1) * QUARTER)
 
-    def entries(first, last):
-        return slice(first // LIST_ROWS, last // LIST_ROWS)
+    def run_of_512(i):
+        return slice(i * HALF, (i + 1) * HALF)
 
     with ExitStack() as ctx:
         held = ctx.enter_context(tc.tile_pool(name="held", bufs=1))
@@ -96,8 +121,7 @@ def tile_list_rgg_L_kernel(
         wa_at, wb_at = 0, N // PACK
         wa_s, wb_s = w_s[:, wa_at:wb_at], w_s[:, wb_at : wb_at + N // PACK]
         placed = [held.tile([P, T], F32, name="placed%d" % i) for i in range(WINDOWS)]
-
-        weight_col = held.tile([P, J // P], F32)
+        weight_col = held.tile([P, SQUARES], F32)
         weight_rows = held.tile([P, P], F32)
         identity = held.tile([P, P], F32)
         state = [held.tile([P, T], F32, name="state0")]
@@ -120,7 +144,7 @@ def tile_list_rgg_L_kernel(
         move_scales(w_s, staged[:])
         nc.sync.dma_start(out=wa_w[:], in_=words_of(wa_words))
         nc.sync.dma_start(out=wb_w[:], in_=words_of(wb_words))
-        nc.sync.dma_start(out=state[0][:, 0:J], in_=rT[run_of_128(0), 0:J])
+        nc.sync.dma_start(out=state[0][:, 0 : T // 2], in_=rT[run_of_128(0), 0 : T // 2])
 
         nc.scalar.copy(
             wc_bf[:].rearrange("p (c m) i -> p c i m", m=COLUMN_RUN),
@@ -131,18 +155,24 @@ def tile_list_rgg_L_kernel(
         nc.vector.tensor_copy(picked_s[:, J : 2 * J], tab_s[:].bitcast(U8).indirect(dst_list[:]))
 
         move_scales(planes, picked_s[:].bitcast(I32))
-        nc.sync.dma_start(out=state[0][:, J:T], in_=rT[run_of_128(0), J:T])
+        nc.sync.dma_start(out=state[0][:, T // 2 : T], in_=rT[run_of_128(0), T // 2 : T])
         state.append(shared.tile([P, T], F32, name="state1", offset=STATE1_AT))
         state.append(shared.tile([P, T], F32, name="state2", offset=STATE2_AT))
         state.append(shared.tile([P, T], F32, name="state3", offset=STATE3_AT))
         weight_all = shared.tile([P, J], F32, offset=WEIGHTS_AT)
         nc.sync.dma_start(out=state[1][:], in_=rT[run_of_128(1), :])
-        nc.sync.dma_start(out=state[2][:, 0:J], in_=rT[run_of_128(2), 0:J])
-        nc.sync.dma_start(out=weight_rows[WEIGHT_ROW:P, :], in_=wgo[0].rearrange("(c j) -> c j", j=P))
-        nc.sync.dma_start(out=state[2][:, J:T], in_=rT[run_of_128(2), J:T])
+        nc.sync.dma_start(out=state[2][:, 0 : T // 2], in_=rT[run_of_128(2), 0 : T // 2])
+        nc.sync.dma_start(out=weight_rows[WEIGHT_ROW:P, :], in_=wgo[0, 0:HALF].rearrange("(c j) -> c j", j=P))
+        nc.sync.dma_start(out=state[2][:, T // 2 : T], in_=rT[run_of_128(2), T // 2 : T])
         nc.sync.dma_start(out=state[LAST][:], in_=rT[run_of_128(LAST), :])
         for h in reversed(range(HALVES)):
             nc.sync.dma_start(out=weight_all[:, run_of_512(h)], in_=wgo[:, run_of_512(h)])
+
+        def targets(edges):
+            return dst_list[:, edges.start // LIST_ROWS : edges.stop // LIST_ROWS]
+
+        def piece_at(name, kib, width):
+            return shared.tile([P, width], F32, name=name, offset=PIECES_AT + int(KIB * kib))
 
         src_words = held.tile([P, J], U32, align_bytes=64)
         dst_words = [
@@ -150,43 +180,38 @@ def tile_list_rgg_L_kernel(
             shared.tile([P, HALF], U32, name="dst_words1", offset=LATE_WORDS_AT, align_bytes=64),
         ]
         nc.vector.tensor_copy(src_words[:], tab_w[:].bitcast(U32).indirect(src_list[:]))
-        nc.vector.tensor_copy(dst_words[0][:], tab_w[:].bitcast(U32).indirect(dst_list[:, entries(0, HALF)]))
+        nc.vector.tensor_copy(dst_words[0][:], tab_w[:].bitcast(U32).indirect(targets(run_of_512(0))))
         nc.vector.quantize_mx(out=wc_w[:].bitcast(FP8X4), scales=wc_s[:], in_=wc_bf[:].rearrange("p n i -> p (n i)"))
-        nc.vector.tensor_copy(dst_words[1][:], tab_w[:].bitcast(U32).indirect(dst_list[:, entries(HALF, J)]))
+        nc.vector.tensor_copy(dst_words[1][:], tab_w[:].bitcast(U32).indirect(targets(run_of_512(1))))
 
-        def offsets_of(piece):
-            return dst_list[:, entries(piece.start, piece.stop)]
+        def gather_state(b, edges, values):
+            nc.vector.tensor_copy(values, state[b][:].indirect(targets(edges)))
 
-        def placed_at(name, kib, width):
-            return shared.tile([P, width], F32, name=name, offset=PIECES_AT + int(1024 * kib))
-
-        picked = {}
-
-        def pick(b, edges, tile):
-            nc.vector.tensor_copy(tile, state[b][:].indirect(offsets_of(edges)))
-            for s in range(edges.start // P, edges.stop // P):
-                picked[b, s] = tile[:, s * P - edges.start : (s + 1) * P - edges.start]
-
-        picked0 = shared.tile([P, J], F32, offset=CAST_AT)
-        picked1 = held.tile([P, J], F32)
-        picked2 = held.tile([P, HALF], F32)
+        early = [
+            shared.tile([P, J], F32, name="early0", offset=CAST_AT),
+            held.tile([P, J], F32, name="early1"),
+            held.tile([P, HALF], F32, name="early2"),
+        ]
         for h in range(HALVES):
-            pick(0, run_of_512(h), picked0[:, run_of_512(h)])
-        pick(1, slice(0, J), picked1[:])
-        pick(2, run_of_512(0), picked2[:])
+            gather_state(0, run_of_512(h), early[0][:, run_of_512(h)])
+        gather_state(1, slice(0, J), early[1][:])
+        gather_state(2, run_of_512(0), early[2][:])
 
         za_banks = [psum.tile([P, HALF], F32, name="za%d" % i) for i in range(BANKS)]
         ms_banks = [psum.tile([P, HALF], F32, name="ms%d" % i) for i in range(BANKS)]
-
         turned_banks = [psum.tile([P, HALF], F32, name="turned%d" % i) for i in range(BANKS)]
         back_banks = [psum.tile([P, HALF], F32, name="back%d" % i) for i in range(BANKS)]
 
         gated = {}
 
-        def products(b, h, gates, messages):
+        def gate(b, h):
             n, j = run_of_128(b), run_of_512(h)
-            bank = len(gated) % BANKS
-            za, ms = za_banks[bank], ms_banks[bank]
+            za, ms = za_banks[len(gated) % BANKS], ms_banks[len(gated) % BANKS]
+            if (b, h) in FACTORS_AT:
+                factors = piece_at("factors%d%d" % (b, h), FACTORS_AT[b, h], 2 * HALF)
+            else:
+                factors = held.tile([P, 2 * HALF], F32, name="factors%d%d" % (b, h))
+            gates, messages = factors[:, 0:HALF], factors[:, HALF : 2 * HALF]
             dst_w, src_w = dst_words[h][:].bitcast(FP8X4), src_words[:, j].bitcast(FP8X4)
             nc.tensor.matmul_mx(
                 za[:], lhsT=wb_w[:, n].bitcast(FP8X4), lhsT_scale=wb_s.bitcast(U8)[:, n],
@@ -202,43 +227,25 @@ def tile_list_rgg_L_kernel(
             )
             nc.scalar.activation(gates, za[:], SIGMOID)
             nc.scalar.copy(messages, ms[:])
-
-        WEIGHTED_A, SUM2, SUM3, SUM11, SUM21, WEIGHTED20 = 3.5, 9, 13, 20, 27, 31
-        WEIGHTED_B = SUM3 + 0.5
-        factors_at = {(1, 1): WEIGHTED_A - 3.5, (1, 0): WEIGHTED_A + 0.5, (2, 0): WEIGHTED_B + 0.75, (3, 1): WEIGHTED20}
-        gated_at = {
-            (1, 1): SUM2 + 0.5, (1, 0): factors_at[1, 1], (2, 0): SUM2 + 0.5, (2, 1): factors_at[2, 0],
-            (3, 0): SUM21 + 1,
-        }
-
-        def gate(b, h):
-            if (b, h) in factors_at:
-                factors = placed_at("factors%d%d" % (b, h), factors_at[b, h], J)
-            else:
-                factors = held.tile([P, J], F32, name="factors%d%d" % (b, h))
-            products(b, h, factors[:, 0:HALF], factors[:, HALF:J])
-            if (b, h) in gated_at:
-                gated[b, h] = placed_at("gated%d%d" % (b, h), gated_at[b, h], HALF)
+            if (b, h) in GATED_AT:
+                gated[b, h] = piece_at("gated%d%d" % (b, h), GATED_AT[b, h], HALF)
             else:
                 gated[b, h] = held.tile([P, HALF], F32, name="gated%d%d" % (b, h))
-            nc.gpsimd.tensor_tensor(gated[b, h][:], factors[:, 0:HALF], factors[:, HALF:J], MULT)
+            nc.gpsimd.tensor_tensor(gated[b, h][:], gates, messages, MULT)
 
-        def turn_and_add(b, squares, turned):
-            for i, s in enumerate(squares):
-                nc.tensor.matmul(turned[:, run_of_128(i)], picked[b, s], identity[:], start=i == 0, stop=False, is_transpose=True)
-            for i, s in enumerate(squares):
-                nc.tensor.matmul(
-                    turned[:, run_of_128(i)], gated[b, s // SQUARES][:, run_of_128(s % SQUARES)], identity[:],
-                    start=False, stop=i == len(squares) - 1, is_transpose=True,
-                )
+        def add_turned(turned, values, start, stop):
+            nc.tensor.matmul(turned, values, identity[:], start=start, stop=stop, is_transpose=True)
 
-        def turn_pairs(b, squares, turned):
+        def turn_quarter(squares, turned):
             for i, s in enumerate(squares):
-                nc.tensor.matmul(
-                    turned[:, run_of_128(i)], gated[b, s // SQUARES][:, run_of_128(s % SQUARES)], identity[:],
-                    start=True, stop=False, is_transpose=True,
-                )
-                nc.tensor.matmul(turned[:, run_of_128(i)], picked[b, s], identity[:], start=False, stop=True, is_transpose=True)
+                add_turned(turned[:, run_of_128(i)], early[0][:, run_of_128(s)], i == 0, False)
+            for i, s in enumerate(squares):
+                add_turned(turned[:, run_of_128(i)], gated[0, 0][:, run_of_128(s)], False, i == len(squares) - 1)
+
+        def turn_half(b, turned):
+            for s in range(SQUARES):
+                add_turned(turned[:, run_of_128(s)], gated[b, 0][:, run_of_128(s)], True, False)
+                add_turned(turned[:, run_of_128(s)], early[b][:, run_of_128(s)], False, True)
 
         def weigh_and_turn_back(squares, turned, back, weighted, result):
             for i, s in enumerate(squares):
@@ -248,69 +255,70 @@ def tile_list_rgg_L_kernel(
             nc.scalar.copy(result, back[:, 0 : len(squares) * P])
 
         def scatter(window, edges, values):
-            nc.vector.tensor_copy(placed[window][:].indirect(offsets_of(edges)), values)
+            nc.vector.tensor_copy(placed[window][:].indirect(targets(edges)), values)
+
+        def store(window, b):
+            nc.sync.dma_start(out=out[run_of_128(b), :], in_=placed[window][:])
 
         late = {}
 
-        def pick_late(b, q, kib):
-            late[b, q] = placed_at("late%d%d" % (b, q), kib, QUARTER)
-            pick(b, run_of_256(q), late[b, q][:])
+        def gather_late(b, q, kib):
+            late[b, q] = piece_at("late%d%d" % (b, q), kib, QUARTER)
+            gather_state(b, run_of_256(q), late[b, q][:])
 
-        pieces = [held.tile([P, QUARTER], F32, name="result0%d" % q) for q in range(4)]
-        results = [None] + [held.tile([P, J], F32, name="results%d" % b) for b in range(1, ROW_BLOCKS)]
+        def finish_quarters(b, sums_at, finished, lates):
+            sums = {q: piece_at("sum%d%d" % (b, q), sums_at[q], QUARTER) for q in (2, 3)}
+            for q in (2, 3):
+                nc.gpsimd.tensor_tensor(sums[q][:], gated[b, 1][:, run_of_256(q - 2)], early[b][:, run_of_256(q)], ADD)
+            for q in (2, 3):
+                nc.gpsimd.tensor_tensor(finished[q], sums[q][:], weight_all[:, run_of_256(q)], MULT)
+            for q in (2, 3):
+                gather_late(*lates[q])
+                scatter(b, run_of_256(q), finished[q])
 
-        def finish_on_gpsimd(b, residual, kib):
-            summed = placed_at("sum%d1" % b, kib, HALF)
-            for i, values in enumerate(residual):
-                width = HALF // len(residual)
-                part = slice(i * width, (i + 1) * width)
-                nc.gpsimd.tensor_tensor(summed[:, part], gated[b, 1][:, part], values, ADD)
-            nc.gpsimd.tensor_tensor(results[b][:, run_of_512(1)], summed[:], weight_all[:, run_of_512(1)], MULT)
+        quarters = [held.tile([P, QUARTER], F32, name="result0%d" % q)[:] for q in range(4)]
+        results = {b: held.tile([P, J], F32, name="results%d" % b) for b in range(1, ROW_BLOCKS)}
 
         gate(0, 0)
         gate(0, 1)
         nc.tensor.transpose(back_banks[1][:, 0:P], weight_rows[:], identity[:])
         nc.scalar.copy(weight_col[:], back_banks[1][:, WEIGHT_ROW:P])
-        turn_and_add(0, (0, 1), za_banks[0])
-        weigh_and_turn_back((0, 1), za_banks[0], za_banks[1], placed_at("weighted_a", WEIGHTED_A, QUARTER), pieces[0][:])
-        scatter(0, run_of_256(0), pieces[0][:])
-        turn_and_add(0, (2, 3), turned_banks[1])
-        sums = {2: placed_at("sum2", SUM2, QUARTER), 3: placed_at("sum3", SUM3, QUARTER)}
-        for q in (2, 3):
-            nc.gpsimd.tensor_tensor(sums[q][:], gated[0, 1][:, run_of_256(q - 2)], picked0[:, run_of_256(q)], ADD)
-        for q in (2, 3):
-            nc.gpsimd.tensor_tensor(pieces[q][:], sums[q][:], weight_all[:, run_of_256(q)], MULT)
-        for q, kib in ((2, SUM2 - 0.5), (3, SUM3 - 0.75)):
-            pick_late(2, q, kib)
-            scatter(0, run_of_256(q), pieces[q][:])
-        weigh_and_turn_back((2, 3), turned_banks[1], back_banks[1], placed_at("weighted_b", WEIGHTED_B, QUARTER), pieces[1][:])
-        pick_late(LAST, 0, WEIGHTED_B - 0.25)
-        scatter(0, run_of_256(1), pieces[1][:])
-        nc.sync.dma_start(out=out[run_of_128(0), :], in_=placed[0][:])
+        turn_quarter((0, 1), za_banks[0])
+        weigh_and_turn_back((0, 1), za_banks[0], za_banks[1], piece_at("weighted_q0", WEIGHTED_Q0, QUARTER), quarters[0])
+        scatter(0, run_of_256(0), quarters[0])
+        turn_quarter((2, 3), turned_banks[1])
+        finish_quarters(0, {2: SUM_02, 3: SUM_03}, quarters, {2: (2, 2, LATE_22), 3: (2, 3, LATE_23)})
+        weigh_and_turn_back((2, 3), turned_banks[1], back_banks[1], piece_at("weighted_q1", WEIGHTED_Q1, QUARTER), quarters[1])
+        gather_late(LAST, 0, LATE_30)
+        scatter(0, run_of_256(1), quarters[1])
+        store(0, 0)
 
         gate(1, 1)
         gate(1, 0)
-        finish_on_gpsimd(1, [picked1[:, run_of_512(1)]], SUM11)
-        pick_late(LAST, 1, SUM11)
-        scatter(1, run_of_512(1), results[1][:, run_of_512(1)])
-        turn_pairs(1, range(SQUARES), turned_banks[0])
-        weigh_and_turn_back(range(SQUARES), turned_banks[0], back_banks[0], placed_at("weighted10", SUM11 + 1, HALF), results[1][:, run_of_512(0)])
-        pick_late(LAST, 2, SUM11 + 1)
+        finished = {q: results[1][:, run_of_256(q)] for q in (2, 3)}
+        finish_quarters(1, {2: SUM_12, 3: SUM_13}, finished, {2: (LAST, 1, LATE_31), 3: (LAST, 2, LATE_32)})
+        turn_half(1, turned_banks[0])
+        weighted = piece_at("weighted10", WEIGHTED_10, HALF)
+        weigh_and_turn_back(range(SQUARES), turned_banks[0], back_banks[0], weighted, results[1][:, run_of_512(0)])
+        gather_late(LAST, 3, LATE_33)
         scatter(1, run_of_512(0), results[1][:, run_of_512(0)])
-        nc.sync.dma_start(out=out[run_of_128(1), :], in_=placed[1][:])
+        store(1, 1)
 
         gate(2, 0)
         gate(2, 1)
-        turn_pairs(2, range(SQUARES), turned_banks[1])
-        weigh_and_turn_back(range(SQUARES), turned_banks[1], back_banks[1], placed_at("weighted20", WEIGHTED20, HALF), results[2][:, run_of_512(0)])
-        finish_on_gpsimd(2, [late[2, 2][:], late[2, 3][:]], SUM21)
-        pick_late(LAST, 3, SUM21)
+        turn_half(2, turned_banks[1])
+        weighted = piece_at("weighted20", WEIGHTED_20, HALF)
+        weigh_and_turn_back(range(SQUARES), turned_banks[1], back_banks[1], weighted, results[2][:, run_of_512(0)])
+        summed = piece_at("sum21", SUM_21, HALF)
+        for q in (2, 3):
+            nc.gpsimd.tensor_tensor(summed[:, run_of_256(q - 2)], gated[2, 1][:, run_of_256(q - 2)], late[2, q][:], ADD)
+        nc.gpsimd.tensor_tensor(results[2][:, run_of_512(1)], summed[:], weight_all[:, run_of_512(1)], MULT)
         scatter(0, slice(0, J), results[2][:])
-        nc.sync.dma_start(out=out[run_of_128(2), :], in_=placed[0][:])
+        store(0, 2)
 
         for h in range(HALVES):
             gate(LAST, h)
         for q in range(4):
             nc.gpsimd.tensor_tensor(results[LAST][:, run_of_256(q)], gated[LAST, q // 2][:, run_of_256(q % 2)], late[LAST, q][:], ADD)
         nc.vector.tensor_tensor(placed[1][:].indirect(dst_list[:]), results[LAST][:], weight_all[:], MULT)
-        nc.sync.dma_start(out=out[run_of_128(LAST), :], in_=placed[1][:])
+        store(1, LAST)

@@ -53,15 +53,14 @@ WEIGHTED_Q0 = 3.5
 FACTORS_11 = WEIGHTED_Q0 - 3.5
 FACTORS_10 = WEIGHTED_Q0 + 0.5
 SUM_02 = 9
-LATE_22 = SUM_02 - 0.5
+LATE_23 = SUM_02 - 0.5
 GATED_11 = SUM_02 + 0.5
 SUM_03 = 13
-LATE_23 = SUM_03 - 0.75
+LATE_30 = SUM_03 - 0.75
 WEIGHTED_Q1 = SUM_03 + 0.5
-LATE_30 = WEIGHTED_Q1 - 0.25
+LATE_31 = WEIGHTED_Q1 - 0.25
 FACTORS_20 = WEIGHTED_Q1 + 0.75
 SUM_12 = 19
-LATE_31 = SUM_12
 SUM_13 = 20.5
 LATE_32 = SUM_13 - 0.5
 WEIGHTED_10 = SUM_13 + 0.5
@@ -190,12 +189,12 @@ def tile_list_rgg_L_kernel(
         early = [
             shared.tile([P, J], F32, name="early0", offset=CAST_AT),
             held.tile([P, J], F32, name="early1"),
-            held.tile([P, HALF], F32, name="early2"),
+            held.tile([P, J - QUARTER], F32, name="early2"),
         ]
         for h in range(HALVES):
             gather_state(0, run_of_512(h), early[0][:, run_of_512(h)])
         gather_state(1, slice(0, J), early[1][:])
-        gather_state(2, run_of_512(0), early[2][:])
+        gather_state(2, slice(0, J - QUARTER), early[2][:])
 
         za_banks = [psum.tile([P, HALF], F32, name="za%d" % i) for i in range(BANKS)]
         ms_banks = [psum.tile([P, HALF], F32, name="ms%d" % i) for i in range(BANKS)]
@@ -273,7 +272,8 @@ def tile_list_rgg_L_kernel(
             for q in (2, 3):
                 nc.gpsimd.tensor_tensor(finished[q], sums[q][:], weight_all[:, run_of_256(q)], MULT)
             for q in (2, 3):
-                gather_late(*lates[q])
+                if q in lates:
+                    gather_late(*lates[q])
                 scatter(b, run_of_256(q), finished[q])
 
         quarters = [held.tile([P, QUARTER], F32, name="result0%d" % q)[:] for q in range(4)]
@@ -287,16 +287,16 @@ def tile_list_rgg_L_kernel(
         weigh_and_turn_back((0, 1), za_banks[0], za_banks[1], piece_at("weighted_q0", WEIGHTED_Q0, QUARTER), quarters[0])
         scatter(0, run_of_256(0), quarters[0])
         turn_quarter((2, 3), turned_banks[1])
-        finish_quarters(0, {2: SUM_02, 3: SUM_03}, quarters, {2: (2, 2, LATE_22), 3: (2, 3, LATE_23)})
+        finish_quarters(0, {2: SUM_02, 3: SUM_03}, quarters, {2: (2, 3, LATE_23), 3: (LAST, 0, LATE_30)})
         weigh_and_turn_back((2, 3), turned_banks[1], back_banks[1], piece_at("weighted_q1", WEIGHTED_Q1, QUARTER), quarters[1])
-        gather_late(LAST, 0, LATE_30)
+        gather_late(LAST, 1, LATE_31)
         scatter(0, run_of_256(1), quarters[1])
         store(0, 0)
 
         gate(1, 1)
         gate(1, 0)
         finished = {q: results[1][:, run_of_256(q)] for q in (2, 3)}
-        finish_quarters(1, {2: SUM_12, 3: SUM_13}, finished, {2: (LAST, 1, LATE_31), 3: (LAST, 2, LATE_32)})
+        finish_quarters(1, {2: SUM_12, 3: SUM_13}, finished, {3: (LAST, 2, LATE_32)})
         turn_half(1, turned_banks[0])
         weighted = piece_at("weighted10", WEIGHTED_10, HALF)
         weigh_and_turn_back(range(SQUARES), turned_banks[0], back_banks[0], weighted, results[1][:, run_of_512(0)])
@@ -310,8 +310,8 @@ def tile_list_rgg_L_kernel(
         weighted = piece_at("weighted20", WEIGHTED_20, HALF)
         weigh_and_turn_back(range(SQUARES), turned_banks[1], back_banks[1], weighted, results[2][:, run_of_512(0)])
         summed = piece_at("sum21", SUM_21, HALF)
-        for q in (2, 3):
-            nc.gpsimd.tensor_tensor(summed[:, run_of_256(q - 2)], gated[2, 1][:, run_of_256(q - 2)], late[2, q][:], ADD)
+        for q, values in ((2, early[2][:, run_of_256(2)]), (3, late[2, 3][:])):
+            nc.gpsimd.tensor_tensor(summed[:, run_of_256(q - 2)], gated[2, 1][:, run_of_256(q - 2)], values, ADD)
         nc.gpsimd.tensor_tensor(results[2][:, run_of_512(1)], summed[:], weight_all[:, run_of_512(1)], MULT)
         scatter(0, slice(0, J), results[2][:])
         store(0, 2)

@@ -36,13 +36,17 @@ WINDOWS = 2
 BANKS = 2
 STAGE = P - SCALE_ROWS
 WEIGHT_ROW = P - SQUARES
+FIRST_COLUMNS = 2 * P
+AHEAD = 3 * T // 4
 KIB = 1024
 
 STATE1_AT = 0
 STATE2_AT = STATE1_AT + 4 * T
 TABLE_AT = STATE2_AT - T // 2
-PICKED_AT = STATE2_AT + 4 * T
-STATE3_AT = PICKED_AT + 4 * P
+WB_REST_AT = STATE2_AT + 4 * T
+WA_REST_AT = WB_REST_AT + 4 * (N - FIRST_COLUMNS)
+PICKED_AT = WA_REST_AT - 2 * P
+STATE3_AT = WA_REST_AT + 4 * (N - FIRST_COLUMNS)
 RAW_AT = STATE3_AT + 4 * T
 WEIGHTS_AT = RAW_AT
 LATE_WORDS_AT = RAW_AT + 4 * J
@@ -53,14 +57,15 @@ WEIGHTED_Q0 = 3.5
 FACTORS_11 = WEIGHTED_Q0 - 3.5
 FACTORS_10 = WEIGHTED_Q0 + 0.5
 SUM_02 = 9
-LATE_23 = SUM_02 - 0.5
+LATE_22 = SUM_02 - 0.5
 GATED_11 = SUM_02 + 0.5
 SUM_03 = 13
-LATE_30 = SUM_03 - 0.75
+LATE_23 = SUM_03 - 0.75
 WEIGHTED_Q1 = SUM_03 + 0.5
-LATE_31 = WEIGHTED_Q1 - 0.25
+LATE_30 = WEIGHTED_Q1 - 0.25
 FACTORS_20 = WEIGHTED_Q1 + 0.75
 SUM_12 = 19
+LATE_31 = SUM_12 - 0.5
 SUM_13 = 20.5
 LATE_32 = SUM_13 - 0.5
 WEIGHTED_10 = SUM_13 + 0.5
@@ -106,8 +111,9 @@ def tile_list_rgg_L_kernel(
         dst_list = held.tile([P, J // LIST_ROWS], U16)
         tab_s = shared.tile([P, T // PACK], I32, offset=TABLE_AT, align_bytes=64)
         tab_w = held.tile([P, T], I32, align_bytes=64)
-        wa_w = held.tile([P, N], I32, align_bytes=64)
-        wb_w = held.tile([P, N], I32, align_bytes=64)
+        wa_first = held.tile([P, FIRST_COLUMNS], I32, align_bytes=64)
+        wb_first = held.tile([P, FIRST_COLUMNS], I32, align_bytes=64)
+        wa_w, wb_w = ([first[:, run_of_128(i)] for i in range(FIRST_COLUMNS // P)] for first in (wa_first, wb_first))
         wc_raw = shared.tile([P, PACK, N], F32, offset=RAW_AT, align_bytes=64)
         wc_bf = shared.tile([P, N, PACK], BF16, offset=CAST_AT, align_bytes=64)
         wc_w = held.tile([P, N], U32, align_bytes=64)
@@ -141,9 +147,9 @@ def tile_list_rgg_L_kernel(
         nc.sync.dma_start(out=tab_w[:], in_=words_of(tab_words))
         nc.sync.dma_start(out=wc_raw[:], in_=wc.rearrange("(p i) n -> p i n", i=PACK))
         move_scales(w_s, staged[:])
-        nc.sync.dma_start(out=wa_w[:], in_=words_of(wa_words))
-        nc.sync.dma_start(out=wb_w[:], in_=words_of(wb_words))
-        nc.sync.dma_start(out=state[0][:, 0 : T // 2], in_=rT[run_of_128(0), 0 : T // 2])
+        nc.sync.dma_start(out=wa_first[:], in_=words_of(wa_words)[:, 0:FIRST_COLUMNS])
+        nc.sync.dma_start(out=wb_first[:], in_=words_of(wb_words)[:, 0:FIRST_COLUMNS])
+        nc.sync.dma_start(out=state[0][:, 0:AHEAD], in_=rT[run_of_128(0), 0:AHEAD])
 
         nc.scalar.copy(
             wc_bf[:].rearrange("p (c m) i -> p c i m", m=COLUMN_RUN),
@@ -154,7 +160,7 @@ def tile_list_rgg_L_kernel(
         nc.vector.tensor_copy(picked_s[:, J : 2 * J], tab_s[:].bitcast(U8).indirect(dst_list[:]))
 
         move_scales(planes, picked_s[:].bitcast(I32))
-        nc.sync.dma_start(out=state[0][:, T // 2 : T], in_=rT[run_of_128(0), T // 2 : T])
+        nc.sync.dma_start(out=state[0][:, AHEAD:T], in_=rT[run_of_128(0), AHEAD:T])
         state.append(shared.tile([P, T], F32, name="state1", offset=STATE1_AT))
         state.append(shared.tile([P, T], F32, name="state2", offset=STATE2_AT))
         state.append(shared.tile([P, T], F32, name="state3", offset=STATE3_AT))
@@ -164,8 +170,12 @@ def tile_list_rgg_L_kernel(
         nc.sync.dma_start(out=weight_rows[WEIGHT_ROW:P, :], in_=wgo[0, 0:HALF].rearrange("(c j) -> c j", j=P))
         nc.sync.dma_start(out=state[2][:, T // 2 : T], in_=rT[run_of_128(2), T // 2 : T])
         nc.sync.dma_start(out=state[LAST][:], in_=rT[run_of_128(LAST), :])
-        for h in reversed(range(HALVES)):
-            nc.sync.dma_start(out=weight_all[:, run_of_512(h)], in_=wgo[:, run_of_512(h)])
+        nc.sync.dma_start(out=weight_all[:, run_of_512(1)], in_=wgo[:, run_of_512(1)])
+        for name, blocks, packed, at in (("wb_rest", wb_w, wb_words, WB_REST_AT), ("wa_rest", wa_w, wa_words, WA_REST_AT)):
+            rest = shared.tile([P, N - FIRST_COLUMNS], I32, name=name, offset=at, align_bytes=64)
+            nc.sync.dma_start(out=rest[:], in_=words_of(packed)[:, FIRST_COLUMNS:N])
+            blocks.extend(rest[:, run_of_128(i)] for i in range((N - FIRST_COLUMNS) // P))
+        nc.sync.dma_start(out=weight_all[:, run_of_512(0)], in_=wgo[:, run_of_512(0)])
 
         def targets(edges):
             return dst_list[:, edges.start // LIST_ROWS : edges.stop // LIST_ROWS]
@@ -189,12 +199,12 @@ def tile_list_rgg_L_kernel(
         early = [
             shared.tile([P, J], F32, name="early0", offset=CAST_AT),
             held.tile([P, J], F32, name="early1"),
-            held.tile([P, J - QUARTER], F32, name="early2"),
+            held.tile([P, HALF], F32, name="early2"),
         ]
         for h in range(HALVES):
             gather_state(0, run_of_512(h), early[0][:, run_of_512(h)])
         gather_state(1, slice(0, J), early[1][:])
-        gather_state(2, slice(0, J - QUARTER), early[2][:])
+        gather_state(2, run_of_512(0), early[2][:])
 
         za_banks = [psum.tile([P, HALF], F32, name="za%d" % i) for i in range(BANKS)]
         ms_banks = [psum.tile([P, HALF], F32, name="ms%d" % i) for i in range(BANKS)]
@@ -213,11 +223,11 @@ def tile_list_rgg_L_kernel(
             gates, messages = factors[:, 0:HALF], factors[:, HALF : 2 * HALF]
             dst_w, src_w = dst_words[h][:].bitcast(FP8X4), src_words[:, j].bitcast(FP8X4)
             nc.tensor.matmul_mx(
-                za[:], lhsT=wb_w[:, n].bitcast(FP8X4), lhsT_scale=wb_s.bitcast(U8)[:, n],
+                za[:], lhsT=wb_w[b].bitcast(FP8X4), lhsT_scale=wb_s.bitcast(U8)[:, n],
                 rhs=src_w, rhs_scale=src_s[:, j], start=True, stop=False,
             )
             nc.tensor.matmul_mx(
-                za[:], lhsT=wa_w[:, n].bitcast(FP8X4), lhsT_scale=wa_s.bitcast(U8)[:, n],
+                za[:], lhsT=wa_w[b].bitcast(FP8X4), lhsT_scale=wa_s.bitcast(U8)[:, n],
                 rhs=dst_w, rhs_scale=dst_s[:, j], start=False, stop=True,
             )
             nc.tensor.matmul_mx(
@@ -287,16 +297,16 @@ def tile_list_rgg_L_kernel(
         weigh_and_turn_back((0, 1), za_banks[0], za_banks[1], piece_at("weighted_q0", WEIGHTED_Q0, QUARTER), quarters[0])
         scatter(0, run_of_256(0), quarters[0])
         turn_quarter((2, 3), turned_banks[1])
-        finish_quarters(0, {2: SUM_02, 3: SUM_03}, quarters, {2: (2, 3, LATE_23), 3: (LAST, 0, LATE_30)})
+        finish_quarters(0, {2: SUM_02, 3: SUM_03}, quarters, {2: (2, 2, LATE_22), 3: (2, 3, LATE_23)})
         weigh_and_turn_back((2, 3), turned_banks[1], back_banks[1], piece_at("weighted_q1", WEIGHTED_Q1, QUARTER), quarters[1])
-        gather_late(LAST, 1, LATE_31)
+        gather_late(LAST, 0, LATE_30)
         scatter(0, run_of_256(1), quarters[1])
         store(0, 0)
 
         gate(1, 1)
         gate(1, 0)
         finished = {q: results[1][:, run_of_256(q)] for q in (2, 3)}
-        finish_quarters(1, {2: SUM_12, 3: SUM_13}, finished, {3: (LAST, 2, LATE_32)})
+        finish_quarters(1, {2: SUM_12, 3: SUM_13}, finished, {2: (LAST, 1, LATE_31), 3: (LAST, 2, LATE_32)})
         turn_half(1, turned_banks[0])
         weighted = piece_at("weighted10", WEIGHTED_10, HALF)
         weigh_and_turn_back(range(SQUARES), turned_banks[0], back_banks[0], weighted, results[1][:, run_of_512(0)])
@@ -310,8 +320,8 @@ def tile_list_rgg_L_kernel(
         weighted = piece_at("weighted20", WEIGHTED_20, HALF)
         weigh_and_turn_back(range(SQUARES), turned_banks[1], back_banks[1], weighted, results[2][:, run_of_512(0)])
         summed = piece_at("sum21", SUM_21, HALF)
-        for q, values in ((2, early[2][:, run_of_256(2)]), (3, late[2, 3][:])):
-            nc.gpsimd.tensor_tensor(summed[:, run_of_256(q - 2)], gated[2, 1][:, run_of_256(q - 2)], values, ADD)
+        for q in (2, 3):
+            nc.gpsimd.tensor_tensor(summed[:, run_of_256(q - 2)], gated[2, 1][:, run_of_256(q - 2)], late[2, q][:], ADD)
         nc.gpsimd.tensor_tensor(results[2][:, run_of_512(1)], summed[:], weight_all[:, run_of_512(1)], MULT)
         scatter(0, slice(0, J), results[2][:])
         store(0, 2)

@@ -62,14 +62,17 @@ GATED_11 = SUM_02 + 0.5
 SUM_03 = 13
 LATE_23 = SUM_03 - 0.75
 WEIGHTED_Q1 = SUM_03 + 0.5
-LATE_30 = WEIGHTED_Q1 - 0.25
-FACTORS_20 = WEIGHTED_Q1 + 0.75
+WEIGHTED_Q1_LAST = 37
+LATE_30 = WEIGHTED_Q1_LAST - 0.75
+FACTORS_20 = WEIGHTED_Q1_LAST + 0.25
 SUM_12 = 19
 LATE_31 = SUM_12 - 0.5
-SUM_13 = 20.5
+SUM_13 = 21.5
 LATE_32 = SUM_13 - 0.5
 WEIGHTED_10 = SUM_13 + 0.5
-LATE_33 = WEIGHTED_10
+LATE_33 = WEIGHTED_10 + 1.5
+RESULTS_0 = {0: LATE_23 - 0.75, 2: LATE_30 - 0.75, 3: LATE_31 - 0.75, 1: LATE_32 - 0.75}
+RESULT_12 = LATE_33 + 0.75
 SUM_21 = 27
 GATED_30 = SUM_21 + 1
 GATED_31 = SUM_21 - 1
@@ -258,9 +261,9 @@ def tile_list_rgg_L_kernel(
 
         def weigh_and_turn_back(squares, turned, back, weighted, result):
             for i, s in enumerate(squares):
-                nc.scalar.activation(weighted[:, run_of_128(i)], turned[:, run_of_128(i)], COPY, scale=weight_col[:, s : s + 1])
+                nc.scalar.activation(weighted[i], turned[:, run_of_128(i)], COPY, scale=weight_col[:, s : s + 1])
             for i in range(len(squares)):
-                nc.tensor.transpose(back[:, run_of_128(i)], weighted[:, run_of_128(i)], identity[:])
+                nc.tensor.transpose(back[:, run_of_128(i)], weighted[i], identity[:])
             nc.scalar.copy(result, back[:, 0 : len(squares) * P])
 
         def scatter(window, edges, values):
@@ -270,6 +273,10 @@ def tile_list_rgg_L_kernel(
             nc.sync.dma_start(out=out[run_of_128(b), :], in_=placed[window][:])
 
         late = {}
+
+        def squares_at(name, kib, count):
+            tile = piece_at(name, kib, count * P)
+            return [tile[:, run_of_128(i)] for i in range(count)]
 
         def gather_late(b, q, kib):
             late[b, q] = piece_at("late%d%d" % (b, q), kib, QUARTER)
@@ -286,7 +293,7 @@ def tile_list_rgg_L_kernel(
                     gather_late(*lates[q])
                 scatter(b, run_of_256(q), finished[q])
 
-        quarters = [held.tile([P, QUARTER], F32, name="result0%d" % q)[:] for q in range(4)]
+        quarters = [piece_at("result0%d" % q, RESULTS_0[q], QUARTER)[:] for q in range(4)]
         results = {b: held.tile([P, J], F32, name="results%d" % b) for b in range(1, ROW_BLOCKS)}
 
         gate(0, 0)
@@ -294,21 +301,22 @@ def tile_list_rgg_L_kernel(
         nc.tensor.transpose(back_banks[1][:, 0:P], weight_rows[:], identity[:])
         nc.scalar.copy(weight_col[:], back_banks[1][:, WEIGHT_ROW:P])
         turn_quarter((0, 1), za_banks[0])
-        weigh_and_turn_back((0, 1), za_banks[0], za_banks[1], piece_at("weighted_q0", WEIGHTED_Q0, QUARTER), quarters[0])
+        weigh_and_turn_back((0, 1), za_banks[0], za_banks[1], squares_at("weighted_q0", WEIGHTED_Q0, 2), quarters[0])
         scatter(0, run_of_256(0), quarters[0])
         turn_quarter((2, 3), turned_banks[1])
         finish_quarters(0, {2: SUM_02, 3: SUM_03}, quarters, {2: (2, 2, LATE_22), 3: (2, 3, LATE_23)})
-        weigh_and_turn_back((2, 3), turned_banks[1], back_banks[1], piece_at("weighted_q1", WEIGHTED_Q1, QUARTER), quarters[1])
+        weighted = squares_at("weighted_q1", WEIGHTED_Q1, 1) + squares_at("weighted_q1_last", WEIGHTED_Q1_LAST, 1)
+        weigh_and_turn_back((2, 3), turned_banks[1], back_banks[1], weighted, quarters[1])
         gather_late(LAST, 0, LATE_30)
         scatter(0, run_of_256(1), quarters[1])
         store(0, 0)
 
         gate(1, 1)
         gate(1, 0)
-        finished = {q: results[1][:, run_of_256(q)] for q in (2, 3)}
+        finished = {2: piece_at("result12", RESULT_12, QUARTER)[:], 3: results[1][:, run_of_256(3)]}
         finish_quarters(1, {2: SUM_12, 3: SUM_13}, finished, {2: (LAST, 1, LATE_31), 3: (LAST, 2, LATE_32)})
         turn_half(1, turned_banks[0])
-        weighted = piece_at("weighted10", WEIGHTED_10, HALF)
+        weighted = squares_at("weighted10", WEIGHTED_10, SQUARES)
         weigh_and_turn_back(range(SQUARES), turned_banks[0], back_banks[0], weighted, results[1][:, run_of_512(0)])
         gather_late(LAST, 3, LATE_33)
         scatter(1, run_of_512(0), results[1][:, run_of_512(0)])
@@ -317,7 +325,7 @@ def tile_list_rgg_L_kernel(
         gate(2, 0)
         gate(2, 1)
         turn_half(2, turned_banks[1])
-        weighted = piece_at("weighted20", WEIGHTED_20, HALF)
+        weighted = squares_at("weighted20", WEIGHTED_20, SQUARES)
         weigh_and_turn_back(range(SQUARES), turned_banks[1], back_banks[1], weighted, results[2][:, run_of_512(0)])
         summed = piece_at("sum21", SUM_21, HALF)
         for q in (2, 3):

@@ -26,62 +26,34 @@ QUADRANT = 32
 GROUP_ROWS = QUADRANT * PACK // MX_BLOCK
 COLUMN_RUN = 4
 LIST_ROWS = 16
-ROW_BLOCKS = N // P
-LAST = ROW_BLOCKS - 1
-HALF = 512
-HALVES = J // HALF
+HALF = J // 2
 QUARTER = J // 4
-SQUARES = HALF // P
-WINDOWS = 2
-BANKS = 2
 STAGE = P - SCALE_ROWS
-WEIGHT_ROW = P - SQUARES
-FIRST_COLUMNS = 2 * P
-AHEAD = 3 * T // 4
-KIB = 1024
+TURNED_SQUARES = 4
+WEIGHT_ROW = P - TURNED_SQUARES
+PAIR = 2 * P
+LAP = 64
+UNITS = [(0, 0), (1, 0), (0, 1), (1, 1), (2, 0), (3, 0), (2, 1), (3, 1)]
+LAST = len(UNITS) - 1
+WINDOW_OF = {0: 0, 1: 1, 2: 2, 3: 0}
+RING = 6
 
-STATE1_AT = 0
-STATE2_AT = STATE1_AT + 4 * T
-TABLE_AT = STATE2_AT - T // 2
-WB_REST_AT = STATE2_AT + 4 * T
-WA_REST_AT = WB_REST_AT + 4 * (N - FIRST_COLUMNS)
-PICKED_AT = WA_REST_AT - 2 * P
-STATE3_AT = WA_REST_AT + 4 * (N - FIRST_COLUMNS)
-RAW_AT = STATE3_AT + 4 * T
-WEIGHTS_AT = RAW_AT
-LATE_WORDS_AT = RAW_AT + 4 * J
-CAST_AT = RAW_AT + 4 * PACK * N
-PIECES_AT = CAST_AT + 4 * J
+STATE2_AT = 0
+TABLE_AT = STATE2_AT + 4 * T - 64
+WEIGHTS0_AT = TABLE_AT + 64
+WEIGHTS1_AT = TABLE_AT + T - 64
+RAW1_AT = WEIGHTS1_AT + 4 * HALF
+WA1_AT = RAW1_AT
+PICKED1_AT = RAW1_AT + 4 * PACK * PAIR - 64
+WB1_AT = PICKED1_AT + 128 - 4 * PAIR
+STATE3_AT = PICKED1_AT + HALF - 64
+RAW_LATE_AT = STATE3_AT + 4 * T
+SRC1_AT = RAW_LATE_AT
+GATED0_AT = RAW_LATE_AT + 4 * PACK * PAIR
+ROWS_AT = GATED0_AT + 4 * QUARTER - 256
+DST1_AT = GATED0_AT + 4 * QUARTER
 
-WEIGHTED_Q0 = 3.5
-FACTORS_11 = WEIGHTED_Q0 - 3.5
-FACTORS_10 = WEIGHTED_Q0 + 0.5
-SUM_02 = 9
-LATE_22 = SUM_02 - 0.5
-GATED_11 = SUM_02 + 0.5
-SUM_03 = 13
-LATE_23 = SUM_03 - 0.75
-WEIGHTED_Q1 = SUM_03 + 0.5
-WEIGHTED_Q1_LAST = 37
-LATE_30 = WEIGHTED_Q1_LAST - 0.75
-FACTORS_20 = WEIGHTED_Q1_LAST + 0.25
-SUM_12 = 19
-LATE_31 = SUM_12 - 0.5
-SUM_13 = 21.5
-LATE_32 = SUM_13 - 0.5
-WEIGHTED_10 = SUM_13 + 0.5
-LATE_33 = WEIGHTED_10 + 1.5
-RESULTS_0 = {0: LATE_23 - 0.75, 2: LATE_30 - 0.75, 3: LATE_31 - 0.75, 1: LATE_32 - 0.75}
-RESULT_12 = LATE_33 + 0.75
-SUM_21 = 27
-GATED_30 = SUM_21 + 1
-GATED_31 = SUM_21 - 1
-WEIGHTED_20 = 31
-FACTORS_31 = WEIGHTED_20
-FACTORS_AT = {(1, 1): FACTORS_11, (1, 0): FACTORS_10, (2, 0): FACTORS_20, (LAST, 1): FACTORS_31}
-GATED_AT = {
-    (1, 1): GATED_11, (1, 0): FACTORS_11, (2, 0): GATED_11, (2, 1): FACTORS_20, (LAST, 0): GATED_30, (LAST, 1): GATED_31,
-}
+STRETCH = HALF - LAP + QUARTER - LAP + QUARTER
 
 
 def tile_list_rgg_L_kernel(
@@ -96,14 +68,8 @@ def tile_list_rgg_L_kernel(
         for r in range(GROUP_ROWS):
             nc.sync.dma_start(out=plane[r:P:QUADRANT, :], in_=rows[STAGE + r : P : GROUP_ROWS, :])
 
-    def run_of_128(i):
-        return slice(i * P, (i + 1) * P)
-
-    def run_of_256(i):
-        return slice(i * QUARTER, (i + 1) * QUARTER)
-
-    def run_of_512(i):
-        return slice(i * HALF, (i + 1) * HALF)
+    def run(i, width):
+        return slice(i * width, (i + 1) * width)
 
     with ExitStack() as ctx:
         held = ctx.enter_context(tc.tile_pool(name="held", bufs=1))
@@ -114,33 +80,64 @@ def tile_list_rgg_L_kernel(
         dst_list = held.tile([P, J // LIST_ROWS], U16)
         tab_s = shared.tile([P, T // PACK], I32, offset=TABLE_AT, align_bytes=64)
         tab_w = held.tile([P, T], I32, align_bytes=64)
-        wa_first = held.tile([P, FIRST_COLUMNS], I32, align_bytes=64)
-        wb_first = held.tile([P, FIRST_COLUMNS], I32, align_bytes=64)
-        wa_w, wb_w = ([first[:, run_of_128(i)] for i in range(FIRST_COLUMNS // P)] for first in (wa_first, wb_first))
-        wc_raw = shared.tile([P, PACK, N], F32, offset=RAW_AT, align_bytes=64)
-        wc_bf = shared.tile([P, N, PACK], BF16, offset=CAST_AT, align_bytes=64)
-        wc_w = held.tile([P, N], U32, align_bytes=64)
-        wc_s = held.tile([P, N], U8, align_bytes=64)
-        picked_s = shared.tile([P, 2 * J], U8, offset=PICKED_AT, align_bytes=64)
         staged = held.tile([P, 2 * N // PACK], I32, align_bytes=64)
-        planes = held.tile([P, 2 * J // PACK], I32, align_bytes=64)
         w_s = held.tile([P, 2 * N // PACK], I32, align_bytes=64)
-        src_s, dst_s = planes[:].bitcast(U8)[:, 0:J], planes[:].bitcast(U8)[:, J : 2 * J]
+        planes0 = held.tile([P, (J + HALF) // PACK], I32, align_bytes=64)
+        planes1 = held.tile([P, HALF // PACK], I32, align_bytes=64)
         wa_at, wb_at = 0, N // PACK
-        wa_s, wb_s = w_s[:, wa_at:wb_at], w_s[:, wb_at : wb_at + N // PACK]
-        placed = [held.tile([P, T], F32, name="placed%d" % i) for i in range(WINDOWS)]
-        weight_col = held.tile([P, SQUARES], F32)
-        weight_rows = held.tile([P, P], F32)
+        wa_s, wb_s = w_s[:].bitcast(U8)[:, 0:N], w_s[:].bitcast(U8)[:, N : 2 * N]
+        src_s = planes0[:].bitcast(U8)[:, 0:J]
+        dst_s = [planes0[:].bitcast(U8)[:, J : J + HALF], planes1[:].bitcast(U8)]
+        placed = [held.tile([P, T], F32, name="placed%d" % i) for i in range(3)]
+        weight_col = held.tile([P, TURNED_SQUARES], F32)
+        weight_rows = shared.tile([P, P], F32, offset=ROWS_AT, align_bytes=64)
         identity = held.tile([P, P], F32)
-        state = [held.tile([P, T], F32, name="state0")]
+        state = [held.tile([P, T], F32, name="state%d" % b) for b in range(2)]
+        wa_w = [held.tile([P, PAIR], I32, name="wa0", align_bytes=64)]
+        wb_w = [held.tile([P, PAIR], I32, name="wb0", align_bytes=64)]
+        wc_raw = [
+            shared.tile([P, PACK, PAIR], F32, name="wc_raw0", offset=RAW1_AT, align_bytes=64),
+            shared.tile([P, PACK, PAIR], F32, name="wc_raw1", offset=RAW_LATE_AT, align_bytes=64),
+        ]
+        wc_bf = [held.tile([P, PAIR, PACK], BF16, name="wc_bf%d" % i, align_bytes=64) for i in range(2)]
+        wc_w = [held.tile([P, PAIR], U32, name="wc_w%d" % i, align_bytes=64) for i in range(2)]
+        wc_s = [held.tile([P, PAIR], U8, name="wc_s%d" % i, align_bytes=64) for i in range(2)]
+        banks = [psum.tile([P, HALF], F32, name="bank%d" % i) for i in range(8)]
+        early = [held.tile([P, HALF], F32, name="early%d" % i) for i in range(2)]
+        factors = [held.tile([P, 2 * HALF], F32, name="factors%d" % i) for i in range(2)]
+        work = held.tile([P, LAST * STRETCH], F32)
+        turned = held.tile([P, LAST * QUARTER], F32)
+        merged = held.tile([P, HALF], F32)
+        tail = held.tile([P, HALF], F32)
 
+        def entries(offsets, edges):
+            return offsets[:, edges.start // LIST_ROWS : edges.stop // LIST_ROWS]
+
+        def load_wc(i):
+            nc.sync.dma_start(out=wc_raw[i][:], in_=wc[:, run(i, PAIR)].rearrange("(p i) n -> p i n", i=PACK))
+
+        def cast_wc(i):
+            nc.scalar.copy(
+                wc_bf[i][:].rearrange("p (c m) i -> p c i m", m=COLUMN_RUN),
+                wc_raw[i][:].rearrange("p i (c m) -> p c i m", m=COLUMN_RUN),
+            )
+
+        def quantise_wc(i):
+            nc.vector.quantize_mx(
+                out=wc_w[i][:].bitcast(FP8X4), scales=wc_s[i][:], in_=wc_bf[i][:].rearrange("p n i -> p (n i)")
+            )
+
+        h0, h1 = run(0, HALF), run(1, HALF)
+
+        nc.vector.memset(placed[2][:], 0.0)
         nc.gpsimd.memset(tab_s[0:STAGE, :], 0)
         nc.gpsimd.memset(w_s[:], 0)
-        nc.gpsimd.memset(planes[:], 0)
-        for window in placed:
-            nc.gpsimd.memset(window[:], 0.0)
+        nc.gpsimd.memset(planes0[:], 0)
+        nc.gpsimd.memset(planes1[:], 0)
         nc.gpsimd.memset(weight_rows[0:WEIGHT_ROW, :], 0.0)
         make_identity(nc, identity[:])
+        for window in placed[0:2]:
+            nc.gpsimd.memset(window[:], 0.0)
 
         nc.sync.dma_start(out=tab_s[STAGE:P, :], in_=tab_scales[0].bitcast(I32))
         nc.sync.dma_start(src_list[:], offs)
@@ -148,195 +145,161 @@ def tile_list_rgg_L_kernel(
         nc.sync.dma_start(out=staged[STAGE:P, wa_at:wb_at], in_=wa_scales[0].bitcast(I32))
         nc.sync.dma_start(out=staged[STAGE:P, wb_at : wb_at + N // PACK], in_=wb_scales[0].bitcast(I32))
         nc.sync.dma_start(out=tab_w[:], in_=words_of(tab_words))
-        nc.sync.dma_start(out=wc_raw[:], in_=wc.rearrange("(p i) n -> p i n", i=PACK))
+        load_wc(0)
+        nc.sync.dma_start(out=wa_w[0][:], in_=words_of(wa_words)[:, 0:PAIR])
         move_scales(w_s, staged[:])
-        nc.sync.dma_start(out=wa_first[:], in_=words_of(wa_words)[:, 0:FIRST_COLUMNS])
-        nc.sync.dma_start(out=wb_first[:], in_=words_of(wb_words)[:, 0:FIRST_COLUMNS])
-        nc.sync.dma_start(out=state[0][:, 0:AHEAD], in_=rT[run_of_128(0), 0:AHEAD])
+        load_wc(1)
+        nc.sync.dma_start(out=state[0][:, 0 : T // 2], in_=rT[run(0, P), 0 : T // 2])
+        nc.sync.dma_start(out=wb_w[0][:], in_=words_of(wb_words)[:, 0:PAIR])
 
-        nc.scalar.copy(
-            wc_bf[:].rearrange("p (c m) i -> p c i m", m=COLUMN_RUN),
-            wc_raw[:].rearrange("p i (c m) -> p c i m", m=COLUMN_RUN),
+        picked0 = held.tile([P, J + HALF], U8, align_bytes=64)
+        nc.vector.tensor_copy(picked0[:, 0:J], tab_s[:].bitcast(U8).indirect(src_list[:]))
+        nc.vector.tensor_copy(picked0[:, J : J + HALF], tab_s[:].bitcast(U8).indirect(entries(dst_list, h0)))
+        move_scales(planes0, picked0[:].bitcast(I32))
+        nc.sync.dma_start(out=state[0][:, T // 2 : T], in_=rT[run(0, P), T // 2 : T])
+        nc.sync.dma_start(
+            out=weight_rows[WEIGHT_ROW:P, :], in_=wgo[0, :].rearrange("(h q c j) -> h q c j", h=2, q=2, j=P)[:, 1]
         )
+        nc.sync.dma_start(out=state[1][:], in_=rT[run(1, P), :])
 
-        nc.vector.tensor_copy(picked_s[:, 0:J], tab_s[:].bitcast(U8).indirect(src_list[:]))
-        nc.vector.tensor_copy(picked_s[:, J : 2 * J], tab_s[:].bitcast(U8).indirect(dst_list[:]))
+        def gather_words(words, offsets, h):
+            nc.vector.tensor_copy(words[:], tab_w[:].bitcast(U32).indirect(entries(offsets, run(h, HALF))))
 
-        move_scales(planes, picked_s[:].bitcast(I32))
-        nc.sync.dma_start(out=state[0][:, AHEAD:T], in_=rT[run_of_128(0), AHEAD:T])
-        state.append(shared.tile([P, T], F32, name="state1", offset=STATE1_AT))
+        src_words = [held.tile([P, HALF], U32, name="src_words0", align_bytes=64)]
+        dst_words = [held.tile([P, HALF], U32, name="dst_words0", align_bytes=64)]
+        gather_words(src_words[0], src_list, 0)
+        gather_words(dst_words[0], dst_list, 0)
+        for i in range(2):
+            cast_wc(i)
+        quantise_wc(0)
+
+        picked1 = shared.tile([P, HALF], U8, offset=PICKED1_AT, align_bytes=64)
+        nc.vector.tensor_copy(picked1[:], tab_s[:].bitcast(U8).indirect(entries(dst_list, h1)))
+        quantise_wc(1)
+        move_scales(planes1, picked1[:].bitcast(I32))
+        weights0 = shared.tile([P, QUARTER], F32, offset=WEIGHTS0_AT, align_bytes=64)
+        nc.sync.dma_start(out=weights0[:], in_=wgo[:, 0:QUARTER])
+        weights1 = shared.tile([P, HALF], F32, offset=WEIGHTS1_AT, align_bytes=64)
+        wa_w.append(shared.tile([P, PAIR], I32, name="wa1", offset=WA1_AT, align_bytes=64))
+        wb_w.append(shared.tile([P, PAIR], I32, name="wb1", offset=WB1_AT, align_bytes=64))
         state.append(shared.tile([P, T], F32, name="state2", offset=STATE2_AT))
         state.append(shared.tile([P, T], F32, name="state3", offset=STATE3_AT))
-        weight_all = shared.tile([P, J], F32, offset=WEIGHTS_AT)
-        nc.sync.dma_start(out=state[1][:], in_=rT[run_of_128(1), :])
-        nc.sync.dma_start(out=state[2][:, 0 : T // 2], in_=rT[run_of_128(2), 0 : T // 2])
-        nc.sync.dma_start(out=weight_rows[WEIGHT_ROW:P, :], in_=wgo[0, 0:HALF].rearrange("(c j) -> c j", j=P))
-        nc.sync.dma_start(out=state[2][:, T // 2 : T], in_=rT[run_of_128(2), T // 2 : T])
-        nc.sync.dma_start(out=state[LAST][:], in_=rT[run_of_128(LAST), :])
-        nc.sync.dma_start(out=weight_all[:, run_of_512(1)], in_=wgo[:, run_of_512(1)])
-        for name, blocks, packed, at in (("wb_rest", wb_w, wb_words, WB_REST_AT), ("wa_rest", wa_w, wa_words, WA_REST_AT)):
-            rest = shared.tile([P, N - FIRST_COLUMNS], I32, name=name, offset=at, align_bytes=64)
-            nc.sync.dma_start(out=rest[:], in_=words_of(packed)[:, FIRST_COLUMNS:N])
-            blocks.extend(rest[:, run_of_128(i)] for i in range((N - FIRST_COLUMNS) // P))
-        nc.sync.dma_start(out=weight_all[:, run_of_512(0)], in_=wgo[:, run_of_512(0)])
+        nc.sync.dma_start(out=weights1[:], in_=wgo[:, h1])
+        nc.sync.dma_start(out=state[2][:], in_=rT[run(2, P), :])
+        nc.sync.dma_start(out=wa_w[1][:], in_=words_of(wa_words)[:, PAIR:N])
+        nc.sync.dma_start(out=wb_w[1][:], in_=words_of(wb_words)[:, PAIR:N])
+        nc.sync.dma_start(out=state[3][:], in_=rT[run(3, P), :])
 
-        def targets(edges):
-            return dst_list[:, edges.start // LIST_ROWS : edges.stop // LIST_ROWS]
+        def edges_of(u, part):
+            return run(2 * UNITS[u][1] + part, QUARTER)
 
-        def piece_at(name, kib, width):
-            return shared.tile([P, width], F32, name=name, offset=PIECES_AT + int(KIB * kib))
+        def gather_state(values, b, edges):
+            nc.vector.tensor_copy(values, state[b][:].indirect(entries(dst_list, edges)))
 
-        src_words = held.tile([P, J], U32, align_bytes=64)
-        dst_words = [
-            held.tile([P, HALF], U32, name="dst_words0", align_bytes=64),
-            shared.tile([P, HALF], U32, name="dst_words1", offset=LATE_WORDS_AT, align_bytes=64),
+        def window(u, edges):
+            return placed[WINDOW_OF[UNITS[u][0]]][:].indirect(entries(dst_list, edges))
+
+        def store(u):
+            b = UNITS[u][0]
+            nc.sync.dma_start(out=out[run(b, P), :], in_=placed[WINDOW_OF[b]][:])
+
+        def gate(u, j, za, ms):
+            b, h = UNITS[u]
+            width = j.stop - j.start
+            pair, n = b // 2, run(b % 2, P)
+            src_w, dst_w = src_words[h][:, j].bitcast(FP8X4), dst_words[h][:, j].bitcast(FP8X4)
+            src_plane = src_s[:, run(h, HALF)][:, j]
+            nc.tensor.matmul_mx(
+                za[:, 0:width], lhsT=wb_w[pair][:, n].bitcast(FP8X4), lhsT_scale=wb_s[:, run(b, P)],
+                rhs=src_w, rhs_scale=src_plane, start=True, stop=False,
+            )
+            nc.tensor.matmul_mx(
+                za[:, 0:width], lhsT=wa_w[pair][:, n].bitcast(FP8X4), lhsT_scale=wa_s[:, run(b, P)],
+                rhs=dst_w, rhs_scale=dst_s[h][:, j], start=False, stop=True,
+            )
+            nc.tensor.matmul_mx(
+                ms[:, 0:width], lhsT=wc_w[pair][:, n].bitcast(FP8X4), lhsT_scale=wc_s[pair][:, n],
+                rhs=src_w, rhs_scale=src_plane, start=True, stop=True,
+            )
+            nc.scalar.activation(factors[u % 2][:, h0][:, j], za[:, 0:width], SIGMOID)
+            nc.scalar.copy(factors[u % 2][:, h1][:, j], ms[:, 0:width])
+
+        gated0 = [
+            held.tile([P, QUARTER], F32, name="gated00"),
+            shared.tile([P, QUARTER], F32, name="gated01", offset=GATED0_AT, align_bytes=64),
         ]
-        nc.vector.tensor_copy(src_words[:], tab_w[:].bitcast(U32).indirect(src_list[:]))
-        nc.vector.tensor_copy(dst_words[0][:], tab_w[:].bitcast(U32).indirect(targets(run_of_512(0))))
-        nc.vector.quantize_mx(out=wc_w[:].bitcast(FP8X4), scales=wc_s[:], in_=wc_bf[:].rearrange("p n i -> p (n i)"))
-        nc.vector.tensor_copy(dst_words[1][:], tab_w[:].bitcast(U32).indirect(targets(run_of_512(1))))
 
-        def gather_state(b, edges, values):
-            nc.vector.tensor_copy(values, state[b][:].indirect(targets(edges)))
+        def gated(u, j):
+            if u == 0:
+                return gated0[j.start // QUARTER][:]
+            return work[:, (u - 1) * STRETCH : (u - 1) * STRETCH + HALF][:, j]
 
-        early = [
-            shared.tile([P, J], F32, name="early0", offset=CAST_AT),
-            held.tile([P, J], F32, name="early1"),
-            held.tile([P, HALF], F32, name="early2"),
-        ]
-        for h in range(HALVES):
-            gather_state(0, run_of_512(h), early[0][:, run_of_512(h)])
-        gather_state(1, slice(0, J), early[1][:])
-        gather_state(2, run_of_512(0), early[2][:])
+        def summed(u):
+            at = u * STRETCH + HALF - LAP
+            return work[:, at : at + QUARTER]
 
-        za_banks = [psum.tile([P, HALF], F32, name="za%d" % i) for i in range(BANKS)]
-        ms_banks = [psum.tile([P, HALF], F32, name="ms%d" % i) for i in range(BANKS)]
-        turned_banks = [psum.tile([P, HALF], F32, name="turned%d" % i) for i in range(BANKS)]
-        back_banks = [psum.tile([P, HALF], F32, name="back%d" % i) for i in range(BANKS)]
+        def first_values(u):
+            if u < 2:
+                return early[u][:, 0:QUARTER]
+            return work[:, (u - 1) * STRETCH - QUARTER : (u - 1) * STRETCH]
 
-        gated = {}
+        def second_values(u):
+            return early[min(u, 1)][:, QUARTER:HALF]
 
-        def gate(b, h):
-            n, j = run_of_128(b), run_of_512(h)
-            za, ms = za_banks[len(gated) % BANKS], ms_banks[len(gated) % BANKS]
-            if (b, h) in FACTORS_AT:
-                factors = piece_at("factors%d%d" % (b, h), FACTORS_AT[b, h], 2 * HALF)
+        def multiply(u, j):
+            nc.gpsimd.tensor_tensor(gated(u, j), factors[u % 2][:, h0][:, j], factors[u % 2][:, h1][:, j], MULT)
+
+        first, second, whole = run(0, QUARTER), run(1, QUARTER), slice(0, HALF)
+
+        gate(0, first, banks[6], banks[7])
+        nc.tensor.transpose(banks[6][:, 0:P], weight_rows[:], identity[:])
+        gate(0, second, banks[0], banks[1])
+        nc.scalar.copy(weight_col[:], banks[6][:, WEIGHT_ROW:P])
+        src_words.append(shared.tile([P, HALF], U32, name="src_words1", offset=SRC1_AT, align_bytes=64))
+        dst_words.append(shared.tile([P, HALF], U32, name="dst_words1", offset=DST1_AT, align_bytes=64))
+        gather_words(src_words[1], src_list, 1)
+        gather_state(early[0][:], 0, h0)
+        gather_words(dst_words[1], dst_list, 1)
+        gather_state(early[1][:], 1, h0)
+        multiply(0, first)
+        multiply(0, second)
+        gate(1, whole, banks[6], banks[7])
+
+        weighted = tail[:, second]
+        for u in range(LAST):
+            h = UNITS[u][1]
+            forward = [banks[2 * u % RING], banks[(2 * u + 1) % RING]]
+            back = banks[(2 * u + 2) % RING]
+            weights = weights0[:] if h == 0 else weights1[:, first]
+            joined = u == LAST - 1
+            nc.gpsimd.tensor_tensor(summed(u), gated(u, first), first_values(u), ADD)
+            for s in range(2):
+                square = forward[s][:, 0:P]
+                nc.tensor.matmul(square, gated(u, second)[:, run(s, P)], identity[:], start=True, stop=False, is_transpose=True)
+                nc.tensor.matmul(square, second_values(u)[:, run(s, P)], identity[:], start=False, stop=True, is_transpose=True)
+            if u > 0:
+                gather_state(second_values(u + 1), UNITS[u + 1][0], edges_of(u + 1, 1))
+            result = merged[:, first] if joined or u == 0 else gated(u, second)
+            nc.gpsimd.tensor_tensor(result, summed(u), weights, MULT)
+            if not joined:
+                nc.vector.tensor_copy(window(u, edges_of(u, 0)), result)
+                gather_state(first_values(u + 2), UNITS[u + 2][0], edges_of(u + 2, 0))
+            multiply(u + 1, whole)
+            for s in range(2):
+                nc.scalar.activation(weighted[:, run(s, P)], forward[s][:, 0:P], COPY, scale=weight_col[:, 2 * h + s : 2 * h + s + 1])
+            for s in range(2):
+                nc.tensor.transpose(back[:, run(s, P)], weighted[:, run(s, P)], identity[:])
+            result = merged[:, second] if joined else turned[:, run(u, QUARTER)]
+            nc.scalar.copy(result, back[:, 0:QUARTER])
+            if joined:
+                nc.vector.tensor_copy(window(u, h1), merged[:])
             else:
-                factors = held.tile([P, 2 * HALF], F32, name="factors%d%d" % (b, h))
-            gates, messages = factors[:, 0:HALF], factors[:, HALF : 2 * HALF]
-            dst_w, src_w = dst_words[h][:].bitcast(FP8X4), src_words[:, j].bitcast(FP8X4)
-            nc.tensor.matmul_mx(
-                za[:], lhsT=wb_w[b].bitcast(FP8X4), lhsT_scale=wb_s.bitcast(U8)[:, n],
-                rhs=src_w, rhs_scale=src_s[:, j], start=True, stop=False,
-            )
-            nc.tensor.matmul_mx(
-                za[:], lhsT=wa_w[b].bitcast(FP8X4), lhsT_scale=wa_s.bitcast(U8)[:, n],
-                rhs=dst_w, rhs_scale=dst_s[:, j], start=False, stop=True,
-            )
-            nc.tensor.matmul_mx(
-                ms[:], lhsT=wc_w[:, n].bitcast(FP8X4), lhsT_scale=wc_s[:, n],
-                rhs=src_w, rhs_scale=src_s[:, j], start=True, stop=True,
-            )
-            nc.scalar.activation(gates, za[:], SIGMOID)
-            nc.scalar.copy(messages, ms[:])
-            if (b, h) in GATED_AT:
-                gated[b, h] = piece_at("gated%d%d" % (b, h), GATED_AT[b, h], HALF)
-            else:
-                gated[b, h] = held.tile([P, HALF], F32, name="gated%d%d" % (b, h))
-            nc.gpsimd.tensor_tensor(gated[b, h][:], gates, messages, MULT)
+                gate(u + 2, whole, forward[0], forward[1])
+                nc.vector.tensor_copy(window(u, edges_of(u, 1)), result)
+            if h == 1:
+                store(u)
 
-        def add_turned(turned, values, start, stop):
-            nc.tensor.matmul(turned, values, identity[:], start=start, stop=stop, is_transpose=True)
-
-        def turn_quarter(squares, turned):
-            for i, s in enumerate(squares):
-                add_turned(turned[:, run_of_128(i)], early[0][:, run_of_128(s)], i == 0, False)
-            for i, s in enumerate(squares):
-                add_turned(turned[:, run_of_128(i)], gated[0, 0][:, run_of_128(s)], False, i == len(squares) - 1)
-
-        def turn_half(b, turned):
-            for s in range(SQUARES):
-                add_turned(turned[:, run_of_128(s)], gated[b, 0][:, run_of_128(s)], True, False)
-                add_turned(turned[:, run_of_128(s)], early[b][:, run_of_128(s)], False, True)
-
-        def weigh_and_turn_back(squares, turned, back, weighted, result):
-            for i, s in enumerate(squares):
-                nc.scalar.activation(weighted[i], turned[:, run_of_128(i)], COPY, scale=weight_col[:, s : s + 1])
-            for i in range(len(squares)):
-                nc.tensor.transpose(back[:, run_of_128(i)], weighted[i], identity[:])
-            nc.scalar.copy(result, back[:, 0 : len(squares) * P])
-
-        def scatter(window, edges, values):
-            nc.vector.tensor_copy(placed[window][:].indirect(targets(edges)), values)
-
-        def store(window, b):
-            nc.sync.dma_start(out=out[run_of_128(b), :], in_=placed[window][:])
-
-        late = {}
-
-        def squares_at(name, kib, count):
-            tile = piece_at(name, kib, count * P)
-            return [tile[:, run_of_128(i)] for i in range(count)]
-
-        def gather_late(b, q, kib):
-            late[b, q] = piece_at("late%d%d" % (b, q), kib, QUARTER)
-            gather_state(b, run_of_256(q), late[b, q][:])
-
-        def finish_quarters(b, sums_at, finished, lates):
-            sums = {q: piece_at("sum%d%d" % (b, q), sums_at[q], QUARTER) for q in (2, 3)}
-            for q in (2, 3):
-                nc.gpsimd.tensor_tensor(sums[q][:], gated[b, 1][:, run_of_256(q - 2)], early[b][:, run_of_256(q)], ADD)
-            for q in (2, 3):
-                nc.gpsimd.tensor_tensor(finished[q], sums[q][:], weight_all[:, run_of_256(q)], MULT)
-            for q in (2, 3):
-                if q in lates:
-                    gather_late(*lates[q])
-                scatter(b, run_of_256(q), finished[q])
-
-        quarters = [piece_at("result0%d" % q, RESULTS_0[q], QUARTER)[:] for q in range(4)]
-        results = {b: held.tile([P, J], F32, name="results%d" % b) for b in range(1, ROW_BLOCKS)}
-
-        gate(0, 0)
-        gate(0, 1)
-        nc.tensor.transpose(back_banks[1][:, 0:P], weight_rows[:], identity[:])
-        nc.scalar.copy(weight_col[:], back_banks[1][:, WEIGHT_ROW:P])
-        turn_quarter((0, 1), za_banks[0])
-        weigh_and_turn_back((0, 1), za_banks[0], za_banks[1], squares_at("weighted_q0", WEIGHTED_Q0, 2), quarters[0])
-        scatter(0, run_of_256(0), quarters[0])
-        turn_quarter((2, 3), turned_banks[1])
-        finish_quarters(0, {2: SUM_02, 3: SUM_03}, quarters, {2: (2, 2, LATE_22), 3: (2, 3, LATE_23)})
-        weighted = squares_at("weighted_q1", WEIGHTED_Q1, 1) + squares_at("weighted_q1_last", WEIGHTED_Q1_LAST, 1)
-        weigh_and_turn_back((2, 3), turned_banks[1], back_banks[1], weighted, quarters[1])
-        gather_late(LAST, 0, LATE_30)
-        scatter(0, run_of_256(1), quarters[1])
-        store(0, 0)
-
-        gate(1, 1)
-        gate(1, 0)
-        finished = {2: piece_at("result12", RESULT_12, QUARTER)[:], 3: results[1][:, run_of_256(3)]}
-        finish_quarters(1, {2: SUM_12, 3: SUM_13}, finished, {2: (LAST, 1, LATE_31), 3: (LAST, 2, LATE_32)})
-        turn_half(1, turned_banks[0])
-        weighted = squares_at("weighted10", WEIGHTED_10, SQUARES)
-        weigh_and_turn_back(range(SQUARES), turned_banks[0], back_banks[0], weighted, results[1][:, run_of_512(0)])
-        gather_late(LAST, 3, LATE_33)
-        scatter(1, run_of_512(0), results[1][:, run_of_512(0)])
-        store(1, 1)
-
-        gate(2, 0)
-        gate(2, 1)
-        turn_half(2, turned_banks[1])
-        weighted = squares_at("weighted20", WEIGHTED_20, SQUARES)
-        weigh_and_turn_back(range(SQUARES), turned_banks[1], back_banks[1], weighted, results[2][:, run_of_512(0)])
-        summed = piece_at("sum21", SUM_21, HALF)
-        for q in (2, 3):
-            nc.gpsimd.tensor_tensor(summed[:, run_of_256(q - 2)], gated[2, 1][:, run_of_256(q - 2)], late[2, q][:], ADD)
-        nc.gpsimd.tensor_tensor(results[2][:, run_of_512(1)], summed[:], weight_all[:, run_of_512(1)], MULT)
-        scatter(0, slice(0, J), results[2][:])
-        store(0, 2)
-
-        for h in range(HALVES):
-            gate(LAST, h)
-        for q in range(4):
-            nc.gpsimd.tensor_tensor(results[LAST][:, run_of_256(q)], gated[LAST, q // 2][:, run_of_256(q % 2)], late[LAST, q][:], ADD)
-        nc.vector.tensor_tensor(placed[1][:].indirect(dst_list[:]), results[LAST][:], weight_all[:], MULT)
-        store(1, LAST)
+        nc.gpsimd.tensor_tensor(tail[:, first], gated(LAST, first), first_values(LAST), ADD)
+        nc.gpsimd.tensor_tensor(tail[:, second], gated(LAST, second), second_values(LAST), ADD)
+        nc.vector.tensor_tensor(window(LAST, h1), tail[:], weights1[:], MULT)
+        store(LAST)

@@ -29,31 +29,57 @@ LIST_ROWS = 16
 HALF = J // 2
 QUARTER = J // 4
 STAGE = P - SCALE_ROWS
-TURNED_SQUARES = 4
+TURNED_SQUARES = 2
 WEIGHT_ROW = P - TURNED_SQUARES
 PAIR = 2 * P
 LAP = 64
 UNITS = [(0, 0), (1, 0), (0, 1), (1, 1), (2, 0), (3, 0), (2, 1), (3, 1)]
 LAST = len(UNITS) - 1
-WINDOW_OF = {0: 0, 1: 1, 2: 2, 3: 0}
-RING = 6
+WINDOW_OF = {0: 0, 1: 1, 2: 2, 3: 3}
 
 STATE2_AT = 0
 TABLE_AT = STATE2_AT + 4 * T - 64
-WEIGHTS0_AT = TABLE_AT + 64
-WEIGHTS1_AT = TABLE_AT + T - 64
-RAW1_AT = WEIGHTS1_AT + 4 * HALF
-WA1_AT = RAW1_AT
-PICKED1_AT = RAW1_AT + 4 * PACK * PAIR - 64
-WB1_AT = PICKED1_AT + 128 - 4 * PAIR
+WEIGHTS0_AT = TABLE_AT + T - 64
+WEIGHTS1_AT = WEIGHTS0_AT + 4 * HALF
+PICKED1_AT = WEIGHTS1_AT + 4 * HALF - 64
 STATE3_AT = PICKED1_AT + HALF - 64
-RAW_LATE_AT = STATE3_AT + 4 * T
-SRC1_AT = RAW_LATE_AT
-GATED0_AT = RAW_LATE_AT + 4 * PACK * PAIR
+RAW1_AT = STATE3_AT + 4 * T
+SRC1_AT = RAW1_AT
+RAW_LATE_AT = RAW1_AT + 4 * PACK * PAIR
+WA1_AT = RAW_LATE_AT
+WB1_AT = WA1_AT + 4 * PAIR
+CAST1_AT = RAW_LATE_AT + 4 * PACK * PAIR
+GATED0_AT = CAST1_AT + 2 * PACK * PAIR
 ROWS_AT = GATED0_AT + 4 * QUARTER - 256
 DST1_AT = GATED0_AT + 4 * QUARTER
 
-STRETCH = HALF - LAP + QUARTER - LAP + QUARTER
+PIECES = 2 * len(UNITS)
+LEAD = 5
+SINGLE = PIECES - 4
+TURNED = (1, 5, 9, 11, 13)
+STEP = QUARTER - LAP
+SLIDE = HALF - LAP
+
+SUM_AT, VALUES_AT = {}, {}
+
+
+def lay_out_work():
+    at = LAST * SLIDE
+    for p in range(SINGLE + 1):
+        if p in TURNED:
+            continue
+        if p - 1 in TURNED and p - 1 + LEAD < PIECES:
+            VALUES_AT[p - 1 + LEAD] = at
+            at = at + STEP
+        SUM_AT[p] = at
+        at = at + STEP
+        if p + LEAD < PIECES:
+            VALUES_AT[p + LEAD] = at
+        at = at + QUARTER
+    return at
+
+
+WORK = lay_out_work()
 
 
 def tile_list_rgg_L_kernel(
@@ -88,8 +114,8 @@ def tile_list_rgg_L_kernel(
         wa_s, wb_s = w_s[:].bitcast(U8)[:, 0:N], w_s[:].bitcast(U8)[:, N : 2 * N]
         src_s = planes0[:].bitcast(U8)[:, 0:J]
         dst_s = [planes0[:].bitcast(U8)[:, J : J + HALF], planes1[:].bitcast(U8)]
-        placed = [held.tile([P, T], F32, name="placed%d" % i) for i in range(3)]
-        weight_col = held.tile([P, TURNED_SQUARES], F32)
+        placed = [held.tile([P, T], F32, name="placed%d" % i) for i in range(4)]
+        weight_col = [held.tile([P, TURNED_SQUARES], F32, name="weight_col%d" % h) for h in range(2)]
         weight_rows = shared.tile([P, P], F32, offset=ROWS_AT, align_bytes=64)
         identity = held.tile([P, P], F32)
         state = [held.tile([P, T], F32, name="state%d" % b) for b in range(2)]
@@ -99,14 +125,18 @@ def tile_list_rgg_L_kernel(
             shared.tile([P, PACK, PAIR], F32, name="wc_raw0", offset=RAW1_AT, align_bytes=64),
             shared.tile([P, PACK, PAIR], F32, name="wc_raw1", offset=RAW_LATE_AT, align_bytes=64),
         ]
-        wc_bf = [held.tile([P, PAIR, PACK], BF16, name="wc_bf%d" % i, align_bytes=64) for i in range(2)]
+        wc_bf = [
+            held.tile([P, PAIR, PACK], BF16, name="wc_bf0", align_bytes=64),
+            shared.tile([P, PAIR, PACK], BF16, name="wc_bf1", offset=CAST1_AT, align_bytes=64),
+        ]
         wc_w = [held.tile([P, PAIR], U32, name="wc_w%d" % i, align_bytes=64) for i in range(2)]
         wc_s = [held.tile([P, PAIR], U8, name="wc_s%d" % i, align_bytes=64) for i in range(2)]
         banks = [psum.tile([P, HALF], F32, name="bank%d" % i) for i in range(8)]
         early = [held.tile([P, HALF], F32, name="early%d" % i) for i in range(2)]
+        early.append(held.tile([P, QUARTER], F32, name="early2"))
         factors = [held.tile([P, 2 * HALF], F32, name="factors%d" % i) for i in range(2)]
-        work = held.tile([P, LAST * STRETCH], F32)
-        turned = held.tile([P, LAST * QUARTER], F32)
+        work = held.tile([P, WORK], F32)
+        results = held.tile([P, (LAST - 1) * HALF], F32)
         merged = held.tile([P, HALF], F32)
         tail = held.tile([P, HALF], F32)
 
@@ -129,14 +159,15 @@ def tile_list_rgg_L_kernel(
 
         h0, h1 = run(0, HALF), run(1, HALF)
 
-        nc.vector.memset(placed[2][:], 0.0)
+        nc.vector.memset(placed[3][:, 0 : T // 2 + 1], 0.0)
+        nc.vector.memset(placed[3][:, T // 2 + 1 : T], 0.0)
         nc.gpsimd.memset(tab_s[0:STAGE, :], 0)
         nc.gpsimd.memset(w_s[:], 0)
         nc.gpsimd.memset(planes0[:], 0)
         nc.gpsimd.memset(planes1[:], 0)
         nc.gpsimd.memset(weight_rows[0:WEIGHT_ROW, :], 0.0)
         make_identity(nc, identity[:])
-        for window in placed[0:2]:
+        for window in placed[0:3]:
             nc.gpsimd.memset(window[:], 0.0)
 
         nc.sync.dma_start(out=tab_s[STAGE:P, :], in_=tab_scales[0].bitcast(I32))
@@ -155,10 +186,12 @@ def tile_list_rgg_L_kernel(
         picked0 = held.tile([P, J + HALF], U8, align_bytes=64)
         nc.vector.tensor_copy(picked0[:, 0:J], tab_s[:].bitcast(U8).indirect(src_list[:]))
         nc.vector.tensor_copy(picked0[:, J : J + HALF], tab_s[:].bitcast(U8).indirect(entries(dst_list, h0)))
+        picked1 = shared.tile([P, HALF], U8, offset=PICKED1_AT, align_bytes=64)
+        nc.vector.tensor_copy(picked1[:], tab_s[:].bitcast(U8).indirect(entries(dst_list, h1)))
         move_scales(planes0, picked0[:].bitcast(I32))
         nc.sync.dma_start(out=state[0][:, T // 2 : T], in_=rT[run(0, P), T // 2 : T])
         nc.sync.dma_start(
-            out=weight_rows[WEIGHT_ROW:P, :], in_=wgo[0, :].rearrange("(h q c j) -> h q c j", h=2, q=2, j=P)[:, 1]
+            out=weight_rows[WEIGHT_ROW:P, :], in_=wgo[0, run(1, QUARTER)].rearrange("(c j) -> c j", j=P)
         )
         nc.sync.dma_start(out=state[1][:], in_=rT[run(1, P), :])
 
@@ -173,22 +206,24 @@ def tile_list_rgg_L_kernel(
             cast_wc(i)
         quantise_wc(0)
 
-        picked1 = shared.tile([P, HALF], U8, offset=PICKED1_AT, align_bytes=64)
-        nc.vector.tensor_copy(picked1[:], tab_s[:].bitcast(U8).indirect(entries(dst_list, h1)))
+        src_words.append(shared.tile([P, HALF], U32, name="src_words1", offset=SRC1_AT, align_bytes=64))
+        gather_words(src_words[1], src_list, 1)
         quantise_wc(1)
         move_scales(planes1, picked1[:].bitcast(I32))
-        weights0 = shared.tile([P, QUARTER], F32, offset=WEIGHTS0_AT, align_bytes=64)
-        nc.sync.dma_start(out=weights0[:], in_=wgo[:, 0:QUARTER])
+        weights0 = shared.tile([P, HALF], F32, offset=WEIGHTS0_AT, align_bytes=64)
+        nc.sync.dma_start(out=weights0[:, 0:QUARTER], in_=wgo[:, 0:QUARTER])
+        nc.sync.dma_start(out=weights0[:, QUARTER:HALF], in_=wgo[:, QUARTER:HALF])
         weights1 = shared.tile([P, HALF], F32, offset=WEIGHTS1_AT, align_bytes=64)
         wa_w.append(shared.tile([P, PAIR], I32, name="wa1", offset=WA1_AT, align_bytes=64))
         wb_w.append(shared.tile([P, PAIR], I32, name="wb1", offset=WB1_AT, align_bytes=64))
         state.append(shared.tile([P, T], F32, name="state2", offset=STATE2_AT))
         state.append(shared.tile([P, T], F32, name="state3", offset=STATE3_AT))
-        nc.sync.dma_start(out=weights1[:], in_=wgo[:, h1])
         nc.sync.dma_start(out=state[2][:], in_=rT[run(2, P), :])
+        nc.sync.dma_start(out=weights1[:, 0:QUARTER], in_=wgo[:, run(2, QUARTER)])
         nc.sync.dma_start(out=wa_w[1][:], in_=words_of(wa_words)[:, PAIR:N])
         nc.sync.dma_start(out=wb_w[1][:], in_=words_of(wb_words)[:, PAIR:N])
         nc.sync.dma_start(out=state[3][:], in_=rT[run(3, P), :])
+        nc.sync.dma_start(out=weights1[:, QUARTER:HALF], in_=wgo[:, run(3, QUARTER)])
 
         def edges_of(u, part):
             return run(2 * UNITS[u][1] + part, QUARTER)
@@ -225,26 +260,34 @@ def tile_list_rgg_L_kernel(
             nc.scalar.copy(factors[u % 2][:, h1][:, j], ms[:, 0:width])
 
         gated0 = [
-            held.tile([P, QUARTER], F32, name="gated00"),
+            shared.tile([P, QUARTER], F32, name="gated00", offset=CAST1_AT, align_bytes=64),
             shared.tile([P, QUARTER], F32, name="gated01", offset=GATED0_AT, align_bytes=64),
         ]
 
         def gated(u, j):
             if u == 0:
                 return gated0[j.start // QUARTER][:]
-            return work[:, (u - 1) * STRETCH : (u - 1) * STRETCH + HALF][:, j]
+            at = (LAST - u) * SLIDE
+            return work[:, at : at + HALF][:, j]
 
-        def summed(u):
-            at = u * STRETCH + HALF - LAP
-            return work[:, at : at + QUARTER]
+        def part_of(p):
+            return p % 2 if p | 1 in TURNED or p // 2 == LAST else 1 - p % 2
 
-        def first_values(u):
-            if u < 2:
-                return early[u][:, 0:QUARTER]
-            return work[:, (u - 1) * STRETCH - QUARTER : (u - 1) * STRETCH]
+        def columns(p):
+            return run(part_of(p), QUARTER)
 
-        def second_values(u):
-            return early[min(u, 1)][:, QUARTER:HALF]
+        def summed(p):
+            return work[:, SUM_AT[p] : SUM_AT[p] + QUARTER]
+
+        def values(p):
+            if p < LEAD:
+                return early[p // 2][:, columns(p)]
+            return work[:, VALUES_AT[p] : VALUES_AT[p] + QUARTER]
+
+        def gather_late(slot):
+            p = slot + LEAD
+            if p < PIECES:
+                gather_state(values(p), UNITS[p // 2][0], edges_of(p // 2, part_of(p)))
 
         def multiply(u, j):
             nc.gpsimd.tensor_tensor(gated(u, j), factors[u % 2][:, h0][:, j], factors[u % 2][:, h1][:, j], MULT)
@@ -254,52 +297,64 @@ def tile_list_rgg_L_kernel(
         gate(0, first, banks[6], banks[7])
         nc.tensor.transpose(banks[6][:, 0:P], weight_rows[:], identity[:])
         gate(0, second, banks[0], banks[1])
-        nc.scalar.copy(weight_col[:], banks[6][:, WEIGHT_ROW:P])
-        src_words.append(shared.tile([P, HALF], U32, name="src_words1", offset=SRC1_AT, align_bytes=64))
+        nc.scalar.copy(weight_col[0][:], banks[6][:, WEIGHT_ROW:P])
         dst_words.append(shared.tile([P, HALF], U32, name="dst_words1", offset=DST1_AT, align_bytes=64))
-        gather_words(src_words[1], src_list, 1)
         gather_state(early[0][:], 0, h0)
+        gather_state(early[2][:], 0, edges_of(2, 0))
         gather_words(dst_words[1], dst_list, 1)
         gather_state(early[1][:], 1, h0)
         multiply(0, first)
         multiply(0, second)
         gate(1, whole, banks[6], banks[7])
 
-        weighted = tail[:, second]
-        for u in range(LAST):
-            h = UNITS[u][1]
-            forward = [banks[2 * u % RING], banks[(2 * u + 1) % RING]]
-            back = banks[(2 * u + 2) % RING]
-            weights = weights0[:] if h == 0 else weights1[:, first]
-            joined = u == LAST - 1
-            nc.gpsimd.tensor_tensor(summed(u), gated(u, first), first_values(u), ADD)
-            for s in range(2):
-                square = forward[s][:, 0:P]
-                nc.tensor.matmul(square, gated(u, second)[:, run(s, P)], identity[:], start=True, stop=False, is_transpose=True)
-                nc.tensor.matmul(square, second_values(u)[:, run(s, P)], identity[:], start=False, stop=True, is_transpose=True)
-            if u > 0:
-                gather_state(second_values(u + 1), UNITS[u + 1][0], edges_of(u + 1, 1))
-            result = merged[:, first] if joined or u == 0 else gated(u, second)
-            nc.gpsimd.tensor_tensor(result, summed(u), weights, MULT)
-            if not joined:
-                nc.vector.tensor_copy(window(u, edges_of(u, 0)), result)
-                gather_state(first_values(u + 2), UNITS[u + 2][0], edges_of(u + 2, 0))
-            multiply(u + 1, whole)
-            for s in range(2):
-                nc.scalar.activation(weighted[:, run(s, P)], forward[s][:, 0:P], COPY, scale=weight_col[:, 2 * h + s : 2 * h + s + 1])
-            for s in range(2):
-                nc.tensor.transpose(back[:, run(s, P)], weighted[:, run(s, P)], identity[:])
-            result = merged[:, second] if joined else turned[:, run(u, QUARTER)]
-            nc.scalar.copy(result, back[:, 0:QUARTER])
-            if joined:
-                nc.vector.tensor_copy(window(u, h1), merged[:])
+        weights = [weights0, weights1]
+        pairs = [banks[0:2], banks[4:6]]
+        back = banks[3]
+        for p in range(PIECES - 2):
+            u, h = p // 2, UNITS[p // 2][1]
+            pair = pairs[len([t for t in TURNED if t <= p | 1]) % 2 - 1]
+            result = results[:, run(p, QUARTER)] if p < SINGLE else merged[:, columns(p)]
+            if p in TURNED:
+                if p == TURNED[1]:
+                    for s in range(2):
+                        nc.tensor.transpose(banks[7][:, run(s, P)], weights1[:, second][:, run(s, P)], identity[:])
+                    nc.scalar.copy(weight_col[1][:], banks[7][:, 0:QUARTER:P])
+                if p >= SINGLE:
+                    weighted = [gated(LAST, first)[:, run(s, P)] for s in range(2)]
+                elif p + 2 in TURNED:
+                    weighted = [summed(p + 1)[:, run(s, P)] for s in range(2)]
+                else:
+                    weighted = [summed(p + 1 + s)[:, 0:P] for s in range(2)]
+                for s in range(2):
+                    nc.scalar.activation(weighted[s], pair[s][:, 0:P], COPY, scale=weight_col[h][:, s : s + 1])
+                for s in range(2):
+                    nc.tensor.transpose(back[:, run(s, P)], weighted[s], identity[:])
+                nc.scalar.copy(result, back[:, 0:QUARTER])
             else:
-                gate(u + 2, whole, forward[0], forward[1])
-                nc.vector.tensor_copy(window(u, edges_of(u, 1)), result)
-            if h == 1:
+                if p + 1 in TURNED:
+                    for s in range(2):
+                        square = pair[s][:, 0:P]
+                        nc.tensor.matmul(square, gated(u, second)[:, run(s, P)], identity[:], start=True, stop=False, is_transpose=True)
+                        nc.tensor.matmul(square, values(p + 1)[:, run(s, P)], identity[:], start=False, stop=True, is_transpose=True)
+                nc.gpsimd.tensor_tensor(summed(p), gated(u, columns(p)), values(p), ADD)
+                nc.gpsimd.tensor_tensor(result, summed(p), weights[h][:, columns(p)], MULT)
+                if p - 1 in TURNED:
+                    gather_late(p - 1)
+                if (p + 1 in TURNED or p % 2) and p < SINGLE:
+                    multiply(u + 1, whole)
+            if p < SINGLE:
+                if p % 2:
+                    gate(u + 2, whole, pair[0], pair[1])
+                nc.vector.tensor_copy(window(u, edges_of(u, part_of(p))), result)
+                if p not in TURNED:
+                    gather_late(p)
+            elif p % 2:
+                nc.vector.tensor_copy(window(u, h1), merged[:])
+            if p % 2 and h == 1:
                 store(u)
 
-        nc.gpsimd.tensor_tensor(tail[:, first], gated(LAST, first), first_values(LAST), ADD)
-        nc.gpsimd.tensor_tensor(tail[:, second], gated(LAST, second), second_values(LAST), ADD)
+        multiply(LAST, whole)
+        for p in range(PIECES - 2, PIECES):
+            nc.gpsimd.tensor_tensor(tail[:, columns(p)], gated(LAST, columns(p)), values(p), ADD)
         nc.vector.tensor_tensor(window(LAST, h1), tail[:], weights1[:], MULT)
         store(LAST)

@@ -33,15 +33,15 @@ TURNED_SQUARES = 2
 WEIGHT_ROW = P - TURNED_SQUARES
 PAIR = 2 * P
 LAP = 64
-UNITS = [(0, 0), (1, 0), (0, 1), (1, 1), (2, 0), (3, 0), (2, 1), (3, 1)]
+UNITS = [(0, 0), (1, 0), (0, 1), (1, 1), (2, 0), (2, 1), (3, 0), (3, 1)]
 LAST = len(UNITS) - 1
-WINDOW_OF = {0: 0, 1: 1, 2: 2, 3: 3}
+WINDOW_OF = {0: 0, 1: 1, 2: 2, 3: 0}
 
 STATE2_AT = 0
 TABLE_AT = STATE2_AT + 4 * T - 64
-WEIGHTS0_AT = TABLE_AT + T - 64
-WEIGHTS1_AT = WEIGHTS0_AT + 4 * HALF
-PICKED1_AT = WEIGHTS1_AT + 4 * HALF - 64
+WEIGHTS_AT = TABLE_AT + T - 64
+DST1_AT = WEIGHTS_AT + 4 * J
+PICKED1_AT = DST1_AT + 4 * HALF - 64
 STATE3_AT = PICKED1_AT + HALF - 64
 RAW1_AT = STATE3_AT + 4 * T
 SRC1_AT = RAW1_AT
@@ -49,14 +49,11 @@ RAW_LATE_AT = RAW1_AT + 4 * PACK * PAIR
 WA1_AT = RAW_LATE_AT
 WB1_AT = WA1_AT + 4 * PAIR
 CAST1_AT = RAW_LATE_AT + 4 * PACK * PAIR
-GATED0_AT = CAST1_AT + 2 * PACK * PAIR
-ROWS_AT = GATED0_AT + 4 * QUARTER - 256
-DST1_AT = GATED0_AT + 4 * QUARTER
 
 PIECES = 2 * len(UNITS)
 LEAD = 5
 SINGLE = PIECES - 4
-TURNED = (1, 5, 9, 11, 13)
+TURNED = (1, 5, 9, 11)
 STEP = QUARTER - LAP
 SLIDE = HALF - LAP
 
@@ -65,7 +62,7 @@ SUM_AT, VALUES_AT = {}, {}
 
 def lay_out_work():
     at = LAST * SLIDE
-    for p in range(SINGLE + 1):
+    for p in range(SINGLE):
         if p in TURNED:
             continue
         if p - 1 in TURNED and p - 1 + LEAD < PIECES:
@@ -114,9 +111,9 @@ def tile_list_rgg_L_kernel(
         wa_s, wb_s = w_s[:].bitcast(U8)[:, 0:N], w_s[:].bitcast(U8)[:, N : 2 * N]
         src_s = planes0[:].bitcast(U8)[:, 0:J]
         dst_s = [planes0[:].bitcast(U8)[:, J : J + HALF], planes1[:].bitcast(U8)]
-        placed = [held.tile([P, T], F32, name="placed%d" % i) for i in range(4)]
+        placed = [held.tile([P, T], F32, name="placed%d" % i) for i in range(3)]
         weight_col = [held.tile([P, TURNED_SQUARES], F32, name="weight_col%d" % h) for h in range(2)]
-        weight_rows = shared.tile([P, P], F32, offset=ROWS_AT, align_bytes=64)
+        weight_rows = held.tile([P, P], F32)
         identity = held.tile([P, P], F32)
         state = [held.tile([P, T], F32, name="state%d" % b) for b in range(2)]
         wa_w = [held.tile([P, PAIR], I32, name="wa0", align_bytes=64)]
@@ -137,8 +134,7 @@ def tile_list_rgg_L_kernel(
         factors = [held.tile([P, 2 * HALF], F32, name="factors%d" % i) for i in range(2)]
         work = held.tile([P, WORK], F32)
         results = held.tile([P, (LAST - 1) * HALF], F32)
-        merged = held.tile([P, HALF], F32)
-        tail = held.tile([P, HALF], F32)
+        tail = held.tile([P, J], F32)
 
         def entries(offsets, edges):
             return offsets[:, edges.start // LIST_ROWS : edges.stop // LIST_ROWS]
@@ -159,16 +155,17 @@ def tile_list_rgg_L_kernel(
 
         h0, h1 = run(0, HALF), run(1, HALF)
 
-        nc.vector.memset(placed[3][:, 0 : T // 2 + 1], 0.0)
-        nc.vector.memset(placed[3][:, T // 2 + 1 : T], 0.0)
+        nc.vector.memset(placed[2][:, 0 : T // 4 + 1], 0.0)
+        nc.vector.memset(placed[2][:, T // 4 + 1 : T // 2], 0.0)
         nc.gpsimd.memset(tab_s[0:STAGE, :], 0)
         nc.gpsimd.memset(w_s[:], 0)
         nc.gpsimd.memset(planes0[:], 0)
         nc.gpsimd.memset(planes1[:], 0)
         nc.gpsimd.memset(weight_rows[0:WEIGHT_ROW, :], 0.0)
         make_identity(nc, identity[:])
-        for window in placed[0:3]:
+        for window in placed[0:2]:
             nc.gpsimd.memset(window[:], 0.0)
+        nc.gpsimd.memset(placed[2][:, T // 2 : T], 0.0)
 
         nc.sync.dma_start(out=tab_s[STAGE:P, :], in_=tab_scales[0].bitcast(I32))
         nc.sync.dma_start(src_list[:], offs)
@@ -210,20 +207,22 @@ def tile_list_rgg_L_kernel(
         gather_words(src_words[1], src_list, 1)
         quantise_wc(1)
         move_scales(planes1, picked1[:].bitcast(I32))
-        weights0 = shared.tile([P, HALF], F32, offset=WEIGHTS0_AT, align_bytes=64)
-        nc.sync.dma_start(out=weights0[:, 0:QUARTER], in_=wgo[:, 0:QUARTER])
-        nc.sync.dma_start(out=weights0[:, QUARTER:HALF], in_=wgo[:, QUARTER:HALF])
-        weights1 = shared.tile([P, HALF], F32, offset=WEIGHTS1_AT, align_bytes=64)
+        weights = shared.tile([P, J], F32, offset=WEIGHTS_AT, align_bytes=64)
+
+        def load_weights(q):
+            nc.sync.dma_start(out=weights[:, run(q, QUARTER)], in_=wgo[:, run(q, QUARTER)])
+
+        load_weights(0)
+        load_weights(1)
         wa_w.append(shared.tile([P, PAIR], I32, name="wa1", offset=WA1_AT, align_bytes=64))
         wb_w.append(shared.tile([P, PAIR], I32, name="wb1", offset=WB1_AT, align_bytes=64))
         state.append(shared.tile([P, T], F32, name="state2", offset=STATE2_AT))
         state.append(shared.tile([P, T], F32, name="state3", offset=STATE3_AT))
         nc.sync.dma_start(out=state[2][:], in_=rT[run(2, P), :])
-        nc.sync.dma_start(out=weights1[:, 0:QUARTER], in_=wgo[:, run(2, QUARTER)])
+        load_weights(2)
         nc.sync.dma_start(out=wa_w[1][:], in_=words_of(wa_words)[:, PAIR:N])
         nc.sync.dma_start(out=wb_w[1][:], in_=words_of(wb_words)[:, PAIR:N])
         nc.sync.dma_start(out=state[3][:], in_=rT[run(3, P), :])
-        nc.sync.dma_start(out=weights1[:, QUARTER:HALF], in_=wgo[:, run(3, QUARTER)])
 
         def edges_of(u, part):
             return run(2 * UNITS[u][1] + part, QUARTER)
@@ -261,7 +260,7 @@ def tile_list_rgg_L_kernel(
 
         gated0 = [
             shared.tile([P, QUARTER], F32, name="gated00", offset=CAST1_AT, align_bytes=64),
-            shared.tile([P, QUARTER], F32, name="gated01", offset=GATED0_AT, align_bytes=64),
+            held.tile([P, QUARTER], F32, name="gated01"),
         ]
 
         def gated(u, j):
@@ -271,7 +270,7 @@ def tile_list_rgg_L_kernel(
             return work[:, at : at + HALF][:, j]
 
         def part_of(p):
-            return p % 2 if p | 1 in TURNED or p // 2 == LAST else 1 - p % 2
+            return p % 2 if p | 1 in TURNED or p >= SINGLE else 1 - p % 2
 
         def columns(p):
             return run(part_of(p), QUARTER)
@@ -295,31 +294,30 @@ def tile_list_rgg_L_kernel(
         first, second, whole = run(0, QUARTER), run(1, QUARTER), slice(0, HALF)
 
         gate(0, first, banks[6], banks[7])
-        nc.tensor.transpose(banks[6][:, 0:P], weight_rows[:], identity[:])
+        nc.tensor.transpose(banks[2][:, 0:P], weight_rows[:], identity[:])
         gate(0, second, banks[0], banks[1])
-        nc.scalar.copy(weight_col[0][:], banks[6][:, WEIGHT_ROW:P])
+        nc.scalar.copy(weight_col[0][:], banks[2][:, WEIGHT_ROW:P])
         dst_words.append(shared.tile([P, HALF], U32, name="dst_words1", offset=DST1_AT, align_bytes=64))
         gather_state(early[0][:], 0, h0)
         gather_state(early[2][:], 0, edges_of(2, 0))
-        gather_words(dst_words[1], dst_list, 1)
         gather_state(early[1][:], 1, h0)
+        gather_words(dst_words[1], dst_list, 1)
         multiply(0, first)
         multiply(0, second)
         gate(1, whole, banks[6], banks[7])
 
-        weights = [weights0, weights1]
         pairs = [banks[0:2], banks[4:6]]
         back = banks[3]
-        for p in range(PIECES - 2):
+        for p in range(SINGLE):
             u, h = p // 2, UNITS[p // 2][1]
             pair = pairs[len([t for t in TURNED if t <= p | 1]) % 2 - 1]
-            result = results[:, run(p, QUARTER)] if p < SINGLE else merged[:, columns(p)]
+            result = results[:, run(p, QUARTER)] if p else weights[:, run(3, QUARTER)]
             if p in TURNED:
                 if p == TURNED[1]:
                     for s in range(2):
-                        nc.tensor.transpose(banks[7][:, run(s, P)], weights1[:, second][:, run(s, P)], identity[:])
+                        nc.tensor.transpose(banks[7][:, run(s, P)], weights[:, run(3, QUARTER)][:, run(s, P)], identity[:])
                     nc.scalar.copy(weight_col[1][:], banks[7][:, 0:QUARTER:P])
-                if p >= SINGLE:
+                if p + 1 == SINGLE:
                     weighted = [gated(LAST, first)[:, run(s, P)] for s in range(2)]
                 elif p + 2 in TURNED:
                     weighted = [summed(p + 1)[:, run(s, P)] for s in range(2)]
@@ -337,24 +335,24 @@ def tile_list_rgg_L_kernel(
                         nc.tensor.matmul(square, gated(u, second)[:, run(s, P)], identity[:], start=True, stop=False, is_transpose=True)
                         nc.tensor.matmul(square, values(p + 1)[:, run(s, P)], identity[:], start=False, stop=True, is_transpose=True)
                 nc.gpsimd.tensor_tensor(summed(p), gated(u, columns(p)), values(p), ADD)
-                nc.gpsimd.tensor_tensor(result, summed(p), weights[h][:, columns(p)], MULT)
+                nc.gpsimd.tensor_tensor(result, summed(p), weights[:, edges_of(u, part_of(p))], MULT)
                 if p - 1 in TURNED:
                     gather_late(p - 1)
-                if (p + 1 in TURNED or p % 2) and p < SINGLE:
+                if p + 1 in TURNED or p % 2:
                     multiply(u + 1, whole)
-            if p < SINGLE:
-                if p % 2:
-                    gate(u + 2, whole, pair[0], pair[1])
-                nc.vector.tensor_copy(window(u, edges_of(u, part_of(p))), result)
-                if p not in TURNED:
-                    gather_late(p)
-            elif p % 2:
-                nc.vector.tensor_copy(window(u, h1), merged[:])
+            if p % 2:
+                gate(u + 2, whole, pair[0], pair[1])
+            nc.vector.tensor_copy(window(u, edges_of(u, part_of(p))), result)
+            if p == 0:
+                load_weights(3)
+            if p not in TURNED:
+                gather_late(p)
             if p % 2 and h == 1:
                 store(u)
 
-        multiply(LAST, whole)
-        for p in range(PIECES - 2, PIECES):
-            nc.gpsimd.tensor_tensor(tail[:, columns(p)], gated(LAST, columns(p)), values(p), ADD)
-        nc.vector.tensor_tensor(window(LAST, h1), tail[:], weights1[:], MULT)
+        for p in range(SINGLE, PIECES):
+            if p == PIECES - 2:
+                multiply(LAST, whole)
+            nc.gpsimd.tensor_tensor(tail[:, edges_of(p // 2, p % 2)], gated(p // 2, columns(p)), values(p), ADD)
+        nc.vector.tensor_tensor(placed[0][:].indirect(dst_list[:]), tail[:], weights[:], MULT)
         store(LAST)

@@ -76,7 +76,10 @@ def lay_out_work():
     return at
 
 
-WORK = lay_out_work()
+LAST_TURNED_AT = lay_out_work()
+LAST_SUM_AT = LAST_TURNED_AT + STEP
+TAIL_AT = LAST_SUM_AT + STEP
+WORK = TAIL_AT + J - QUARTER
 
 
 def tile_list_rgg_L_kernel(
@@ -134,7 +137,7 @@ def tile_list_rgg_L_kernel(
         factors = [held.tile([P, 2 * HALF], F32, name="factors%d" % i) for i in range(2)]
         work = held.tile([P, WORK], F32)
         results = held.tile([P, (LAST - 1) * HALF], F32)
-        tail = held.tile([P, J], F32)
+        tail = work[:, TAIL_AT:WORK]
 
         def entries(offsets, edges):
             return offsets[:, edges.start // LIST_ROWS : edges.stop // LIST_ROWS]
@@ -276,7 +279,8 @@ def tile_list_rgg_L_kernel(
             return run(part_of(p), QUARTER)
 
         def summed(p):
-            return work[:, SUM_AT[p] : SUM_AT[p] + QUARTER]
+            at = SUM_AT.get(p, LAST_SUM_AT)
+            return work[:, at : at + QUARTER]
 
         def values(p):
             if p < LEAD:
@@ -306,6 +310,13 @@ def tile_list_rgg_L_kernel(
         multiply(0, second)
         gate(1, whole, banks[6], banks[7])
 
+        def finish(p, result):
+            nc.gpsimd.tensor_tensor(summed(p), gated(p // 2, columns(p)), values(p), ADD)
+            nc.gpsimd.tensor_tensor(result, summed(p), weights[:, edges_of(p // 2, part_of(p))], MULT)
+
+        def scatter(p, result):
+            nc.vector.tensor_copy(window(p // 2, edges_of(p // 2, part_of(p))), result)
+
         pairs = [banks[0:2], banks[4:6]]
         back = banks[3]
         for p in range(SINGLE):
@@ -327,6 +338,10 @@ def tile_list_rgg_L_kernel(
                     nc.scalar.activation(weighted[s], pair[s][:, 0:P], COPY, scale=weight_col[h][:, s : s + 1])
                 for s in range(2):
                     nc.tensor.transpose(back[:, run(s, P)], weighted[s], identity[:])
+                if p + 1 == SINGLE:
+                    finish(SINGLE, results[:, run(p, QUARTER)])
+                    scatter(SINGLE, results[:, run(p, QUARTER)])
+                    result = work[:, LAST_TURNED_AT : LAST_TURNED_AT + QUARTER]
                 nc.scalar.copy(result, back[:, 0:QUARTER])
             else:
                 if p + 1 in TURNED:
@@ -334,15 +349,14 @@ def tile_list_rgg_L_kernel(
                         square = pair[s][:, 0:P]
                         nc.tensor.matmul(square, gated(u, second)[:, run(s, P)], identity[:], start=True, stop=False, is_transpose=True)
                         nc.tensor.matmul(square, values(p + 1)[:, run(s, P)], identity[:], start=False, stop=True, is_transpose=True)
-                nc.gpsimd.tensor_tensor(summed(p), gated(u, columns(p)), values(p), ADD)
-                nc.gpsimd.tensor_tensor(result, summed(p), weights[:, edges_of(u, part_of(p))], MULT)
+                finish(p, result)
                 if p - 1 in TURNED:
                     gather_late(p - 1)
                 if p + 1 in TURNED or p % 2:
                     multiply(u + 1, whole)
             if p % 2:
                 gate(u + 2, whole, pair[0], pair[1])
-            nc.vector.tensor_copy(window(u, edges_of(u, part_of(p))), result)
+            scatter(p, result)
             if p == 0:
                 load_weights(3)
             if p not in TURNED:
@@ -350,9 +364,10 @@ def tile_list_rgg_L_kernel(
             if p % 2 and h == 1:
                 store(u)
 
-        for p in range(SINGLE, PIECES):
+        for p in range(SINGLE + 1, PIECES):
             if p == PIECES - 2:
                 multiply(LAST, whole)
-            nc.gpsimd.tensor_tensor(tail[:, edges_of(p // 2, p % 2)], gated(p // 2, columns(p)), values(p), ADD)
-        nc.vector.tensor_tensor(placed[0][:].indirect(dst_list[:]), tail[:], weights[:], MULT)
+            nc.gpsimd.tensor_tensor(tail[:, run(p - SINGLE - 1, QUARTER)], gated(p // 2, columns(p)), values(p), ADD)
+        rest = slice(QUARTER, J)
+        nc.vector.tensor_tensor(window(LAST, rest), tail, weights[:, rest], MULT)
         store(LAST)

@@ -42,36 +42,42 @@ TABLE_AT = STATE2_AT + 4 * T - 64
 WEIGHTS_AT = TABLE_AT + T - 64
 DST1_AT = WEIGHTS_AT + 4 * J
 PICKED1_AT = DST1_AT + 4 * HALF - 64
-STATE3_AT = PICKED1_AT + HALF - 64
-RAW1_AT = STATE3_AT + 4 * T
+EARLY2_AT = PICKED1_AT + HALF - 64
+RAW1_AT = EARLY2_AT + 4 * HALF
 SRC1_AT = RAW1_AT
 RAW_LATE_AT = RAW1_AT + 4 * PACK * PAIR
 WA1_AT = RAW_LATE_AT
 WB1_AT = WA1_AT + 4 * PAIR
-CAST1_AT = RAW_LATE_AT + 4 * PACK * PAIR
+STATE3_AT = RAW_LATE_AT + 4 * PACK * PAIR - 64
+CAST1_AT = STATE3_AT + 4 * T
 
 PIECES = 2 * len(UNITS)
-LEAD = 5
+SLOTS = (0, 1, 2, 3, 4, 5, 6, 8, 9, 10)
+EARLY = PIECES - len(SLOTS)
+GATHERED = {slot: EARLY + i for i, slot in enumerate(SLOTS)}
+SWAPPED = (0, 1, 3, 4)
 SINGLE = PIECES - 4
 TURNED = (1, 5, 9, 11)
 STEP = QUARTER - LAP
 SLIDE = HALF - LAP
 
 SUM_AT, VALUES_AT = {}, {}
+GATED_AT = {u: (LAST - u) * SLIDE for u in range(2, LAST + 1)}
 
 
 def lay_out_work():
-    at = LAST * SLIDE
-    for p in range(SINGLE):
-        if p in TURNED:
-            continue
-        if p - 1 in TURNED and p - 1 + LEAD < PIECES:
-            VALUES_AT[p - 1 + LEAD] = at
+    at = (LAST - 1) * SLIDE
+    for p in [3] + [p for p in range(SINGLE) if p != 3 and p not in TURNED]:
+        if p == 0:
+            GATED_AT[1] = at
+            at = at + SLIDE
+        if p - 1 in TURNED and p - 1 in GATHERED:
+            VALUES_AT[GATHERED[p - 1]] = at
             at = at + STEP
         SUM_AT[p] = at
         at = at + STEP
-        if p + LEAD < PIECES:
-            VALUES_AT[p + LEAD] = at
+        if p in GATHERED:
+            VALUES_AT[GATHERED[p]] = at
         at = at + QUARTER
     return at
 
@@ -133,7 +139,6 @@ def tile_list_rgg_L_kernel(
         wc_s = [held.tile([P, PAIR], U8, name="wc_s%d" % i, align_bytes=64) for i in range(2)]
         banks = [psum.tile([P, HALF], F32, name="bank%d" % i) for i in range(8)]
         early = [held.tile([P, HALF], F32, name="early%d" % i) for i in range(2)]
-        early.append(held.tile([P, QUARTER], F32, name="early2"))
         factors = [held.tile([P, 2 * HALF], F32, name="factors%d" % i) for i in range(2)]
         work = held.tile([P, WORK], F32)
         results = held.tile([P, (LAST - 1) * HALF], F32)
@@ -190,8 +195,9 @@ def tile_list_rgg_L_kernel(
         nc.vector.tensor_copy(picked1[:], tab_s[:].bitcast(U8).indirect(entries(dst_list, h1)))
         move_scales(planes0, picked0[:].bitcast(I32))
         nc.sync.dma_start(out=state[0][:, T // 2 : T], in_=rT[run(0, P), T // 2 : T])
+        move_scales(planes1, picked1[:].bitcast(I32))
         nc.sync.dma_start(
-            out=weight_rows[WEIGHT_ROW:P, :], in_=wgo[0, run(1, QUARTER)].rearrange("(c j) -> c j", j=P)
+            out=weight_rows[WEIGHT_ROW:P, :], in_=wgo[0, run(0, QUARTER)].rearrange("(c j) -> c j", j=P)
         )
         nc.sync.dma_start(out=state[1][:], in_=rT[run(1, P), :])
 
@@ -209,19 +215,18 @@ def tile_list_rgg_L_kernel(
         src_words.append(shared.tile([P, HALF], U32, name="src_words1", offset=SRC1_AT, align_bytes=64))
         gather_words(src_words[1], src_list, 1)
         quantise_wc(1)
-        move_scales(planes1, picked1[:].bitcast(I32))
         weights = shared.tile([P, J], F32, offset=WEIGHTS_AT, align_bytes=64)
 
         def load_weights(q):
             nc.sync.dma_start(out=weights[:, run(q, QUARTER)], in_=wgo[:, run(q, QUARTER)])
 
-        load_weights(0)
         load_weights(1)
         wa_w.append(shared.tile([P, PAIR], I32, name="wa1", offset=WA1_AT, align_bytes=64))
         wb_w.append(shared.tile([P, PAIR], I32, name="wb1", offset=WB1_AT, align_bytes=64))
         state.append(shared.tile([P, T], F32, name="state2", offset=STATE2_AT))
         state.append(shared.tile([P, T], F32, name="state3", offset=STATE3_AT))
         nc.sync.dma_start(out=state[2][:], in_=rT[run(2, P), :])
+        load_weights(0)
         load_weights(2)
         nc.sync.dma_start(out=wa_w[1][:], in_=words_of(wa_words)[:, PAIR:N])
         nc.sync.dma_start(out=wb_w[1][:], in_=words_of(wb_words)[:, PAIR:N])
@@ -262,18 +267,17 @@ def tile_list_rgg_L_kernel(
             nc.scalar.copy(factors[u % 2][:, h1][:, j], ms[:, 0:width])
 
         gated0 = [
-            shared.tile([P, QUARTER], F32, name="gated00", offset=CAST1_AT, align_bytes=64),
-            held.tile([P, QUARTER], F32, name="gated01"),
+            held.tile([P, QUARTER], F32, name="gated00"),
+            shared.tile([P, QUARTER], F32, name="gated01", offset=CAST1_AT, align_bytes=64),
         ]
 
         def gated(u, j):
             if u == 0:
                 return gated0[j.start // QUARTER][:]
-            at = (LAST - u) * SLIDE
-            return work[:, at : at + HALF][:, j]
+            return work[:, GATED_AT[u] : GATED_AT[u] + HALF][:, j]
 
         def part_of(p):
-            return p % 2 if p | 1 in TURNED or p >= SINGLE else 1 - p % 2
+            return 1 - p % 2 if p // 2 in SWAPPED else p % 2
 
         def columns(p):
             return run(part_of(p), QUARTER)
@@ -283,13 +287,13 @@ def tile_list_rgg_L_kernel(
             return work[:, at : at + QUARTER]
 
         def values(p):
-            if p < LEAD:
+            if p < EARLY:
                 return early[p // 2][:, columns(p)]
             return work[:, VALUES_AT[p] : VALUES_AT[p] + QUARTER]
 
         def gather_late(slot):
-            p = slot + LEAD
-            if p < PIECES:
+            if slot in GATHERED:
+                p = GATHERED[slot]
                 gather_state(values(p), UNITS[p // 2][0], edges_of(p // 2, part_of(p)))
 
         def multiply(u, j):
@@ -297,17 +301,18 @@ def tile_list_rgg_L_kernel(
 
         first, second, whole = run(0, QUARTER), run(1, QUARTER), slice(0, HALF)
 
-        gate(0, first, banks[6], banks[7])
+        gate(0, second, banks[6], banks[7])
         nc.tensor.transpose(banks[2][:, 0:P], weight_rows[:], identity[:])
-        gate(0, second, banks[0], banks[1])
+        gate(0, first, banks[0], banks[1])
         nc.scalar.copy(weight_col[0][:], banks[2][:, WEIGHT_ROW:P])
         dst_words.append(shared.tile([P, HALF], U32, name="dst_words1", offset=DST1_AT, align_bytes=64))
         gather_state(early[0][:], 0, h0)
-        gather_state(early[2][:], 0, edges_of(2, 0))
-        gather_state(early[1][:], 1, h0)
         gather_words(dst_words[1], dst_list, 1)
-        multiply(0, first)
+        early.append(shared.tile([P, HALF], F32, name="early2", offset=EARLY2_AT, align_bytes=64))
+        gather_state(early[2][:], 0, h1)
+        gather_state(early[1][:], 1, h0)
         multiply(0, second)
+        multiply(0, first)
         gate(1, whole, banks[6], banks[7])
 
         def finish(p, result):
@@ -347,7 +352,7 @@ def tile_list_rgg_L_kernel(
                 if p + 1 in TURNED:
                     for s in range(2):
                         square = pair[s][:, 0:P]
-                        nc.tensor.matmul(square, gated(u, second)[:, run(s, P)], identity[:], start=True, stop=False, is_transpose=True)
+                        nc.tensor.matmul(square, gated(u, columns(p + 1))[:, run(s, P)], identity[:], start=True, stop=False, is_transpose=True)
                         nc.tensor.matmul(square, values(p + 1)[:, run(s, P)], identity[:], start=False, stop=True, is_transpose=True)
                 finish(p, result)
                 if p - 1 in TURNED:

@@ -55,7 +55,7 @@ PIECES = 2 * len(UNITS)
 SLOTS = (0, 1, 2, 3, 4, 5, 6, 8, 9, 10)
 EARLY = PIECES - len(SLOTS)
 GATHERED = {slot: EARLY + i for i, slot in enumerate(SLOTS)}
-SWAPPED = (0, 1, 3, 4)
+SWAPPED = (0, 1, 4)
 SINGLE = PIECES - 4
 TURNED = (1, 5, 9, 11)
 STEP = QUARTER - LAP
@@ -283,6 +283,8 @@ def tile_list_rgg_L_kernel(
             return run(part_of(p), QUARTER)
 
         def summed(p):
+            if p == 7:
+                return factors[0][:, first]
             at = SUM_AT.get(p, LAST_SUM_AT)
             return work[:, at : at + QUARTER]
 
@@ -357,10 +359,10 @@ def tile_list_rgg_L_kernel(
                 finish(p, result)
                 if p - 1 in TURNED:
                     gather_late(p - 1)
-                if p + 1 in TURNED or p % 2:
+                if p + 1 in TURNED or p in (3, 6):
                     multiply(u + 1, whole)
-            if p % 2:
-                gate(u + 2, whole, pair[0], pair[1])
+            for later in {9: (6, 7), 11: ()}.get(p, (u + 2,) if p % 2 else ()):
+                gate(later, whole, pair[0], banks[6] if p == 5 else pair[1])
             scatter(p, result)
             if p == 0:
                 load_weights(3)

@@ -52,7 +52,7 @@ STATE3_AT = RAW_LATE_AT + 4 * PACK * PAIR - 64
 CAST1_AT = STATE3_AT + 4 * T
 
 PIECES = 2 * len(UNITS)
-SLOTS = (0, 1, 2, 3, 4, 5, 6, 8, 9, 10)
+SLOTS = range(11)
 EARLY = PIECES - len(SLOTS)
 GATHERED = {slot: EARLY + i for i, slot in enumerate(SLOTS)}
 SWAPPED = (0, 1, 4)
@@ -139,7 +139,7 @@ def tile_list_rgg_L_kernel(
         wc_s = [held.tile([P, PAIR], U8, name="wc_s%d" % i, align_bytes=64) for i in range(2)]
         banks = [psum.tile([P, HALF], F32, name="bank%d" % i) for i in range(8)]
         early = [held.tile([P, HALF], F32, name="early%d" % i) for i in range(2)]
-        factors = [held.tile([P, 2 * HALF], F32, name="factors%d" % i) for i in range(2)]
+        factors = [held.tile([P, 2 * HALF], F32, name="factors%d" % i) for i in range(3)]
         work = held.tile([P, WORK], F32)
         results = held.tile([P, (LAST - 1) * HALF], F32)
         tail = work[:, TAIL_AT:WORK]
@@ -263,8 +263,8 @@ def tile_list_rgg_L_kernel(
                 ms[:, 0:width], lhsT=wc_w[pair][:, n].bitcast(FP8X4), lhsT_scale=wc_s[pair][:, n],
                 rhs=src_w, rhs_scale=src_plane, start=True, stop=True,
             )
-            nc.scalar.activation(factors[u % 2][:, h0][:, j], za[:, 0:width], SIGMOID)
-            nc.scalar.copy(factors[u % 2][:, h1][:, j], ms[:, 0:width])
+            nc.scalar.activation(factors[2 if u == 6 else u % 2][:, h0][:, j], za[:, 0:width], SIGMOID)
+            nc.scalar.copy(factors[2 if u == 6 else u % 2][:, h1][:, j], ms[:, 0:width])
 
         gated0 = [
             held.tile([P, QUARTER], F32, name="gated00"),
@@ -291,6 +291,8 @@ def tile_list_rgg_L_kernel(
         def values(p):
             if p < EARLY:
                 return early[p // 2][:, columns(p)]
+            if p == GATHERED[7]:
+                return factors[0][:, STEP : STEP + QUARTER]
             return work[:, VALUES_AT[p] : VALUES_AT[p] + QUARTER]
 
         def gather_late(slot):
@@ -299,7 +301,7 @@ def tile_list_rgg_L_kernel(
                 gather_state(values(p), UNITS[p // 2][0], edges_of(p // 2, part_of(p)))
 
         def multiply(u, j):
-            nc.gpsimd.tensor_tensor(gated(u, j), factors[u % 2][:, h0][:, j], factors[u % 2][:, h1][:, j], MULT)
+            nc.gpsimd.tensor_tensor(gated(u, j), factors[2 if u == 6 else u % 2][:, h0][:, j], factors[2 if u == 6 else u % 2][:, h1][:, j], MULT)
 
         first, second, whole = run(0, QUARTER), run(1, QUARTER), slice(0, HALF)
 
@@ -310,8 +312,8 @@ def tile_list_rgg_L_kernel(
         dst_words.append(shared.tile([P, HALF], U32, name="dst_words1", offset=DST1_AT, align_bytes=64))
         gather_state(early[0][:], 0, h0)
         gather_words(dst_words[1], dst_list, 1)
-        early.append(shared.tile([P, HALF], F32, name="early2", offset=EARLY2_AT, align_bytes=64))
-        gather_state(early[2][:], 0, h1)
+        early.append(shared.tile([P, QUARTER], F32, name="early2", offset=EARLY2_AT, align_bytes=64))
+        gather_state(early[2][:], 0, edges_of(2, 0))
         gather_state(early[1][:], 1, h0)
         multiply(0, second)
         multiply(0, first)

from contextlib import ExitStack

import concourse.mybir as mybir
from concourse.masks import make_identity

K, N, T, J = 512, 512, 2048, 1024
FLOPS = 3 * 2 * K * N * J

F32 = mybir.dt.float32
BF16 = mybir.dt.bfloat16
I32 = mybir.dt.int32
U32 = mybir.dt.uint32
U16 = mybir.dt.uint16
U8 = mybir.dt.uint8
FP8X4 = mybir.dt.float8_e4m3fn_x4
MULT = mybir.AluOpType.mult
ADD = mybir.AluOpType.add
SIGMOID = mybir.ActivationFunctionType.Sigmoid
COPY = mybir.ActivationFunctionType.Copy

P = 128
PACK = 4
MX_BLOCK = 32
SCALE_ROWS = K // MX_BLOCK
QUADRANT = 32
GROUP_ROWS = QUADRANT * PACK // MX_BLOCK
COLUMN_RUN = 4
LIST_ROWS = 16
HALF = J // 2
QUARTER = J // 4
STAGE = P - SCALE_ROWS
TURNED_SQUARES = 2
WEIGHT_ROW = P - TURNED_SQUARES
PAIR = 2 * P
LAP = 64
UNITS = [(0, 0), (1, 0), (0, 1), (1, 1), (2, 0), (2, 1), (3, 0), (3, 1)]
LAST = len(UNITS) - 1
WINDOW_OF = {0: 0, 1: 1, 2: 2, 3: 0}

STATE2_AT = 0
TABLE_AT = STATE2_AT + 4 * T - 64
WEIGHTS_AT = TABLE_AT + T - 64
DST1_AT = WEIGHTS_AT + 4 * J
PICKED1_AT = DST1_AT + 4 * HALF - 64
EARLY2_AT = PICKED1_AT + HALF - 64
RAW1_AT = EARLY2_AT + 4 * HALF
SRC1_AT = RAW1_AT
RAW_LATE_AT = RAW1_AT + 4 * PACK * PAIR
WA1_AT = RAW_LATE_AT
WB1_AT = WA1_AT + 4 * PAIR
STATE3_AT = RAW_LATE_AT + 4 * PACK * PAIR - 64
CAST1_AT = STATE3_AT + 4 * T

PIECES = 2 * len(UNITS)
SLOTS = range(11)
EARLY = PIECES - len(SLOTS)
GATHERED = {slot: EARLY + i for i, slot in enumerate(SLOTS)}
SWAPPED = (0, 1, 4)
SINGLE = PIECES - 4
TURNED = (1, 5, 9, 11)
STEP = QUARTER - LAP
SLIDE = HALF - LAP

SUM_AT, VALUES_AT = {}, {}
GATED_AT = {u: (LAST - u) * SLIDE for u in range(2, LAST + 1)}


def lay_out_work():
    at = (LAST - 1) * SLIDE
    for p in [3] + [p for p in range(SINGLE) if p != 3 and p not in TURNED]:
        if p == 0:
            GATED_AT[1] = at
            at = at + SLIDE
        if p - 1 in TURNED and p - 1 in GATHERED:
            VALUES_AT[GATHERED[p - 1]] = at
            at = at + STEP
        SUM_AT[p] = at
        at = at + STEP
        if p in GATHERED:
            VALUES_AT[GATHERED[p]] = at
        at = at + QUARTER
    return at


LAST_TURNED_AT = lay_out_work()
LAST_SUM_AT = LAST_TURNED_AT + STEP
TAIL_AT = LAST_SUM_AT + STEP
WORK = TAIL_AT + J - QUARTER


def tile_list_rgg_L_kernel(
    tc, tab_words, tab_scales, wa_words, wa_scales, wb_words, wb_scales, wc, rT, wgo, offs, offs2, out
):
    nc = tc.nc

    def words_of(packed):
        return packed[0].rearrange("p n t -> p (n t)").bitcast(I32)

    def move_scales(plane, rows):
        for r in range(GROUP_ROWS):
            nc.sync.dma_start(out=plane[r:P:QUADRANT, :], in_=rows[STAGE + r : P : GROUP_ROWS, :])

    def run(i, width):
        return slice(i * width, (i + 1) * width)

    with ExitStack() as ctx:
        held = ctx.enter_context(tc.tile_pool(name="held", bufs=1))
        psum = ctx.enter_context(tc.psum_pool(name="psum", bufs=1))
        shared = ctx.enter_context(tc.tile_pool(name="shared", bufs=1))

        src_list = held.tile([P, J // LIST_ROWS], U16)
        dst_list = held.tile([P, J // LIST_ROWS], U16)
        tab_s = shared.tile([P, T // PACK], I32, offset=TABLE_AT, align_bytes=64)
        tab_w = held.tile([P, T], I32, align_bytes=64)
        staged = held.tile([P, 2 * N // PACK], I32, align_bytes=64)
        w_s = held.tile([P, 2 * N // PACK], I32, align_bytes=64)
        planes0 = held.tile([P, (J + HALF) // PACK], I32, align_bytes=64)
        planes1 = held.tile([P, HALF // PACK], I32, align_bytes=64)
        wa_at, wb_at = 0, N // PACK
        wa_s, wb_s = w_s[:].bitcast(U8)[:, 0:N], w_s[:].bitcast(U8)[:, N : 2 * N]
        src_s = planes0[:].bitcast(U8)[:, 0:J]
        dst_s = [planes0[:].bitcast(U8)[:, J : J + HALF], planes1[:].bitcast(U8)]
        placed = [held.tile([P, T], F32, name="placed%d" % i) for i in range(3)]
        weight_col = [held.tile([P, TURNED_SQUARES], F32, name="weight_col%d" % h) for h in range(2)]
        weight_rows = held.tile([P, P], F32)
        identity = held.tile([P, P], F32)
        state = [held.tile([P, T], F32, name="state%d" % b) for b in range(2)]
        wa_w = [held.tile([P, PAIR], I32, name="wa0", align_bytes=64)]
        wb_w = [held.tile([P, PAIR], I32, name="wb0", align_bytes=64)]
        wc_raw = [
            shared.tile([P, PACK, PAIR], F32, name="wc_raw0", offset=RAW1_AT, align_bytes=64),
            shared.tile([P, PACK, PAIR], F32, name="wc_raw1", offset=RAW_LATE_AT, align_bytes=64),
        ]
        wc_bf = [
            held.tile([P, PAIR, PACK], BF16, name="wc_bf0", align_bytes=64),
            shared.tile([P, PAIR, PACK], BF16, name="wc_bf1", offset=CAST1_AT, align_bytes=64),
        ]
        wc_w = [held.tile([P, PAIR], U32, name="wc_w%d" % i, align_bytes=64) for i in range(2)]
        wc_s = [held.tile([P, PAIR], U8, name="wc_s%d" % i, align_bytes=64) for i in range(2)]
        banks = [psum.tile([P, HALF], F32, name="bank%d" % i) for i in range(8)]
        early = [held.tile([P, HALF], F32, name="early%d" % i) for i in range(2)]
        factors = [held.tile([P, 2 * HALF], F32, name="factors%d" % i) for i in range(3)]
        work = held.tile([P, WORK], F32)
        results = held.tile([P, (LAST - 1) * HALF], F32)
        tail = work[:, TAIL_AT:WORK]

        def entries(offsets, edges):
            return offsets[:, edges.start // LIST_ROWS : edges.stop // LIST_ROWS]

        def load_wc(i):
            nc.sync.dma_start(out=wc_raw[i][:], in_=wc[:, run(i, PAIR)].rearrange("(p i) n -> p i n", i=PACK))

        def cast_wc(i):
            nc.scalar.copy(
                wc_bf[i][:].rearrange("p (c m) i -> p c i m", m=COLUMN_RUN),
                wc_raw[i][:].rearrange("p i (c m) -> p c i m", m=COLUMN_RUN),
            )

        def quantise_wc(i):
            nc.vector.quantize_mx(
                out=wc_w[i][:].bitcast(FP8X4), scales=wc_s[i][:], in_=wc_bf[i][:].rearrange("p n i -> p (n i)")
            )

        h0, h1 = run(0, HALF), run(1, HALF)

        nc.vector.memset(placed[2][:, 0 : T // 4 + 1], 0.0)
        nc.vector.memset(placed[2][:, T // 4 + 1 : T // 2], 0.0)
        nc.gpsimd.memset(tab_s[0:STAGE, :], 0)
        nc.gpsimd.memset(w_s[:], 0)
        nc.gpsimd.memset(planes0[:], 0)
        nc.gpsimd.memset(planes1[:], 0)
        nc.gpsimd.memset(weight_rows[0:WEIGHT_ROW, :], 0.0)
        make_identity(nc, identity[:])
        for window in placed[0:2]:
            nc.gpsimd.memset(window[:], 0.0)
        nc.gpsimd.memset(placed[2][:, T // 2 : T], 0.0)

        nc.sync.dma_start(out=tab_s[STAGE:P, :], in_=tab_scales[0].bitcast(I32))
        nc.sync.dma_start(src_list[:], offs)
        nc.sync.dma_start(dst_list[:], offs2)
        nc.sync.dma_start(out=staged[STAGE:P, wa_at:wb_at], in_=wa_scales[0].bitcast(I32))
        nc.sync.dma_start(out=staged[STAGE:P, wb_at : wb_at + N // PACK], in_=wb_scales[0].bitcast(I32))
        nc.sync.dma_start(out=tab_w[:], in_=words_of(tab_words))
        load_wc(0)
        nc.sync.dma_start(out=wa_w[0][:], in_=words_of(wa_words)[:, 0:PAIR])
        move_scales(w_s, staged[:])
        load_wc(1)
        nc.sync.dma_start(out=state[0][:, 0 : T // 2], in_=rT[run(0, P), 0 : T // 2])
        nc.sync.dma_start(out=wb_w[0][:], in_=words_of(wb_words)[:, 0:PAIR])

        picked0 = held.tile([P, J + HALF], U8, align_bytes=64)
        nc.vector.tensor_copy(picked0[:, 0:J], tab_s[:].bitcast(U8).indirect(src_list[:]))
        nc.vector.tensor_copy(picked0[:, J : J + HALF], tab_s[:].bitcast(U8).indirect(entries(dst_list, h0)))
        picked1 = shared.tile([P, HALF], U8, offset=PICKED1_AT, align_bytes=64)
        nc.vector.tensor_copy(picked1[:], tab_s[:].bitcast(U8).indirect(entries(dst_list, h1)))
        move_scales(planes0, picked0[:].bitcast(I32))
        nc.sync.dma_start(out=state[0][:, T // 2 : T], in_=rT[run(0, P), T // 2 : T])
        move_scales(planes1, picked1[:].bitcast(I32))
        nc.sync.dma_start(
            out=weight_rows[WEIGHT_ROW:P, :], in_=wgo[0, run(0, QUARTER)].rearrange("(c j) -> c j", j=P)
        )
        nc.sync.dma_start(out=state[1][:], in_=rT[run(1, P), :])

        def gather_words(words, offsets, h):
            nc.vector.tensor_copy(words[:], tab_w[:].bitcast(U32).indirect(entries(offsets, run(h, HALF))))

        src_words = [held.tile([P, HALF], U32, name="src_words0", align_bytes=64)]
        dst_words = [held.tile([P, HALF], U32, name="dst_words0", align_bytes=64)]
        gather_words(src_words[0], src_list, 0)
        gather_words(dst_words[0], dst_list, 0)
        for i in range(2):
            cast_wc(i)
        quantise_wc(0)

        src_words.append(shared.tile([P, HALF], U32, name="src_words1", offset=SRC1_AT, align_bytes=64))
        gather_words(src_words[1], src_list, 1)
        quantise_wc(1)
        weights = shared.tile([P, J], F32, offset=WEIGHTS_AT, align_bytes=64)

        def load_weights(q):
            nc.sync.dma_start(out=weights[:, run(q, QUARTER)], in_=wgo[:, run(q, QUARTER)])

        load_weights(1)
        wa_w.append(shared.tile([P, PAIR], I32, name="wa1", offset=WA1_AT, align_bytes=64))
        wb_w.append(shared.tile([P, PAIR], I32, name="wb1", offset=WB1_AT, align_bytes=64))
        state.append(shared.tile([P, T], F32, name="state2", offset=STATE2_AT))
        state.append(shared.tile([P, T], F32, name="state3", offset=STATE3_AT))
        nc.sync.dma_start(out=state[2][:], in_=rT[run(2, P), :])
        load_weights(0)
        load_weights(2)
        nc.sync.dma_start(out=wa_w[1][:], in_=words_of(wa_words)[:, PAIR:N])
        nc.sync.dma_start(out=wb_w[1][:], in_=words_of(wb_words)[:, PAIR:N])
        nc.sync.dma_start(out=state[3][:], in_=rT[run(3, P), :])

        def edges_of(u, part):
            return run(2 * UNITS[u][1] + part, QUARTER)

        def gather_state(values, b, edges):
            nc.vector.tensor_copy(values, state[b][:].indirect(entries(dst_list, edges)))

        def window(u, edges):
            return placed[WINDOW_OF[UNITS[u][0]]][:].indirect(entries(dst_list, edges))

        def store(u):
            b = UNITS[u][0]
            nc.sync.dma_start(out=out[run(b, P), :], in_=placed[WINDOW_OF[b]][:])

        def gate(u, j, za, ms):
            b, h = UNITS[u]
            width = j.stop - j.start
            pair, n = b // 2, run(b % 2, P)
            src_w, dst_w = src_words[h][:, j].bitcast(FP8X4), dst_words[h][:, j].bitcast(FP8X4)
            src_plane = src_s[:, run(h, HALF)][:, j]
            nc.tensor.matmul_mx(
                za[:, 0:width], lhsT=wb_w[pair][:, n].bitcast(FP8X4), lhsT_scale=wb_s[:, run(b, P)],
                rhs=src_w, rhs_scale=src_plane, start=True, stop=False,
            )
            nc.tensor.matmul_mx(
                za[:, 0:width], lhsT=wa_w[pair][:, n].bitcast(FP8X4), lhsT_scale=wa_s[:, run(b, P)],
                rhs=dst_w, rhs_scale=dst_s[h][:, j], start=False, stop=True,
            )
            nc.tensor.matmul_mx(
                ms[:, 0:width], lhsT=wc_w[pair][:, n].bitcast(FP8X4), lhsT_scale=wc_s[pair][:, n],
                rhs=src_w, rhs_scale=src_plane, start=True, stop=True,
            )
            nc.scalar.activation(factors[2 if u == 6 else u % 2][:, h0][:, j], za[:, 0:width], SIGMOID)
            nc.scalar.copy(factors[2 if u == 6 else u % 2][:, h1][:, j], ms[:, 0:width])

        gated0 = [
            held.tile([P, QUARTER], F32, name="gated00"),
            shared.tile([P, QUARTER], F32, name="gated01", offset=CAST1_AT, align_bytes=64),
        ]

        def gated(u, j):
            if u == 0:
                return gated0[j.start // QUARTER][:]
            return work[:, GATED_AT[u] : GATED_AT[u] + HALF][:, j]

        def part_of(p):
            return 1 - p % 2 if p // 2 in SWAPPED else p % 2

        def columns(p):
            return run(part_of(p), QUARTER)

        def summed(p):
            if p == 7:
                return factors[0][:, first]
            at = SUM_AT.get(p, LAST_SUM_AT)
            return work[:, at : at + QUARTER]

        def values(p):
            if p < EARLY:
                return early[p // 2][:, columns(p)]
            if p == GATHERED[7]:
                return factors[0][:, STEP : STEP + QUARTER]
            return work[:, VALUES_AT[p] : VALUES_AT[p] + QUARTER]

        def gather_late(slot):
            if slot in GATHERED:
                p = GATHERED[slot]
                gather_state(values(p), UNITS[p // 2][0], edges_of(p // 2, part_of(p)))

        def multiply(u, j):
            nc.gpsimd.tensor_tensor(gated(u, j), factors[2 if u == 6 else u % 2][:, h0][:, j], factors[2 if u == 6 else u % 2][:, h1][:, j], MULT)

        first, second, whole = run(0, QUARTER), run(1, QUARTER), slice(0, HALF)

        gate(0, second, banks[6], banks[7])
        nc.tensor.transpose(banks[2][:, 0:P], weight_rows[:], identity[:])
        gate(0, first, banks[0], banks[1])
        nc.scalar.copy(weight_col[0][:], banks[2][:, WEIGHT_ROW:P])
        dst_words.append(shared.tile([P, HALF], U32, name="dst_words1", offset=DST1_AT, align_bytes=64))
        gather_state(early[0][:], 0, h0)
        gather_words(dst_words[1], dst_list, 1)
        early.append(shared.tile([P, QUARTER], F32, name="early2", offset=EARLY2_AT, align_bytes=64))
        gather_state(early[2][:], 0, edges_of(2, 0))
        gather_state(early[1][:], 1, h0)
        multiply(0, second)
        multiply(0, first)
        gate(1, whole, banks[6], banks[7])

        def finish(p, result):
            nc.gpsimd.tensor_tensor(summed(p), gated(p // 2, columns(p)), values(p), ADD)
            nc.gpsimd.tensor_tensor(result, summed(p), weights[:, edges_of(p // 2, part_of(p))], MULT)

        def scatter(p, result):
            nc.vector.tensor_copy(window(p // 2, edges_of(p // 2, part_of(p))), result)

        pairs = [banks[0:2], banks[4:6]]
        back = banks[3]
        for p in range(SINGLE):
            u, h = p // 2, UNITS[p // 2][1]
            pair = pairs[len([t for t in TURNED if t <= p | 1]) % 2 - 1]
            result = results[:, run(p, QUARTER)] if p else weights[:, run(3, QUARTER)]
            if p in TURNED:
                if p == TURNED[1]:
                    for s in range(2):
                        nc.tensor.transpose(banks[7][:, run(s, P)], weights[:, run(3, QUARTER)][:, run(s, P)], identity[:])
                    nc.scalar.copy(weight_col[1][:], banks[7][:, 0:QUARTER:P])
                if p + 1 == SINGLE:
                    weighted = [gated(LAST, first)[:, run(s, P)] for s in range(2)]
                elif p + 2 in TURNED:
                    weighted = [summed(p + 1)[:, run(s, P)] for s in range(2)]
                else:
                    weighted = [summed(p + 1 + s)[:, 0:P] for s in range(2)]
                for s in range(2):
                    nc.scalar.activation(weighted[s], pair[s][:, 0:P], COPY, scale=weight_col[h][:, s : s + 1])
                for s in range(2):
                    nc.tensor.transpose(back[:, run(s, P)], weighted[s], identity[:])
                if p + 1 == SINGLE:
                    finish(SINGLE, results[:, run(p, QUARTER)])
                    scatter(SINGLE, results[:, run(p, QUARTER)])
                    result = work[:, LAST_TURNED_AT : LAST_TURNED_AT + QUARTER]
                nc.scalar.copy(result, back[:, 0:QUARTER])
            else:
                if p + 1 in TURNED:
                    for s in range(2):
                        square = pair[s][:, 0:P]
                        nc.tensor.matmul(square, gated(u, columns(p + 1))[:, run(s, P)], identity[:], start=True, stop=False, is_transpose=True)
                        nc.tensor.matmul(square, values(p + 1)[:, run(s, P)], identity[:], start=False, stop=True, is_transpose=True)
                finish(p, result)
                if p - 1 in TURNED:
                    gather_late(p - 1)
                if p + 1 in TURNED or p in (3, 6):
                    multiply(u + 1, whole)
            for later in {9: (6, 7), 11: ()}.get(p, (u + 2,) if p % 2 else ()):
                gate(later, whole, pair[0], banks[6] if p == 5 else pair[1])
            scatter(p, result)
            if p == 0:
                load_weights(3)
            if p not in TURNED:
                gather_late(p)
            if p % 2 and h == 1:
                store(u)

        for p in range(SINGLE + 1, PIECES):
            if p == PIECES - 2:
                multiply(LAST, whole)
            nc.gpsimd.tensor_tensor(tail[:, run(p - SINGLE - 1, QUARTER)], gated(p // 2, columns(p)), values(p), ADD)
        rest = slice(QUARTER, J)
        nc.vector.tensor_tensor(window(LAST, rest), tail, weights[:, rest], MULT)
        store(LAST)
